import numpy as np
import ml_dtypes


def mxq(x, axis, fmt="e4m3"):
    dtype, down = {"e4m3": (ml_dtypes.float8_e4m3fn, 7), "e5m2": (ml_dtypes.float8_e5m2, 14)}[fmt]
    v = np.moveaxis(np.asarray(x, np.float32).astype(ml_dtypes.bfloat16).astype(np.float64), axis, -1)
    blocks = v.reshape(v.shape[:-1] + (-1, 32))
    amax = np.abs(blocks).max(-1, keepdims=True)
    byte = np.maximum(np.where(amax > 0, np.frexp(amax)[1] - 1 + 127, 0) - down, 1)
    scale = np.exp2(byte - 127.0)
    codes = (blocks / scale).astype(np.float32).astype(dtype).astype(np.float64)
    return np.moveaxis((codes * scale).reshape(v.shape), -1, axis)


WIDE = False


def mx_kscale(k):
    if not WIDE:
        return np.ones(k)
    levels = np.array([10, -10, 5, -5, 0])
    if k % 512:
        return np.exp2(np.random.permutation(np.resize(levels, k // 32))).repeat(32)
    a = np.empty((k // 512, 16))
    for p in range(k // 512):
        a[p, :8] = np.random.permutation(np.resize(levels, 8))
        for g in range(8):
            far = levels[np.abs(levels - a[p, g]) >= 10]
            a[p, g + 8] = far[np.random.randint(len(far))]
    return np.exp2(a.ravel()).repeat(32)


BF16 = ml_dtypes.bfloat16


def bf(x):
    return np.asarray(x, np.float32).astype(BF16)


def f64(x):
    return np.asarray(x).astype(np.float64)


E2M1 = np.array([0.0, 0.5, 1.0, 1.5, 2.0, 3.0, 4.0, 6.0, -0.0, -0.5, -1.0, -1.5, -2.0, -3.0, -4.0, -6.0])


def pack_weight(w, fmt):
    k, n = w.shape
    w = f64(bf(w)).reshape(k // 32, 32, n)
    amax = np.abs(w).max(1)
    if fmt == "e4m3":
        byte = np.frexp(amax)[1] - 1 + 127 - 7
    else:
        mant, ex = np.frexp(amax / 6.0)
        byte = np.where(mant > 0.5, ex, ex - 1) + 127
    byte = np.clip(np.where(amax > 0, byte, 1), 1, 254)
    scaled = (w * np.exp2(127.0 - byte)[:, None, :]).reshape(k, n).astype(np.float32)
    by_word = np.ascontiguousarray(scaled.reshape(k // 512, 128, 4, n).transpose(0, 1, 3, 2))
    if fmt == "e4m3":
        words = by_word.astype(ml_dtypes.float8_e4m3fn).view(np.uint8)
    else:
        c = by_word.astype(ml_dtypes.float4_e2m1fn).view(np.uint8) & 0xF
        words = c[..., 0::2] | (c[..., 1::2] << 4)
    return np.ascontiguousarray(words), np.ascontiguousarray(byte.astype(np.uint8).reshape(k // 512, 16, n))


def unpack_weight(words, scales, fmt):
    g, p, n, _ = words.shape
    if fmt == "e4m3":
        vals = np.ascontiguousarray(words).view(ml_dtypes.float8_e4m3fn).astype(np.float64)
    else:
        nib = np.empty((g, p, n, 4), np.uint8)
        nib[..., 0::2] = words & 0xF
        nib[..., 1::2] = words >> 4
        vals = E2M1[nib]
    vals = vals * np.repeat(np.exp2(scales.astype(np.float64) - 127.0), 8, axis=1)[..., None]
    return vals.transpose(0, 1, 3, 2).reshape(g * 512, n)
def pack4(w):
    words, scales = pack_weight(w, "e2m1")
    return words.reshape(words.shape[0], 128, -1), scales


def unpack4(words, scales):
    return unpack_weight(words.reshape(words.shape[0], 128, -1, 2), scales, "e2m1")


B, D, H = 512, 1024, 1536


def draw0():
    s = mx_kscale(D)
    t = mx_kscale(H)
    u = np.random.standard_normal((H, H)) / np.sqrt(H) / t[:, None]
    u_words, u_scales = pack4(u)
    return {
        "x1": bf(np.random.standard_normal((B, D)) * s),
        "x2": bf(np.random.standard_normal((B, D)) * s),
        "h0": bf(np.tanh(np.random.standard_normal((B, H)))),
        "gain": bf((1 + 0.1 * np.random.standard_normal(H)) * t),
        "w": bf(np.random.standard_normal((D, H)) / np.sqrt(D) / s[:, None]),
        "u_words": u_words,
        "u_scales": u_scales,
    }


def core(x1, x2, h0, gain, w, u_words, u_scales):
    wq = mxq(f64(w), 0, "e4m3")
    u = unpack4(u_words, u_scales)
    c = f64(gain)
    r0 = mxq(f64(h0) * c, 1, "e4m3")
    h1 = np.tanh((mxq(f64(x1), 1, "e4m3") @ wq) + (r0 @ u))
    r1 = mxq(h1 * c, 1, "e4m3")
    h2 = np.tanh((mxq(f64(x2), 1, "e4m3") @ wq) + (r1 @ u))
    return h1, h2


def e4m3fn_bytes(y):
    return np.clip(np.asarray(y, np.float64), -448.0, 448.0).astype(np.float32).astype(ml_dtypes.float8_e4m3fn).view(np.uint8)


def e4m3fn_values(b):
    return np.asarray(b, np.uint8).view(ml_dtypes.float8_e4m3fn).astype(np.float64)


def setup_inputs():
    d = draw0()
    x0 = np.asarray(d['w']).astype(np.float64)
    s = (np.max(np.abs(x0), axis=(1,), keepdims=True) / 448.0).astype(np.float32)
    out = {}
    for k, v in d.items():
        if k == 'w':
            out['w_bytes'] = e4m3fn_bytes(x0 / s.astype(np.float64))
            out['w_scale'] = s
        else:
            out[k] = v
    return out


def reference(x1, x2, h0, gain, w_bytes, w_scale, u_words, u_scales):
    return core(x1, x2, h0, gain, e4m3fn_values(w_bytes) * w_scale.astype(np.float64), u_words, u_scales)

@@ -1,0 +1,370 @@
+from contextlib import ExitStack
+
+import concourse.mybir as mybir
+from concourse.masks import make_identity
+
+B, D, H = 512, 1024, 1536
+FLOPS = 2 * 2 * B * H * (D + H)
+
+F32 = mybir.dt.float32
+BF16 = mybir.dt.bfloat16
+I32 = mybir.dt.int32
+U32 = mybir.dt.uint32
+U8 = mybir.dt.uint8
+E4M3 = mybir.dt.float8_e4m3fn
+E4M3X4 = mybir.dt.float8_e4m3fn_x4
+E2M1X4 = mybir.dt.float4_e2m1fn_x4
+MULT = mybir.AluOpType.mult
+COPY = mybir.ActivationFunctionType.Copy
+TANH = mybir.ActivationFunctionType.Tanh
+
+P = 128
+N = 512
+NB = B // P
+NJ = H // N
+NX = D // N
+
+
+def tile_two_step_rnn_fp4_s3_kernel(tc, x1, x2, h0, gain, w_bytes, w_scale, u_words, u_scales, out_0, out_1):
+    nc = tc.nc
+    with ExitStack() as ctx:
+        keep = ctx.enter_context(tc.tile_pool(name="keep", bufs=1))
+        work = ctx.enter_context(tc.tile_pool(name="work", bufs=3))
+        outs = ctx.enter_context(tc.tile_pool(name="outs", bufs=12))
+        psum = ctx.enter_context(tc.psum_pool(name="psum", bufs=1))
+
+        def keep_tile(shape, dtype, name):
+            return keep.tile(shape, dtype, name=name, align_bytes=64)
+
+        warm = keep_tile([P, 16], F32, "warm")
+        nc.vector.memset(warm[:], 0.0)
+        nc.scalar.activation(out=warm[:, 0:1], in_=warm[:, 8:9], func=TANH)
+        ident = keep_tile([P, P], F32, "ident")
+        make_identity(nc, ident[:])
+        u_planes = keep_tile([P, NJ, H], U8, "u_planes")
+        nc.vector.memset(u_planes[:].rearrange("p g n -> p (g n)").bitcast(I32), 0)
+
+        gain_col = keep_tile([P, NJ, 4], BF16, "gain_col")
+        nc.scalar.dma_start(out=gain_col[:], in_=gain.rearrange("(g p t) -> p g t", p=P, t=4))
+        w_sc = keep_tile([P, NX, 4], F32, "w_sc")
+        nc.scalar.dma_start(out=w_sc[:], in_=w_scale.rearrange("(g p t) o -> p g (t o)", p=P, t=4))
+
+        h0_raw = {}
+        u_sb = {}
+        w_raw = {}
+        x_raw = {}
+
+        def load_h0(b):
+            t = keep_tile([P, H], BF16, "h0_%d" % b)
+            nc.sync.dma_start(out=t[:], in_=h0[P * b : P * b + P, :])
+            h0_raw[b] = t
+
+        def load_u(g):
+            t = keep_tile([P, 2 * H], U8, "u_%d" % g)
+            nc.sync.dma_start(out=t[:].bitcast(I32), in_=u_words[g].bitcast(I32))
+            u_sb[g] = t
+
+        def load_u_scales():
+            for q in range(4):
+                nc.sync.dma_start(
+                    out=u_planes[32 * q : 32 * q + 4, :, :].bitcast(I32),
+                    in_=u_scales[:, 4 * q : 4 * q + 4, :].rearrange("g q n -> q g n").bitcast(I32),
+                )
+
+        def load_w(g, j0, j1):
+            t = keep_tile([P, 4, N * (j1 - j0)], U8, "w_bytes_%d_%d" % (g, j0))
+            nc.sync.dma_start(
+                out=t[:],
+                in_=w_bytes[N * g : N * g + N, N * j0 : N * j1].rearrange("(p t) n -> p t n", t=4),
+            )
+            for j in range(j0, j1):
+                w_raw[j, g] = (t, N * (j - j0))
+
+        def load_x(s, x, bs):
+            for b in bs:
+                t = keep_tile([P, D], BF16, "x%d_%d" % (s, b))
+                nc.sync.dma_start(out=t[:], in_=x[P * b : P * b + P, :])
+                x_raw[s, b] = t
+
+        load_h0(0)
+        load_h0(1)
+        load_u_scales()
+        load_u(0)
+        load_w(0, 0, 1)
+        load_h0(2)
+        load_h0(3)
+        load_u(1)
+        load_w(1, 0, 1)
+        load_x(1, x1, [0, 1])
+        load_u(2)
+        load_w(0, 1, 3)
+        load_x(1, x1, [2, 3])
+        load_w(1, 1, 3)
+        load_x(2, x2, [0, 1, 2, 3])
+        gain_row = keep_tile([P, H], BF16, "gain_row")
+        nc.sync.dma_start(out=gain_row[:], in_=gain.partition_broadcast(P))
+
+        r_grp, r_codes, r_scales = {}, {}, {}
+        for s in (1, 2):
+            for g in range(NJ):
+                for pair in range(2):
+                    key = "%d_%d_%d" % (s, g, pair)
+                    r_grp[s, g, pair] = keep_tile([P, 1024], BF16, "rg_" + key)
+                    r_codes[s, g, pair] = keep_tile([P, 256], U32, "rc_" + key)
+                    r_scales[s, g, pair] = keep_tile([P, 256], U8, "rs_" + key)
+        x_grp, x_codes, x_scales = {}, {}, {}
+        for s in (1, 2):
+            for b in range(NB):
+                key = "%d_%d" % (s, b)
+                x_grp[s, b] = keep_tile([P, 1024], BF16, "xg_" + key)
+                x_codes[s, b] = keep_tile([P, 256], U32, "xc_" + key)
+                x_scales[s, b] = keep_tile([P, 256], U8, "xs_" + key)
+        w_codes = {}
+        w_planes = {}
+        for j in range(NJ):
+            for g in range(NX):
+                w_codes[j, g] = keep_tile([P, N], U32, "wc_%d_%d" % (j, g))
+                w_planes[j, g] = keep_tile([P, N], U8, "wp_%d_%d" % (j, g))
+
+        def turn_bank(i):
+            return psum.tile([P, N], F32, tag="turn", name="turn", bufs=2)
+
+        def h0_turn(g, pair):
+            bank = turn_bank(pair)
+            for b in range(2):
+                words = h0_raw[2 * pair + b][:].bitcast(F32)
+                for u in range(2):
+                    nc.tensor.transpose(
+                        bank[:, 256 * u + P * b : 256 * u + P * b + P],
+                        words[:, 256 * g + u : 256 * g + 256 : 2],
+                        ident[:],
+                    )
+            nc.vector.tensor_tensor(
+                out=r_grp[1, g, pair][:].rearrange("p (b u e) -> p b u e", u=2, e=2),
+                in0=bank[:].bitcast(BF16).rearrange("p (u b e) -> p b u e", u=2, e=2),
+                in1=gain_col[:, g, :].rearrange("p (u e) -> p u e", e=2).unsqueeze(1).to_broadcast([P, 256, 2, 2]),
+                op=MULT,
+            )
+
+        def r_quant(s, g, pair):
+            nc.vector.quantize_mx(
+                out=r_codes[s, g, pair][:].bitcast(E4M3X4), scales=r_scales[s, g, pair][:], in_=r_grp[s, g, pair][:]
+            )
+
+        def x_turn(s, b, engine):
+            bank = turn_bank(b % 2)
+            words = x_raw[s, b][:].bitcast(F32)
+            for g in range(NX):
+                for u in range(2):
+                    nc.tensor.transpose(
+                        bank[:, 256 * g + P * u : 256 * g + P * u + P],
+                        words[:, 256 * g + u : 256 * g + 256 : 2],
+                        ident[:],
+                    )
+            dst = x_grp[s, b][:].bitcast(F32).rearrange("p (g r u) -> p g r u", g=2, u=2)
+            frm = bank[:].rearrange("p (g u r) -> p g r u", g=2, u=2)
+            if engine == "scalar":
+                nc.scalar.copy(out=dst, in_=frm)
+            else:
+                nc.vector.tensor_copy(out=dst, in_=frm)
+
+        def x_quant(s, b):
+            nc.vector.quantize_mx(
+                out=x_codes[s, b][:].bitcast(E4M3X4), scales=x_scales[s, b][:], in_=x_grp[s, b][:]
+            )
+
+        wide = {}
+        w_grp = {}
+
+        def w_widen(j, g, n_scalar):
+            wide[j, g] = work.tile([P, 4, N], BF16, tag="wide", name="wide", align_bytes=64, bufs=6)
+            raw, c0 = w_raw[j, g]
+            for t in range(4):
+                src = raw[:, t, c0 : c0 + N].bitcast(E4M3)
+                if t < n_scalar:
+                    nc.scalar.activation(out=wide[j, g][:, t, :], in_=src, func=COPY, scale=w_sc[:, g, t : t + 1])
+                else:
+                    nc.vector.tensor_scalar(
+                        out=wide[j, g][:, t, :], in0=src, scalar1=w_sc[:, g, t : t + 1], scalar2=None, op0=MULT
+                    )
+
+        def w_weave(j, g):
+            w_grp[j, g] = work.tile([P, 4 * N], BF16, tag="w_grp", name="w_grp", align_bytes=64)
+            nc.vector.tensor_copy(
+                out=w_grp[j, g][:].rearrange("p (c i t) -> p c t i", i=4, t=4),
+                in_=wide[j, g][:].rearrange("p t (c i) -> p c t i", i=4),
+            )
+
+        def w_quant(j, g):
+            nc.vector.quantize_mx(
+                out=w_codes[j, g][:].bitcast(E4M3X4), scales=w_planes[j, g][:], in_=w_grp[j, g][:]
+            )
+
+        acc = {}
+
+        def open_group(s, j, b):
+            acc[s, j, b] = psum.tile([P, N], F32, tag="acc", name="acc", bufs=6)
+
+        def u_pass(s, j, b, g, start, stop):
+            pair, half = b // 2, P * (b % 2)
+            nc.tensor.matmul_mx(
+                out=acc[s, j, b][:],
+                lhsT=r_codes[s, g, pair][:, half : half + P].bitcast(E4M3X4),
+                lhsT_scale=r_scales[s, g, pair][:, half : half + P],
+                rhs=u_sb[g][:, 2 * N * j : 2 * N * j + 2 * N].bitcast(E2M1X4),
+                rhs_scale=u_planes[:, g, N * j : N * j + N],
+                start=start,
+                stop=stop,
+            )
+
+        def w_pass(s, j, b, g, start, stop):
+            nc.tensor.matmul_mx(
+                out=acc[s, j, b][:],
+                lhsT=x_codes[s, b][:, P * g : P * g + P].bitcast(E4M3X4),
+                lhsT_scale=x_scales[s, b][:, P * g : P * g + P],
+                rhs=w_codes[j, g][:].bitcast(E4M3X4),
+                rhs_scale=w_planes[j, g][:],
+                start=start,
+                stop=stop,
+            )
+
+        h_sb = {}
+        scaled = {}
+
+        def finish(s, j, b):
+            h = outs.tile([P, N], F32, tag="h", name="h")
+            h_sb[s, j, b] = h
+            nc.scalar.activation(out=h[:], in_=acc[s, j, b][:], func=TANH)
+            out = out_0 if s == 1 else out_1
+            nc.sync.dma_start(out=out[P * b : P * b + P, N * j : N * j + N], in_=h[:])
+
+        def h1_scale(j, b):
+            t = work.tile([P, N], BF16, tag="scaled", name="scaled", bufs=4)
+            scaled[j, b] = t
+            nc.vector.tensor_tensor(
+                out=t[:].rearrange("p (u w e) -> p u w e", u=2, e=2),
+                in0=h_sb[1, j, b][:].rearrange("p (w u e) -> p u w e", u=2, e=2),
+                in1=gain_row[:, N * j : N * j + N].rearrange("p (w u e) -> p u w e", u=2, e=2),
+                op=MULT,
+            )
+
+        def h1_turn(j, pair):
+            bank = turn_bank(pair)
+            for b in range(2):
+                words = scaled[j, 2 * pair + b][:].bitcast(F32)
+                for u in range(2):
+                    nc.tensor.transpose(
+                        bank[:, 256 * u + P * b : 256 * u + P * b + P], words[:, P * u : P * u + P], ident[:]
+                    )
+            nc.scalar.copy(
+                out=r_grp[2, j, pair][:].bitcast(F32).rearrange("p (b u) -> p b u", u=2),
+                in_=bank[:].rearrange("p (u b) -> p b u", u=2),
+            )
+
+        def w_both(s, j, b, first, last):
+            w_pass(s, j, b, 0, first, False)
+            w_pass(s, j, b, 1, False, last)
+
+        for g in range(NJ):
+            h0_turn(g, 0)
+            r_quant(1, g, 0)
+        pair0 = [(j, b) for j in range(NJ) for b in (0, 1)]
+        pair1 = [(j, b) for j in range(NJ) for b in (2, 3)]
+        for j, b in pair0:
+            open_group(1, j, b)
+            u_pass(1, j, b, 0, True, False)
+        w_widen(0, 0, 3)
+        for g in range(NJ):
+            h0_turn(g, 1)
+            r_quant(1, g, 1)
+        w_weave(0, 0)
+        w_quant(0, 0)
+        for j, b in pair0:
+            u_pass(1, j, b, 1, False, False)
+        w_widen(0, 1, 3)
+        for b in (0, 1):
+            x_turn(1, b, "scalar")
+            x_quant(1, b)
+        w_weave(0, 1)
+        w_quant(0, 1)
+        for j, b in pair0:
+            u_pass(1, j, b, 2, False, False)
+        for b in (2, 3):
+            x_turn(1, b, "scalar")
+            x_quant(1, b)
+        w_widen(1, 0, 3)
+        w_weave(1, 0)
+        w_quant(1, 0)
+        for b in (0, 1):
+            w_both(1, 0, b, False, True)
+            finish(1, 0, b)
+        w_widen(1, 1, 3)
+        w_weave(1, 1)
+        w_quant(1, 1)
+        for b in (0, 1):
+            x_turn(2, b, "vector")
+            x_quant(2, b)
+        for b in (2, 3):
+            open_group(1, 0, b)
+            for g in range(NJ):
+                u_pass(1, 0, b, g, g == 0, False)
+            w_both(1, 0, b, False, True)
+            finish(1, 0, b)
+        for b in (0, 1):
+            w_both(1, 1, b, False, True)
+            finish(1, 1, b)
+        w_widen(2, 0, 3)
+        w_weave(2, 0)
+        w_quant(2, 0)
+        w_widen(2, 1, 3)
+        w_weave(2, 1)
+        w_quant(2, 1)
+        for b in (2, 3):
+            x_turn(2, b, "scalar")
+            x_quant(2, b)
+        for b in (2, 3):
+            open_group(1, 1, b)
+            for g in range(NJ):
+                u_pass(1, 1, b, g, g == 0, False)
+            w_both(1, 1, b, False, True)
+            finish(1, 1, b)
+
+        def h1_stage(j, pair):
+            for b in (2 * pair, 2 * pair + 1):
+                h1_scale(j, b)
+            h1_turn(j, pair)
+            r_quant(2, j, pair)
+
+        h1_stage(0, 0)
+        for b in (0, 1):
+            open_group(2, 0, b)
+            w_both(2, 0, b, True, False)
+        for b in (2, 3):
+            open_group(1, 2, b)
+            for g in range(NJ):
+                u_pass(1, 2, b, g, g == 0, False)
+        for b in (0, 1, 2, 3):
+            w_both(1, 2, b, False, True)
+            finish(1, 2, b)
+        h1_stage(1, 0)
+        h1_stage(2, 0)
+        h1_stage(0, 1)
+        h1_stage(1, 1)
+        h1_stage(2, 1)
+
+        for b in (0, 1):
+            open_group(2, 1, b)
+            w_both(2, 1, b, True, False)
+            open_group(2, 2, b)
+            w_both(2, 2, b, True, False)
+        for g in range(NJ):
+            for j, b in pair0:
+                u_pass(2, j, b, g, False, g == NJ - 1)
+        for j, b in pair0:
+            finish(2, j, b)
+        for j, b in pair1:
+            open_group(2, j, b)
+            w_both(2, j, b, True, False)
+            for g in range(NJ):
+                u_pass(2, j, b, g, False, g == NJ - 1)
+            finish(2, j, b)

@@ -23,6 +23,7 @@ N = 512
 NB = B // P
 NJ = H // N
 NX = D // N
+ALIGN = 256
 
 
 def tile_two_step_rnn_fp4_s3_kernel(tc, x1, x2, h0, gain, w_bytes, w_scale, u_words, u_scales, out_0, out_1):
@@ -30,45 +31,40 @@ def tile_two_step_rnn_fp4_s3_kernel(tc, x1, x2, h0, gain, w_bytes, w_scale, u_wo
     with ExitStack() as ctx:
         keep = ctx.enter_context(tc.tile_pool(name="keep", bufs=1))
         work = ctx.enter_context(tc.tile_pool(name="work", bufs=3))
-        outs = ctx.enter_context(tc.tile_pool(name="outs", bufs=12))
         psum = ctx.enter_context(tc.psum_pool(name="psum", bufs=1))
+        ctx.enter_context(tc.manual_schedule())
 
         def keep_tile(shape, dtype, name):
-            return keep.tile(shape, dtype, name=name, align_bytes=64)
+            return keep.tile(shape, dtype, name=name, align_bytes=ALIGN)
 
-        warm = keep_tile([P, 16], F32, "warm")
-        nc.vector.memset(warm[:], 0.0)
-        nc.scalar.activation(out=warm[:, 0:1], in_=warm[:, 8:9], func=TANH)
-        ident = keep_tile([P, P], F32, "ident")
-        make_identity(nc, ident[:])
-        u_planes = keep_tile([P, NJ, H], U8, "u_planes")
-        nc.vector.memset(u_planes[:].rearrange("p g n -> p (g n)").bitcast(I32), 0)
+        def bank_tile(i):
+            return psum.tile([P, N], F32, tag="bank%d" % i, name="bank%d" % i)
 
-        gain_col = keep_tile([P, NJ, 4], BF16, "gain_col")
-        nc.scalar.dma_start(out=gain_col[:], in_=gain.rearrange("(g p t) -> p g t", p=P, t=4))
-        w_sc = keep_tile([P, NX, 4], F32, "w_sc")
-        nc.scalar.dma_start(out=w_sc[:], in_=w_scale.rearrange("(g p t) o -> p g (t o)", p=P, t=4))
-
-        h0_raw = {}
-        u_sb = {}
-        w_raw = {}
-        x_raw = {}
+        h0_raw, u_sb, u_planes, w_raw, x_raw = {}, {}, {}, {}, {}
 
         def load_h0(b):
-            t = keep_tile([P, H], BF16, "h0_%d" % b)
-            nc.sync.dma_start(out=t[:], in_=h0[P * b : P * b + P, :])
-            h0_raw[b] = t
+            h0_raw[b] = keep_tile([P, H], BF16, "h0_%d" % b)
+            nc.sync.dma_start(out=h0_raw[b][:], in_=h0[P * b : P * b + P, :])
 
-        def load_u(g):
-            t = keep_tile([P, 2 * H], U8, "u_%d" % g)
-            nc.sync.dma_start(out=t[:].bitcast(I32), in_=u_words[g].bitcast(I32))
-            u_sb[g] = t
+        def load_u(j):
+            u_sb[j] = keep_tile([P, NJ, 2 * N], U8, "u_%d" % j)
+            nc.sync.dma_start(
+                out=u_sb[j][:].bitcast(I32),
+                in_=u_words[:, :, 2 * N * j : 2 * N * j + 2 * N].rearrange("g p n -> p g n").bitcast(I32),
+            )
 
-        def load_u_scales():
-            for q in range(4):
+        def zero_u_scales(j0, j1):
+            t = keep_tile([P, NJ, N * (j1 - j0)], U8, "us_%d" % j0)
+            nc.vector.memset(t[:].rearrange("p g n -> p (g n)").bitcast(I32), 0)
+            for j in range(j0, j1):
+                u_planes[j] = (t, N * (j - j0))
+
+        def load_u_scales(j0, j1):
+            t = u_planes[j0][0]
+            for r in range(4):
                 nc.sync.dma_start(
-                    out=u_planes[32 * q : 32 * q + 4, :, :].bitcast(I32),
-                    in_=u_scales[:, 4 * q : 4 * q + 4, :].rearrange("g q n -> q g n").bitcast(I32),
+                    out=t[r:P:32, :, :].bitcast(I32),
+                    in_=u_scales[:, r:16:4, N * j0 : N * j1].rearrange("g q n -> q g n").bitcast(I32),
                 )
 
         def load_w(g, j0, j1):
@@ -80,108 +76,83 @@ def tile_two_step_rnn_fp4_s3_kernel(tc, x1, x2, h0, gain, w_bytes, w_scale, u_wo
             for j in range(j0, j1):
                 w_raw[j, g] = (t, N * (j - j0))
 
-        def load_x(s, x, bs):
-            for b in bs:
-                t = keep_tile([P, D], BF16, "x%d_%d" % (s, b))
-                nc.sync.dma_start(out=t[:], in_=x[P * b : P * b + P, :])
-                x_raw[s, b] = t
+        def load_x(s, b):
+            x_raw[s, b] = keep_tile([P, D], BF16, "x%d_%d" % (s, b))
+            nc.sync.dma_start(out=x_raw[s, b][:], in_=(x1 if s == 1 else x2)[P * b : P * b + P, :])
 
-        load_h0(0)
-        load_h0(1)
-        load_u_scales()
-        load_u(0)
-        load_w(0, 0, 1)
-        load_h0(2)
-        load_h0(3)
-        load_u(1)
-        load_w(1, 0, 1)
-        load_x(1, x1, [0, 1])
-        load_u(2)
-        load_w(0, 1, 3)
-        load_x(1, x1, [2, 3])
-        load_w(1, 1, 3)
-        load_x(2, x2, [0, 1, 2, 3])
-        gain_row = keep_tile([P, H], BF16, "gain_row")
-        nc.sync.dma_start(out=gain_row[:], in_=gain.partition_broadcast(P))
+        r_op, x_op, w_op = {}, {}, {}
+        turned, grouped = {}, {}
 
-        r_grp, r_codes, r_scales = {}, {}, {}
-        for s in (1, 2):
-            for g in range(NJ):
-                for pair in range(2):
-                    key = "%d_%d_%d" % (s, g, pair)
-                    r_grp[s, g, pair] = keep_tile([P, 1024], BF16, "rg_" + key)
-                    r_codes[s, g, pair] = keep_tile([P, 256], U32, "rc_" + key)
-                    r_scales[s, g, pair] = keep_tile([P, 256], U8, "rs_" + key)
-        x_grp, x_codes, x_scales = {}, {}, {}
-        for s in (1, 2):
-            for b in range(NB):
-                key = "%d_%d" % (s, b)
-                x_grp[s, b] = keep_tile([P, 1024], BF16, "xg_" + key)
-                x_codes[s, b] = keep_tile([P, 256], U32, "xc_" + key)
-                x_scales[s, b] = keep_tile([P, 256], U8, "xs_" + key)
-        w_codes = {}
-        w_planes = {}
-        for j in range(NJ):
-            for g in range(NX):
-                w_codes[j, g] = keep_tile([P, N], U32, "wc_%d_%d" % (j, g))
-                w_planes[j, g] = keep_tile([P, N], U8, "wp_%d_%d" % (j, g))
+        def quantise(key, width):
+            codes = keep_tile([P, width // 4], U32, "c_" + key)
+            scales = keep_tile([P, width // 4], U8, "s_" + key)
+            nc.vector.quantize_mx(out=codes[:].bitcast(E4M3X4), scales=scales[:], in_=grouped[key][:])
+            return codes, scales
 
-        def turn_bank(i):
-            return psum.tile([P, N], F32, tag="turn", name="turn", bufs=2)
+        def turn(key, i, sources):
+            bank = bank_tile(i)
+            n = len(sources)
+            for u in range(2):
+                for c in range(n):
+                    nc.tensor.transpose(bank[:, P * (n * u + c) : P * (n * u + c) + P], sources[c][u], ident[:])
+            turned[key] = (bank, n)
 
-        def h0_turn(g, pair):
-            bank = turn_bank(pair)
-            for b in range(2):
-                words = h0_raw[2 * pair + b][:].bitcast(F32)
-                for u in range(2):
-                    nc.tensor.transpose(
-                        bank[:, 256 * u + P * b : 256 * u + P * b + P],
-                        words[:, 256 * g + u : 256 * g + 256 : 2],
-                        ident[:],
-                    )
+        def every_second(raw, g):
+            words = raw[:].bitcast(F32)
+            return [words[:, 256 * g + u : 256 * g + 256 : 2] for u in range(2)]
+
+        def h0_turn(b, gs, i):
+            turn("h0_%d_%d" % (b, gs[0]), i, [every_second(h0_raw[b], g) for g in gs])
+
+        def h0_empty(b, gs):
+            key = "h0_%d_%d" % (b, gs[0])
+            bank, n = turned[key]
+            grouped[key] = keep_tile([P, N * n], BF16, "g_" + key)
             nc.vector.tensor_tensor(
-                out=r_grp[1, g, pair][:].rearrange("p (b u e) -> p b u e", u=2, e=2),
-                in0=bank[:].bitcast(BF16).rearrange("p (u b e) -> p b u e", u=2, e=2),
-                in1=gain_col[:, g, :].rearrange("p (u e) -> p u e", e=2).unsqueeze(1).to_broadcast([P, 256, 2, 2]),
+                out=grouped[key][:].rearrange("p (g r u e) -> p g r u e", g=n, u=2, e=2),
+                in0=bank[:, 0 : 2 * P * n].bitcast(BF16).rearrange("p (u g r e) -> p g r u e", u=2, g=n, e=2),
+                in1=gain_col[:, gs[0] : gs[0] + n, :]
+                .rearrange("p g (u e) -> p g u e", e=2)
+                .unsqueeze(2)
+                .to_broadcast([P, n, P, 2, 2]),
                 op=MULT,
             )
 
-        def r_quant(s, g, pair):
-            nc.vector.quantize_mx(
-                out=r_codes[s, g, pair][:].bitcast(E4M3X4), scales=r_scales[s, g, pair][:], in_=r_grp[s, g, pair][:]
-            )
+        def h0_quant(b, gs):
+            codes, scales = quantise("h0_%d_%d" % (b, gs[0]), N * len(gs))
+            for c, g in enumerate(gs):
+                r_op[1, b, g] = (codes, scales, P * c)
 
-        def x_turn(s, b, engine):
-            bank = turn_bank(b % 2)
-            words = x_raw[s, b][:].bitcast(F32)
-            for g in range(NX):
-                for u in range(2):
-                    nc.tensor.transpose(
-                        bank[:, 256 * g + P * u : 256 * g + P * u + P],
-                        words[:, 256 * g + u : 256 * g + 256 : 2],
-                        ident[:],
-                    )
-            dst = x_grp[s, b][:].bitcast(F32).rearrange("p (g r u) -> p g r u", g=2, u=2)
-            frm = bank[:].rearrange("p (g u r) -> p g r u", g=2, u=2)
+        def empty(key, engine):
+            bank, n = turned[key]
+            grouped[key] = keep_tile([P, N * n], BF16, "g_" + key)
+            dst = grouped[key][:].bitcast(F32).rearrange("p (r u) -> p r u", u=2)
+            frm = bank[:, 0 : 2 * P * n].rearrange("p (u r) -> p r u", u=2)
             if engine == "scalar":
                 nc.scalar.copy(out=dst, in_=frm)
             else:
                 nc.vector.tensor_copy(out=dst, in_=frm)
 
+        def x_turn(s, b, i):
+            turn("x%d_%d" % (s, b), i, [every_second(x_raw[s, b], g) for g in range(NX)])
+
+        def x_empty(s, b, engine):
+            empty("x%d_%d" % (s, b), engine)
+
         def x_quant(s, b):
-            nc.vector.quantize_mx(
-                out=x_codes[s, b][:].bitcast(E4M3X4), scales=x_scales[s, b][:], in_=x_grp[s, b][:]
-            )
+            codes, scales = quantise("x%d_%d" % (s, b), D)
+            for g in range(NX):
+                x_op[s, b, g] = (codes, scales, P * g)
 
         wide = {}
-        w_grp = {}
 
-        def w_widen(j, g, n_scalar):
-            wide[j, g] = work.tile([P, 4, N], BF16, tag="wide", name="wide", align_bytes=64, bufs=6)
+        def w_widen(j, g, ts, engine):
+            if (j, g) not in wide:
+                wide[j, g] = work.tile([P, 4, N], BF16, tag="wide", name="wide", align_bytes=ALIGN, bufs=6)
             raw, c0 = w_raw[j, g]
-            for t in range(4):
+            for t in ts:
                 src = raw[:, t, c0 : c0 + N].bitcast(E4M3)
-                if t < n_scalar:
+                if engine == "scalar":
                     nc.scalar.activation(out=wide[j, g][:, t, :], in_=src, func=COPY, scale=w_sc[:, g, t : t + 1])
                 else:
                     nc.vector.tensor_scalar(
@@ -189,182 +160,295 @@ def tile_two_step_rnn_fp4_s3_kernel(tc, x1, x2, h0, gain, w_bytes, w_scale, u_wo
                     )
 
         def w_weave(j, g):
-            w_grp[j, g] = work.tile([P, 4 * N], BF16, tag="w_grp", name="w_grp", align_bytes=64)
+            key = "w_%d_%d" % (j, g)
+            grouped[key] = work.tile([P, 4 * N], BF16, tag="w_grp", name="w_grp", align_bytes=ALIGN)
             nc.vector.tensor_copy(
-                out=w_grp[j, g][:].rearrange("p (c i t) -> p c t i", i=4, t=4),
+                out=grouped[key][:].rearrange("p (c i t) -> p c t i", i=4, t=4),
                 in_=wide[j, g][:].rearrange("p t (c i) -> p c t i", i=4),
             )
 
         def w_quant(j, g):
-            nc.vector.quantize_mx(
-                out=w_codes[j, g][:].bitcast(E4M3X4), scales=w_planes[j, g][:], in_=w_grp[j, g][:]
-            )
+            w_op[j, g] = quantise("w_%d_%d" % (j, g), 4 * N)
 
         acc = {}
 
-        def open_group(s, j, b):
-            acc[s, j, b] = psum.tile([P, N], F32, tag="acc", name="acc", bufs=6)
+        def open_group(s, b, j, i):
+            acc[s, b, j] = bank_tile(i)
 
-        def u_pass(s, j, b, g, start, stop):
-            pair, half = b // 2, P * (b % 2)
+        def u_pass(s, b, j, g, start=False, stop=False, c0=0, c1=N):
+            codes, scales, c = r_op[s, b, g]
+            plane, p0 = u_planes[j]
             nc.tensor.matmul_mx(
-                out=acc[s, j, b][:],
-                lhsT=r_codes[s, g, pair][:, half : half + P].bitcast(E4M3X4),
-                lhsT_scale=r_scales[s, g, pair][:, half : half + P],
-                rhs=u_sb[g][:, 2 * N * j : 2 * N * j + 2 * N].bitcast(E2M1X4),
-                rhs_scale=u_planes[:, g, N * j : N * j + N],
+                out=acc[s, b, j][:, 0 : c1 - c0],
+                lhsT=codes[:, c : c + P].bitcast(E4M3X4),
+                lhsT_scale=scales[:, c : c + P],
+                rhs=u_sb[j][:, g, 2 * c0 : 2 * c1].bitcast(E2M1X4),
+                rhs_scale=plane[:, g, p0 + c0 : p0 + c1],
                 start=start,
                 stop=stop,
             )
 
-        def w_pass(s, j, b, g, start, stop):
+        def w_pass(s, b, j, g, start=False, stop=False, c0=0, c1=N):
+            codes, scales, c = x_op[s, b, g]
             nc.tensor.matmul_mx(
-                out=acc[s, j, b][:],
-                lhsT=x_codes[s, b][:, P * g : P * g + P].bitcast(E4M3X4),
-                lhsT_scale=x_scales[s, b][:, P * g : P * g + P],
-                rhs=w_codes[j, g][:].bitcast(E4M3X4),
-                rhs_scale=w_planes[j, g][:],
+                out=acc[s, b, j][:, 0 : c1 - c0],
+                lhsT=codes[:, c : c + P].bitcast(E4M3X4),
+                lhsT_scale=scales[:, c : c + P],
+                rhs=w_op[j, g][0][:, c0:c1].bitcast(E4M3X4),
+                rhs_scale=w_op[j, g][1][:, c0:c1],
                 start=start,
                 stop=stop,
             )
 
-        h_sb = {}
-        scaled = {}
+        h_sb, scaled = {}, {}
 
-        def finish(s, j, b):
-            h = outs.tile([P, N], F32, tag="h", name="h")
-            h_sb[s, j, b] = h
-            nc.scalar.activation(out=h[:], in_=acc[s, j, b][:], func=TANH)
+        def finish(s, b, j, c0=0, c1=N):
+            h = work.tile([P, N], F32, tag="h", name="h", align_bytes=ALIGN, bufs=12)
+            h_sb[s, b, j] = h
+            nc.scalar.activation(out=h[:, 0 : c1 - c0], in_=acc[s, b, j][:, 0 : c1 - c0], func=TANH)
             out = out_0 if s == 1 else out_1
-            nc.sync.dma_start(out=out[P * b : P * b + P, N * j : N * j + N], in_=h[:])
+            nc.sync.dma_start(out=out[P * b : P * b + P, N * j + c0 : N * j + c1], in_=h[:, 0 : c1 - c0])
 
-        def h1_scale(j, b):
-            t = work.tile([P, N], BF16, tag="scaled", name="scaled", bufs=4)
-            scaled[j, b] = t
+        def h1_scale(b, j):
+            scaled[b, j] = work.tile([P, N], BF16, tag="scaled", name="scaled", align_bytes=ALIGN, bufs=8)
             nc.vector.tensor_tensor(
-                out=t[:].rearrange("p (u w e) -> p u w e", u=2, e=2),
-                in0=h_sb[1, j, b][:].rearrange("p (w u e) -> p u w e", u=2, e=2),
-                in1=gain_row[:, N * j : N * j + N].rearrange("p (w u e) -> p u w e", u=2, e=2),
+                out=scaled[b, j][:].rearrange("p (u w e) -> p u w e", u=2, e=2),
+                in0=h_sb[1, b, j][:].rearrange("p (w u e) -> p u w e", u=2, e=2),
+                in1=gain_row[:, j, :].rearrange("p (u w e) -> p u w e", u=2, e=2),
                 op=MULT,
             )
 
-        def h1_turn(j, pair):
-            bank = turn_bank(pair)
-            for b in range(2):
-                words = scaled[j, 2 * pair + b][:].bitcast(F32)
-                for u in range(2):
-                    nc.tensor.transpose(
-                        bank[:, 256 * u + P * b : 256 * u + P * b + P], words[:, P * u : P * u + P], ident[:]
+        def h1_key(parts):
+            return "h1_%d_%d" % parts[0]
+
+        def h1_turn(parts, i):
+            sources = []
+            for b, j in parts:
+                words = scaled[b, j][:].bitcast(F32)
+                sources.append([words[:, P * u : P * u + P] for u in range(2)])
+            turn(h1_key(parts), i, sources)
+
+        def h1_empty(parts, engine):
+            empty(h1_key(parts), engine)
+
+        def h1_quant(parts):
+            codes, scales = quantise(h1_key(parts), N * len(parts))
+            for c, (b, j) in enumerate(parts):
+                r_op[2, b, j] = (codes, scales, P * c)
+
+        def u_group(b, j, i):
+            open_group(1, b, j, i)
+            for g in range(NJ):
+                u_pass(1, b, j, g, start=g == 0)
+
+        def w_close(b, j):
+            w_pass(1, b, j, 0)
+            w_pass(1, b, j, 1, stop=True)
+
+        def spread_gain(banks):
+            tiles = [bank_tile(i) for i in banks]
+            for g in range(NJ):
+                for t in range(4):
+                    nc.tensor.matmul(
+                        tiles[g][:, P * t : P * t + P],
+                        lhsT=gain_col[:, g, t : t + 1].to_broadcast([P, P]),
+                        rhs=ident_bf[:],
+                        start=True,
+                        stop=True,
                     )
-            nc.scalar.copy(
-                out=r_grp[2, j, pair][:].bitcast(F32).rearrange("p (b u) -> p b u", u=2),
-                in_=bank[:].rearrange("p (u b) -> p b u", u=2),
-            )
+            for g in range(NJ):
+                nc.scalar.copy(
+                    out=gain_row[:, g, :].rearrange("p (u w e) -> p u w e", u=2, e=2),
+                    in_=tiles[g][:].rearrange("p (u e w) -> p u w e", u=2, e=2),
+                )
 
-        def w_both(s, j, b, first, last):
-            w_pass(s, j, b, 0, first, False)
-            w_pass(s, j, b, 1, False, last)
+        gain_col = keep_tile([P, NJ, 4], BF16, "gain_col")
+        nc.scalar.dma_start(out=gain_col[:], in_=gain.rearrange("(g p t) -> p g t", p=P, t=4))
+        w_sc = keep_tile([P, NX, 4], F32, "w_sc")
+        nc.scalar.dma_start(out=w_sc[:], in_=w_scale.rearrange("(g p t) o -> p g (t o)", p=P, t=4))
+        ident = keep_tile([P, P], F32, "ident")
+        make_identity(nc, ident[:])
+        zero_u_scales(0, 1)
+        zero_u_scales(1, 3)
+        ident_bf = keep_tile([P, P], BF16, "ident_bf")
+        nc.vector.tensor_copy(out=ident_bf[:], in_=ident[:])
+        gain_row = keep_tile([P, NJ, N], BF16, "gain_row")
 
-        for g in range(NJ):
-            h0_turn(g, 0)
-            r_quant(1, g, 0)
-        pair0 = [(j, b) for j in range(NJ) for b in (0, 1)]
-        pair1 = [(j, b) for j in range(NJ) for b in (2, 3)]
-        for j, b in pair0:
-            open_group(1, j, b)
-            u_pass(1, j, b, 0, True, False)
-        w_widen(0, 0, 3)
-        for g in range(NJ):
-            h0_turn(g, 1)
-            r_quant(1, g, 1)
+        load_h0(0)
+        load_u(0)
+        load_h0(1)
+        load_u_scales(0, 1)
+        load_w(0, 0, 1)
+        load_h0(2)
+        load_w(1, 0, 1)
+        load_h0(3)
+        load_x(1, 0)
+        load_x(1, 1)
+        load_u(1)
+        load_u_scales(1, 3)
+        load_w(0, 1, 3)
+        load_x(1, 2)
+        load_x(1, 3)
+        load_w(1, 1, 3)
+        load_u(2)
+        for b in range(NB):
+            load_x(2, b)
+
+        A, Bk = (0, 1), (2,)
+
+        def h0_turns(b, i0, i1):
+            h0_turn(b, A, i0)
+            h0_turn(b, Bk, i1)
+
+        def h0_ready(b):
+            h0_empty(b, A)
+            h0_empty(b, Bk)
+            h0_quant(b, A)
+            h0_quant(b, Bk)
+
+        spread_gain((1, 2, 3))
+        h0_turns(0, 6, 7)
+        h0_ready(0)
+        h0_turns(1, 4, 5)
+        h0_ready(1)
+        u_group(0, 0, 0)
+        w_widen(0, 0, (0, 1, 2), "scalar")
+        w_widen(0, 0, (3,), "vector")
         w_weave(0, 0)
+        h0_turns(2, 6, 7)
+        h0_ready(2)
+        u_group(1, 0, 1)
+        w_widen(0, 1, range(4), "scalar")
         w_quant(0, 0)
-        for j, b in pair0:
-            u_pass(1, j, b, 1, False, False)
-        w_widen(0, 1, 3)
-        for b in (0, 1):
-            x_turn(1, b, "scalar")
-            x_quant(1, b)
+        h0_turns(3, 4, 5)
+        h0_ready(3)
         w_weave(0, 1)
+        u_group(2, 0, 2)
+        x_turn(1, 0, 6)
+        x_turn(1, 1, 7)
+        x_empty(1, 0, "scalar")
+        x_empty(1, 1, "scalar")
+        w_widen(1, 0, range(4), "scalar")
+        x_quant(1, 0)
         w_quant(0, 1)
-        for j, b in pair0:
-            u_pass(1, j, b, 2, False, False)
-        for b in (2, 3):
-            x_turn(1, b, "scalar")
-            x_quant(1, b)
-        w_widen(1, 0, 3)
+        x_quant(1, 1)
+        u_group(3, 0, 3)
+        u_group(0, 1, 4)
+        x_turn(1, 2, 6)
+        x_turn(1, 3, 7)
+        w_widen(1, 1, (0, 1), "vector")
+        x_empty(1, 2, "scalar")
+        x_empty(1, 3, "scalar")
+        w_widen(1, 1, (2, 3), "scalar")
         w_weave(1, 0)
+        x_quant(1, 2)
+        x_quant(1, 3)
         w_quant(1, 0)
-        for b in (0, 1):
-            w_both(1, 0, b, False, True)
-            finish(1, 0, b)
-        w_widen(1, 1, 3)
+        u_group(1, 1, 5)
+        for b in range(NB):
+            w_close(b, 0)
+        finish(1, 0, 0)
+        finish(1, 1, 0)
         w_weave(1, 1)
+        w_widen(2, 0, (0, 1), "vector")
         w_quant(1, 1)
-        for b in (0, 1):
-            x_turn(2, b, "vector")
-            x_quant(2, b)
-        for b in (2, 3):
-            open_group(1, 0, b)
-            for g in range(NJ):
-                u_pass(1, 0, b, g, g == 0, False)
-            w_both(1, 0, b, False, True)
-            finish(1, 0, b)
-        for b in (0, 1):
-            w_both(1, 1, b, False, True)
-            finish(1, 1, b)
-        w_widen(2, 0, 3)
+        u_group(2, 1, 0)
+        u_group(3, 1, 1)
+        w_widen(2, 0, (2, 3), "scalar")
+        finish(1, 2, 0)
+        finish(1, 3, 0)
+        w_widen(2, 1, range(4), "scalar")
+        x_turn(2, 0, 6)
+        x_turn(2, 1, 7)
+        for b in range(NB):
+            w_close(b, 1)
         w_weave(2, 0)
+        x_empty(2, 0, "vector")
         w_quant(2, 0)
-        w_widen(2, 1, 3)
         w_weave(2, 1)
+        x_empty(2, 1, "vector")
         w_quant(2, 1)
-        for b in (2, 3):
-            x_turn(2, b, "scalar")
-            x_quant(2, b)
-        for b in (2, 3):
-            open_group(1, 1, b)
-            for g in range(NJ):
-                u_pass(1, 1, b, g, g == 0, False)
-            w_both(1, 1, b, False, True)
-            finish(1, 1, b)
-
-        def h1_stage(j, pair):
-            for b in (2 * pair, 2 * pair + 1):
-                h1_scale(j, b)
-            h1_turn(j, pair)
-            r_quant(2, j, pair)
-
-        h1_stage(0, 0)
+        finish(1, 0, 1)
+        finish(1, 1, 1)
+        u_group(0, 2, 2)
+        u_group(1, 2, 3)
+        finish(1, 2, 1)
+        finish(1, 3, 1)
+        u_group(2, 2, 4)
+        u_group(3, 2, 5)
+        first = [[(b, 0), (b, 1)] for b in range(NB)]
+        last = [[(0, 2), (1, 2)], [(2, 2), (3, 2)]]
         for b in (0, 1):
-            open_group(2, 0, b)
-            w_both(2, 0, b, True, False)
+            h1_scale(b, 0)
+            h1_scale(b, 1)
+        x_quant(2, 0)
+        x_quant(2, 1)
+        for b in range(NB):
+            w_close(b, 2)
+        h1_turn(first[0], 6)
+        h1_turn(first[1], 7)
+        finish(1, 0, 2)
+        finish(1, 1, 2)
+        h1_empty(first[0], "scalar")
+        h1_empty(first[1], "scalar")
+        finish(1, 2, 2)
+        finish(1, 3, 2)
+        h1_scale(0, 2)
+        h1_scale(1, 2)
+        h1_quant(first[0])
+        h1_quant(first[1])
         for b in (2, 3):
-            open_group(1, 2, b)
-            for g in range(NJ):
-                u_pass(1, 2, b, g, g == 0, False)
-        for b in (0, 1, 2, 3):
-            w_both(1, 2, b, False, True)
-            finish(1, 2, b)
-        h1_stage(1, 0)
-        h1_stage(2, 0)
-        h1_stage(0, 1)
-        h1_stage(1, 1)
-        h1_stage(2, 1)
+            h1_scale(b, 0)
 
-        for b in (0, 1):
-            open_group(2, 1, b)
-            w_both(2, 1, b, True, False)
-            open_group(2, 2, b)
-            w_both(2, 2, b, True, False)
-        for g in range(NJ):
-            for j, b in pair0:
-                u_pass(2, j, b, g, False, g == NJ - 1)
-        for j, b in pair0:
-            finish(2, j, b)
-        for j, b in pair1:
-            open_group(2, j, b)
-            w_both(2, j, b, True, False)
+        def head(b, j, i):
+            open_group(2, b, j, i)
+            w_pass(2, b, j, 0, start=True)
+            w_pass(2, b, j, 1)
+
+        for j in range(NJ):
+            head(0, j, j)
+        h1_turn(last[0], 6)
+        x_turn(2, 2, 7)
+        h1_empty(last[0], "scalar")
+        x_empty(2, 2, "scalar")
+        h1_quant(last[0])
+        for b in (2, 3):
+            h1_scale(b, 1)
+        h1_scale(2, 2)
+        h1_scale(3, 2)
+        x_quant(2, 2)
+        for j in range(NJ):
+            u_pass(2, 0, j, 0)
+            u_pass(2, 0, j, 1)
+        for j in range(NJ):
+            u_pass(2, 0, j, 2, stop=True)
+            finish(2, 0, j)
+        h1_turn(first[2], 6)
+        h1_turn(last[1], 7)
+        h1_empty(first[2], "vector")
+        h1_empty(last[1], "vector")
+        h1_quant(first[2])
+        h1_quant(last[1])
+
+        def group2(b, j, i, c0=0, c1=N):
+            open_group(2, b, j, i)
+            w_pass(2, b, j, 0, start=True, c0=c0, c1=c1)
+            w_pass(2, b, j, 1, c0=c0, c1=c1)
             for g in range(NJ):
-                u_pass(2, j, b, g, False, g == NJ - 1)
-            finish(2, j, b)
+                u_pass(2, b, j, g, stop=g == NJ - 1, c0=c0, c1=c1)
+            finish(2, b, j, c0, c1)
+
+        for j in range(NJ):
+            group2(1, j, 3 + j)
+        h1_turn(first[3], 6)
+        x_turn(2, 3, 7)
+        h1_empty(first[3], "vector")
+        x_empty(2, 3, "vector")
+        h1_quant(first[3])
+        x_quant(2, 3)
+        for j in range(NJ):
+            group2(2, j, j)
+        group2(3, 0, 3)
+        group2(3, 1, 4)
+        group2(3, 2, 5, 0, 256)
+        group2(3, 2, 0, 256, 512)

@@ -133,8 +133,24 @@ def tile_two_step_rnn_fp4_s3_kernel(tc, x1, x2, h0, gain, w_bytes, w_scale, u_wo
             else:
                 nc.vector.tensor_copy(out=dst, in_=frm)
 
+        x_sorted = {}
+
+        def x_sort(s, b, engine):
+            x_sorted[s, b] = keep_tile([P, D], BF16, "xs%d_%d" % (s, b))
+            dst = x_sorted[s, b][:].rearrange("p (u w e) -> p u w e", u=2, e=2)
+            frm = x_raw[s, b][:].rearrange("p (w u e) -> p u w e", u=2, e=2)
+            if engine == "scalar":
+                nc.scalar.copy(out=dst, in_=frm)
+            else:
+                nc.vector.tensor_copy(out=dst, in_=frm)
+
         def x_turn(s, b, i):
-            turn("x%d_%d" % (s, b), i, [every_second(x_raw[s, b], g) for g in range(NX)])
+            if (s, b) in x_sorted:
+                words = x_sorted[s, b][:].bitcast(F32)
+                sources = [[words[:, 256 * u + P * g : 256 * u + P * g + P] for u in range(2)] for g in range(NX)]
+            else:
+                sources = [every_second(x_raw[s, b], g) for g in range(NX)]
+            turn("x%d_%d" % (s, b), i, sources)
 
         def x_empty(s, b, engine):
             empty("x%d_%d" % (s, b), engine)
@@ -214,7 +230,7 @@ def tile_two_step_rnn_fp4_s3_kernel(tc, x1, x2, h0, gain, w_bytes, w_scale, u_wo
             nc.vector.tensor_tensor(
                 out=scaled[b, j][:].rearrange("p (u w e) -> p u w e", u=2, e=2),
                 in0=h_sb[1, b, j][:].rearrange("p (w u e) -> p u w e", u=2, e=2),
-                in1=gain_row[:, j, :].rearrange("p (u w e) -> p u w e", u=2, e=2),
+                in1=gain_row[:, N * j : N * j + N].rearrange("p (w u e) -> p u w e", u=2, e=2),
                 op=MULT,
             )
 
@@ -245,54 +261,40 @@ def tile_two_step_rnn_fp4_s3_kernel(tc, x1, x2, h0, gain, w_bytes, w_scale, u_wo
             w_pass(1, b, j, 0)
             w_pass(1, b, j, 1, stop=True)
 
-        def spread_gain(banks):
-            tiles = [bank_tile(i) for i in banks]
-            for g in range(NJ):
-                for t in range(4):
-                    nc.tensor.matmul(
-                        tiles[g][:, P * t : P * t + P],
-                        lhsT=gain_col[:, g, t : t + 1].to_broadcast([P, P]),
-                        rhs=ident_bf[:],
-                        start=True,
-                        stop=True,
-                    )
-            for g in range(NJ):
-                nc.scalar.copy(
-                    out=gain_row[:, g, :].rearrange("p (u w e) -> p u w e", u=2, e=2),
-                    in_=tiles[g][:].rearrange("p (u e w) -> p u w e", u=2, e=2),
-                )
-
         gain_col = keep_tile([P, NJ, 4], BF16, "gain_col")
         nc.scalar.dma_start(out=gain_col[:], in_=gain.rearrange("(g p t) -> p g t", p=P, t=4))
-        w_sc = keep_tile([P, NX, 4], F32, "w_sc")
-        nc.scalar.dma_start(out=w_sc[:], in_=w_scale.rearrange("(g p t) o -> p g (t o)", p=P, t=4))
         ident = keep_tile([P, P], F32, "ident")
         make_identity(nc, ident[:])
         zero_u_scales(0, 1)
-        zero_u_scales(1, 3)
-        ident_bf = keep_tile([P, P], BF16, "ident_bf")
-        nc.vector.tensor_copy(out=ident_bf[:], in_=ident[:])
-        gain_row = keep_tile([P, NJ, N], BF16, "gain_row")
+        zero_u_scales(1, 2)
+        zero_u_scales(2, 3)
 
         load_h0(0)
-        load_u(0)
         load_h0(1)
+        load_u(0)
         load_u_scales(0, 1)
+        w_sc = keep_tile([P, NX, 4], F32, "w_sc")
+        nc.sync.dma_start(out=w_sc[:], in_=w_scale.rearrange("(g p t) o -> p g (t o)", p=P, t=4))
         load_w(0, 0, 1)
         load_h0(2)
         load_w(1, 0, 1)
         load_h0(3)
         load_x(1, 0)
         load_x(1, 1)
-        load_u(1)
-        load_u_scales(1, 3)
-        load_w(0, 1, 3)
+        load_w(0, 1, 2)
         load_x(1, 2)
         load_x(1, 3)
-        load_w(1, 1, 3)
+        load_u(1)
+        load_u_scales(1, 2)
+        load_w(1, 1, 2)
+        load_w(0, 2, 3)
+        load_w(1, 2, 3)
         load_u(2)
+        load_u_scales(2, 3)
         for b in range(NB):
             load_x(2, b)
+        gain_row = keep_tile([P, H], BF16, "gain_row")
+        nc.sync.dma_start(out=gain_row[:], in_=gain.partition_broadcast(P))
 
         A, Bk = (0, 1), (2,)
 
@@ -306,82 +308,80 @@ def tile_two_step_rnn_fp4_s3_kernel(tc, x1, x2, h0, gain, w_bytes, w_scale, u_wo
             h0_quant(b, A)
             h0_quant(b, Bk)
 
-        spread_gain((1, 2, 3))
         h0_turns(0, 6, 7)
-        h0_ready(0)
         h0_turns(1, 4, 5)
+        h0_ready(0)
         h0_ready(1)
         u_group(0, 0, 0)
-        w_widen(0, 0, (0, 1, 2), "scalar")
-        w_widen(0, 0, (3,), "vector")
-        w_weave(0, 0)
+        w_widen(0, 0, (0, 1), "scalar")
+        w_widen(0, 0, (2, 3), "vector")
         h0_turns(2, 6, 7)
         h0_ready(2)
         u_group(1, 0, 1)
         w_widen(0, 1, range(4), "scalar")
-        w_quant(0, 0)
+        w_weave(0, 0)
         h0_turns(3, 4, 5)
         h0_ready(3)
-        w_weave(0, 1)
         u_group(2, 0, 2)
-        x_turn(1, 0, 6)
-        x_turn(1, 1, 7)
-        x_empty(1, 0, "scalar")
-        x_empty(1, 1, "scalar")
-        w_widen(1, 0, range(4), "scalar")
+        w_widen(1, 0, (0,), "scalar")
+        for b, i in enumerate((6, 7, 4, 5)):
+            x_turn(1, b, i)
+            x_empty(1, b, "scalar")
+        w_quant(0, 0)
+        w_weave(0, 1)
         x_quant(1, 0)
         w_quant(0, 1)
-        x_quant(1, 1)
+        for b in (1, 2, 3):
+            x_quant(1, b)
         u_group(3, 0, 3)
-        u_group(0, 1, 4)
-        x_turn(1, 2, 6)
-        x_turn(1, 3, 7)
-        w_widen(1, 1, (0, 1), "vector")
-        x_empty(1, 2, "scalar")
-        x_empty(1, 3, "scalar")
-        w_widen(1, 1, (2, 3), "scalar")
+        u_group(0, 1, 6)
+        u_group(1, 1, 7)
+        w_widen(1, 0, (1,), "scalar")
+        w_widen(1, 0, (2, 3), "vector")
+        w_widen(1, 1, (0, 1, 2), "scalar")
         w_weave(1, 0)
-        x_quant(1, 2)
-        x_quant(1, 3)
+        w_widen(1, 1, (3,), "vector")
         w_quant(1, 0)
-        u_group(1, 1, 5)
+        w_weave(1, 1)
         for b in range(NB):
             w_close(b, 0)
+        u_group(2, 1, 4)
+        u_group(3, 1, 5)
+        w_widen(2, 0, (0, 1, 2), "scalar")
+        w_widen(2, 0, (3,), "vector")
+        w_quant(1, 1)
         finish(1, 0, 0)
         finish(1, 1, 0)
-        w_weave(1, 1)
-        w_widen(2, 0, (0, 1), "vector")
-        w_quant(1, 1)
-        u_group(2, 1, 0)
-        u_group(3, 1, 1)
-        w_widen(2, 0, (2, 3), "scalar")
-        finish(1, 2, 0)
-        finish(1, 3, 0)
+        u_group(0, 2, 0)
+        u_group(1, 2, 1)
         w_widen(2, 1, range(4), "scalar")
-        x_turn(2, 0, 6)
-        x_turn(2, 1, 7)
+        w_weave(2, 0)
         for b in range(NB):
             w_close(b, 1)
-        w_weave(2, 0)
-        x_empty(2, 0, "vector")
+        finish(1, 2, 0)
+        finish(1, 3, 0)
+        x_sort(2, 0, "vector")
         w_quant(2, 0)
+        x_sort(2, 1, "vector")
         w_weave(2, 1)
-        x_empty(2, 1, "vector")
-        w_quant(2, 1)
         finish(1, 0, 1)
         finish(1, 1, 1)
-        u_group(0, 2, 2)
-        u_group(1, 2, 3)
+        h1_scale(0, 0)
+        w_quant(2, 1)
+        x_turn(2, 0, 6)
+        x_turn(2, 1, 7)
+        u_group(2, 2, 2)
+        u_group(3, 2, 3)
+        x_empty(2, 0, "scalar")
+        x_empty(2, 1, "scalar")
         finish(1, 2, 1)
         finish(1, 3, 1)
-        u_group(2, 2, 4)
-        u_group(3, 2, 5)
         first = [[(b, 0), (b, 1)] for b in range(NB)]
         last = [[(0, 2), (1, 2)], [(2, 2), (3, 2)]]
-        for b in (0, 1):
-            h1_scale(b, 0)
-            h1_scale(b, 1)
+        h1_scale(0, 1)
         x_quant(2, 0)
+        h1_scale(1, 0)
+        h1_scale(1, 1)
         x_quant(2, 1)
         for b in range(NB):
             w_close(b, 2)
@@ -395,40 +395,36 @@ def tile_two_step_rnn_fp4_s3_kernel(tc, x1, x2, h0, gain, w_bytes, w_scale, u_wo
         finish(1, 3, 2)
         h1_scale(0, 2)
         h1_scale(1, 2)
+        h1_scale(2, 0)
         h1_quant(first[0])
+        h1_scale(2, 1)
         h1_quant(first[1])
-        for b in (2, 3):
-            h1_scale(b, 0)
 
         def head(b, j, i):
             open_group(2, b, j, i)
             w_pass(2, b, j, 0, start=True)
             w_pass(2, b, j, 1)
 
-        for j in range(NJ):
-            head(0, j, j)
+        for j, i in enumerate((4, 5, 0)):
+            head(0, j, i)
         h1_turn(last[0], 6)
-        x_turn(2, 2, 7)
+        h1_turn(first[2], 7)
         h1_empty(last[0], "scalar")
-        x_empty(2, 2, "scalar")
-        h1_quant(last[0])
-        for b in (2, 3):
-            h1_scale(b, 1)
+        h1_empty(first[2], "scalar")
         h1_scale(2, 2)
+        h1_quant(last[0])
         h1_scale(3, 2)
-        x_quant(2, 2)
+        h1_scale(3, 0)
+        h1_scale(3, 1)
+        x_sort(2, 2, "vector")
+        x_sort(2, 3, "vector")
+        h1_quant(first[2])
         for j in range(NJ):
             u_pass(2, 0, j, 0)
             u_pass(2, 0, j, 1)
         for j in range(NJ):
             u_pass(2, 0, j, 2, stop=True)
             finish(2, 0, j)
-        h1_turn(first[2], 6)
-        h1_turn(last[1], 7)
-        h1_empty(first[2], "vector")
-        h1_empty(last[1], "vector")
-        h1_quant(first[2])
-        h1_quant(last[1])
 
         def group2(b, j, i, c0=0, c1=N):
             open_group(2, b, j, i)
@@ -438,16 +434,23 @@ def tile_two_step_rnn_fp4_s3_kernel(tc, x1, x2, h0, gain, w_bytes, w_scale, u_wo
                 u_pass(2, b, j, g, stop=g == NJ - 1, c0=c0, c1=c1)
             finish(2, b, j, c0, c1)
 
-        for j in range(NJ):
-            group2(1, j, 3 + j)
+        group2(1, 0, 1)
+        h1_turn(last[1], 2)
+        x_turn(2, 2, 3)
         h1_turn(first[3], 6)
         x_turn(2, 3, 7)
+        h1_empty(last[1], "vector")
+        x_empty(2, 2, "vector")
+        h1_quant(last[1])
+        x_quant(2, 2)
         h1_empty(first[3], "vector")
         x_empty(2, 3, "vector")
         h1_quant(first[3])
         x_quant(2, 3)
-        for j in range(NJ):
-            group2(2, j, j)
+        group2(1, 1, 4)
+        group2(1, 2, 5)
+        for j, i in enumerate((0, 1, 2)):
+            group2(2, j, i)
         group2(3, 0, 3)
         group2(3, 1, 4)
         group2(3, 2, 5, 0, 256)

@@ -219,7 +219,7 @@ def tile_two_step_rnn_fp4_s3_kernel(tc, x1, x2, h0, gain, w_bytes, w_scale, u_wo
         h_sb, scaled = {}, {}
 
         def finish(s, b, j, c0=0, c1=N):
-            h = work.tile([P, N], F32, tag="h", name="h", align_bytes=ALIGN, bufs=12)
+            h = work.tile([P, N], F32, tag="h", name="h", align_bytes=ALIGN, bufs=10)
             h_sb[s, b, j] = h
             nc.scalar.activation(out=h[:, 0 : c1 - c0], in_=acc[s, b, j][:, 0 : c1 - c0], func=TANH)
             out = out_0 if s == 1 else out_1
@@ -263,6 +263,11 @@ def tile_two_step_rnn_fp4_s3_kernel(tc, x1, x2, h0, gain, w_bytes, w_scale, u_wo
 
         gain_col = keep_tile([P, NJ, 4], BF16, "gain_col")
         nc.scalar.dma_start(out=gain_col[:], in_=gain.rearrange("(g p t) -> p g t", p=P, t=4))
+        zeros = keep_tile([P, N], BF16, "zeros")
+        nc.gpsimd.memset(zeros[:].bitcast(I32), 0)
+        table = keep_tile([P, 16], F32, "table")
+        nc.vector.memset(table[:], 0.0)
+        nc.scalar.activation(out=table[:, 0:1], in_=table[:, 8:9], func=TANH)
         ident = keep_tile([P, P], F32, "ident")
         make_identity(nc, ident[:])
         zero_u_scales(0, 1)
@@ -308,8 +313,16 @@ def tile_two_step_rnn_fp4_s3_kernel(tc, x1, x2, h0, gain, w_bytes, w_scale, u_wo
             h0_quant(b, A)
             h0_quant(b, Bk)
 
+
+        def warm_up(count):
+            bank = bank_tile(3)
+            for c in range(count):
+                nc.tensor.matmul(bank[:], lhsT=zeros[:, 0:P], rhs=zeros[:], start=True, stop=True)
+
+        warm_up(5)
         h0_turns(0, 6, 7)
         h0_turns(1, 4, 5)
+        warm_up(2)
         h0_ready(0)
         h0_ready(1)
         u_group(0, 0, 0)

@@ -101,26 +101,27 @@ def tile_two_step_rnn_fp4_s3_kernel(tc, x1, x2, h0, gain, w_bytes, w_scale, u_wo
             words = raw[:].bitcast(F32)
             return [words[:, 256 * g + u : 256 * g + 256 : 2] for u in range(2)]
 
-        def h0_turn(b, gs, i):
-            turn("h0_%d_%d" % (b, gs[0]), i, [every_second(h0_raw[b], g) for g in gs])
+        def h0_key(parts):
+            return "h0_%d_%d" % parts[0]
 
-        def h0_empty(b, gs):
-            key = "h0_%d_%d" % (b, gs[0])
+        def h0_turn(parts, i):
+            turn(h0_key(parts), i, [every_second(h0_raw[b], g) for b, g in parts])
+
+        def h0_empty(parts):
+            key = h0_key(parts)
             bank, n = turned[key]
+            g0, g1 = parts[0][1], parts[-1][1] + 1
             grouped[key] = keep_tile([P, N * n], BF16, "g_" + key)
             nc.vector.tensor_tensor(
-                out=grouped[key][:].rearrange("p (g r u e) -> p g r u e", g=n, u=2, e=2),
-                in0=bank[:, 0 : 2 * P * n].bitcast(BF16).rearrange("p (u g r e) -> p g r u e", u=2, g=n, e=2),
-                in1=gain_col[:, gs[0] : gs[0] + n, :]
-                .rearrange("p g (u e) -> p g u e", e=2)
-                .unsqueeze(2)
-                .to_broadcast([P, n, P, 2, 2]),
+                out=grouped[key][:].rearrange("p (c r u e) -> p c r u e", c=n, u=2, e=2),
+                in0=bank[:, 0 : 2 * P * n].bitcast(BF16).rearrange("p (u c r e) -> p c r u e", u=2, c=n, e=2),
+                in1=gain_col[:, g0:g1, :].rearrange("p g (u e) -> p g u e", e=2).unsqueeze(2).to_broadcast([P, n, P, 2, 2]),
                 op=MULT,
             )
 
-        def h0_quant(b, gs):
-            codes, scales = quantise("h0_%d_%d" % (b, gs[0]), N * len(gs))
-            for c, g in enumerate(gs):
+        def h0_quant(parts):
+            codes, scales = quantise(h0_key(parts), N * len(parts))
+            for c, (b, g) in enumerate(parts):
                 r_op[1, b, g] = (codes, scales, P * c)
 
         def empty(key, engine):
@@ -136,7 +137,7 @@ def tile_two_step_rnn_fp4_s3_kernel(tc, x1, x2, h0, gain, w_bytes, w_scale, u_wo
         x_sorted = {}
 
         def x_sort(s, b, engine):
-            x_sorted[s, b] = keep_tile([P, D], BF16, "xs%d_%d" % (s, b))
+            x_sorted[s, b] = work.tile([P, D], BF16, tag="sorted", name="sorted", align_bytes=ALIGN, bufs=4)
             dst = x_sorted[s, b][:].rearrange("p (u w e) -> p u w e", u=2, e=2)
             frm = x_raw[s, b][:].rearrange("p (w u e) -> p u w e", u=2, e=2)
             if engine == "scalar":
@@ -164,7 +165,7 @@ def tile_two_step_rnn_fp4_s3_kernel(tc, x1, x2, h0, gain, w_bytes, w_scale, u_wo
 
         def w_widen(j, g, ts, engine):
             if (j, g) not in wide:
-                wide[j, g] = work.tile([P, 4, N], BF16, tag="wide", name="wide", align_bytes=ALIGN, bufs=6)
+                wide[j, g] = work.tile([P, 4, N], BF16, tag="wide", name="wide", align_bytes=ALIGN, bufs=4)
             raw, c0 = w_raw[j, g]
             for t in ts:
                 src = raw[:, t, c0 : c0 + N].bitcast(E4M3)
@@ -175,13 +176,15 @@ def tile_two_step_rnn_fp4_s3_kernel(tc, x1, x2, h0, gain, w_bytes, w_scale, u_wo
                         out=wide[j, g][:, t, :], in0=src, scalar1=w_sc[:, g, t : t + 1], scalar2=None, op0=MULT
                     )
 
-        def w_weave(j, g):
+        def w_weave(j, g, engine="vector"):
             key = "w_%d_%d" % (j, g)
             grouped[key] = work.tile([P, 4 * N], BF16, tag="w_grp", name="w_grp", align_bytes=ALIGN)
-            nc.vector.tensor_copy(
-                out=grouped[key][:].rearrange("p (c i t) -> p c t i", i=4, t=4),
-                in_=wide[j, g][:].rearrange("p t (c i) -> p c t i", i=4),
-            )
+            dst = grouped[key][:].rearrange("p (c i t) -> p c t i", i=4, t=4)
+            frm = wide[j, g][:].rearrange("p t (c i) -> p c t i", i=4)
+            if engine == "scalar":
+                nc.scalar.copy(out=dst, in_=frm)
+            else:
+                nc.vector.tensor_copy(out=dst, in_=frm)
 
         def w_quant(j, g):
             w_op[j, g] = quantise("w_%d_%d" % (j, g), 4 * N)
@@ -263,6 +266,8 @@ def tile_two_step_rnn_fp4_s3_kernel(tc, x1, x2, h0, gain, w_bytes, w_scale, u_wo
 
         gain_col = keep_tile([P, NJ, 4], BF16, "gain_col")
         nc.scalar.dma_start(out=gain_col[:], in_=gain.rearrange("(g p t) -> p g t", p=P, t=4))
+        w_sc = keep_tile([P, NX, 4], F32, "w_sc")
+        nc.scalar.dma_start(out=w_sc[:], in_=w_scale.rearrange("(g p t) o -> p g (t o)", p=P, t=4))
         zeros = keep_tile([P, N], BF16, "zeros")
         nc.gpsimd.memset(zeros[:].bitcast(I32), 0)
         table = keep_tile([P, 16], F32, "table")
@@ -274,23 +279,19 @@ def tile_two_step_rnn_fp4_s3_kernel(tc, x1, x2, h0, gain, w_bytes, w_scale, u_wo
         zero_u_scales(1, 2)
         zero_u_scales(2, 3)
 
+        load_w(0, 0, 1)
         load_h0(0)
         load_h0(1)
         load_u(0)
         load_u_scales(0, 1)
-        w_sc = keep_tile([P, NX, 4], F32, "w_sc")
-        nc.sync.dma_start(out=w_sc[:], in_=w_scale.rearrange("(g p t) o -> p g (t o)", p=P, t=4))
-        load_w(0, 0, 1)
         load_h0(2)
         load_w(1, 0, 1)
         load_h0(3)
-        load_x(1, 0)
-        load_x(1, 1)
-        load_w(0, 1, 2)
-        load_x(1, 2)
-        load_x(1, 3)
+        for b in range(NB):
+            load_x(1, b)
         load_u(1)
         load_u_scales(1, 2)
+        load_w(0, 1, 2)
         load_w(1, 1, 2)
         load_w(0, 2, 3)
         load_w(1, 2, 3)
@@ -301,17 +302,18 @@ def tile_two_step_rnn_fp4_s3_kernel(tc, x1, x2, h0, gain, w_bytes, w_scale, u_wo
         gain_row = keep_tile([P, H], BF16, "gain_row")
         nc.sync.dma_start(out=gain_row[:], in_=gain.partition_broadcast(P))
 
-        A, Bk = (0, 1), (2,)
+        first = [[(b, 0), (b, 1)] for b in range(NB)]
+        last = [[(0, 2), (1, 2)], [(2, 2), (3, 2)]]
 
         def h0_turns(b, i0, i1):
-            h0_turn(b, A, i0)
-            h0_turn(b, Bk, i1)
+            h0_turn(first[b], i0)
+            h0_turn([(b, 2)], i1)
 
         def h0_ready(b):
-            h0_empty(b, A)
-            h0_empty(b, Bk)
-            h0_quant(b, A)
-            h0_quant(b, Bk)
+            h0_empty(first[b])
+            h0_empty([(b, 2)])
+            h0_quant(first[b])
+            h0_quant([(b, 2)])
 
 
         def warm_up(count):
@@ -319,28 +321,33 @@ def tile_two_step_rnn_fp4_s3_kernel(tc, x1, x2, h0, gain, w_bytes, w_scale, u_wo
             for c in range(count):
                 nc.tensor.matmul(bank[:], lhsT=zeros[:, 0:P], rhs=zeros[:], start=True, stop=True)
 
-        warm_up(5)
+        warm_up(6)
+        w_widen(0, 0, range(4), "vector")
+        w_weave(0, 0, "scalar")
         h0_turns(0, 6, 7)
         h0_turns(1, 4, 5)
         warm_up(2)
         h0_ready(0)
         h0_ready(1)
         u_group(0, 0, 0)
-        w_widen(0, 0, (0, 1), "scalar")
-        w_widen(0, 0, (2, 3), "vector")
+        w_quant(0, 0)
         h0_turns(2, 6, 7)
         h0_ready(2)
         u_group(1, 0, 1)
         w_widen(0, 1, range(4), "scalar")
-        w_weave(0, 0)
         h0_turns(3, 4, 5)
-        h0_ready(3)
+        x_sort(1, 0, "scalar")
+        h0_empty(first[3])
+        x_sort(1, 1, "vector")
+        x_sort(1, 2, "scalar")
+        h0_empty([(3, 2)])
+        h0_quant(first[3])
+        h0_quant([(3, 2)])
+        x_sort(1, 3, "vector")
         u_group(2, 0, 2)
-        w_widen(1, 0, (0,), "scalar")
         for b, i in enumerate((6, 7, 4, 5)):
             x_turn(1, b, i)
             x_empty(1, b, "scalar")
-        w_quant(0, 0)
         w_weave(0, 1)
         x_quant(1, 0)
         w_quant(0, 1)
@@ -349,7 +356,7 @@ def tile_two_step_rnn_fp4_s3_kernel(tc, x1, x2, h0, gain, w_bytes, w_scale, u_wo
         u_group(3, 0, 3)
         u_group(0, 1, 6)
         u_group(1, 1, 7)
-        w_widen(1, 0, (1,), "scalar")
+        w_widen(1, 0, (0, 1), "scalar")
         w_widen(1, 0, (2, 3), "vector")
         w_widen(1, 1, (0, 1, 2), "scalar")
         w_weave(1, 0)
@@ -360,19 +367,20 @@ def tile_two_step_rnn_fp4_s3_kernel(tc, x1, x2, h0, gain, w_bytes, w_scale, u_wo
             w_close(b, 0)
         u_group(2, 1, 4)
         u_group(3, 1, 5)
-        w_widen(2, 0, (0, 1, 2), "scalar")
-        w_widen(2, 0, (3,), "vector")
-        w_quant(1, 1)
         finish(1, 0, 0)
         finish(1, 1, 0)
+        w_widen(2, 0, (0, 1), "scalar")
+        w_widen(2, 0, (2, 3), "vector")
+        w_quant(1, 1)
         u_group(0, 2, 0)
         u_group(1, 2, 1)
-        w_widen(2, 1, range(4), "scalar")
+        w_widen(2, 1, (0, 1), "scalar")
+        finish(1, 2, 0)
+        finish(1, 3, 0)
+        w_widen(2, 1, (2, 3), "scalar")
         w_weave(2, 0)
         for b in range(NB):
             w_close(b, 1)
-        finish(1, 2, 0)
-        finish(1, 3, 0)
         x_sort(2, 0, "vector")
         w_quant(2, 0)
         x_sort(2, 1, "vector")
@@ -381,20 +389,18 @@ def tile_two_step_rnn_fp4_s3_kernel(tc, x1, x2, h0, gain, w_bytes, w_scale, u_wo
         finish(1, 1, 1)
         h1_scale(0, 0)
         w_quant(2, 1)
-        x_turn(2, 0, 6)
-        x_turn(2, 1, 7)
         u_group(2, 2, 2)
         u_group(3, 2, 3)
-        x_empty(2, 0, "scalar")
-        x_empty(2, 1, "scalar")
+        x_turn(2, 0, 6)
+        x_turn(2, 1, 7)
         finish(1, 2, 1)
         finish(1, 3, 1)
-        first = [[(b, 0), (b, 1)] for b in range(NB)]
-        last = [[(0, 2), (1, 2)], [(2, 2), (3, 2)]]
+        x_empty(2, 0, "scalar")
+        x_empty(2, 1, "scalar")
         h1_scale(0, 1)
-        x_quant(2, 0)
         h1_scale(1, 0)
         h1_scale(1, 1)
+        x_quant(2, 0)
         x_quant(2, 1)
         for b in range(NB):
             w_close(b, 2)
@@ -467,4 +473,5 @@ def tile_two_step_rnn_fp4_s3_kernel(tc, x1, x2, h0, gain, w_bytes, w_scale, u_wo
         group2(3, 0, 3)
         group2(3, 1, 4)
         group2(3, 2, 5, 0, 256)
-        group2(3, 2, 0, 256, 512)
+        group2(3, 2, 0, 256, 384)
+        group2(3, 2, 1, 384, 512)

@@ -138,8 +138,8 @@ def tile_two_step_rnn_fp4_s3_kernel(tc, x1, x2, h0, gain, w_bytes, w_scale, u_wo
 
         def x_sort(s, b, engine):
             x_sorted[s, b] = work.tile([P, D], BF16, tag="sorted", name="sorted", align_bytes=ALIGN, bufs=4)
-            dst = x_sorted[s, b][:].rearrange("p (u w e) -> p u w e", u=2, e=2)
-            frm = x_raw[s, b][:].rearrange("p (w u e) -> p u w e", u=2, e=2)
+            dst = x_sorted[s, b][:].bitcast(F32).rearrange("p (u w) -> p u w", u=2)
+            frm = x_raw[s, b][:].bitcast(F32).rearrange("p (w u) -> p u w", u=2)
             if engine == "scalar":
                 nc.scalar.copy(out=dst, in_=frm)
             else:
@@ -282,9 +282,9 @@ def tile_two_step_rnn_fp4_s3_kernel(tc, x1, x2, h0, gain, w_bytes, w_scale, u_wo
         load_w(0, 0, 1)
         load_h0(0)
         load_h0(1)
+        load_h0(2)
         load_u(0)
         load_u_scales(0, 1)
-        load_h0(2)
         load_w(1, 0, 1)
         load_h0(3)
         for b in range(NB):
@@ -317,7 +317,7 @@ def tile_two_step_rnn_fp4_s3_kernel(tc, x1, x2, h0, gain, w_bytes, w_scale, u_wo
 
 
         def warm_up(count):
-            bank = bank_tile(3)
+            bank = bank_tile(1)
             for c in range(count):
                 nc.tensor.matmul(bank[:], lhsT=zeros[:, 0:P], rhs=zeros[:], start=True, stop=True)
 
@@ -326,35 +326,33 @@ def tile_two_step_rnn_fp4_s3_kernel(tc, x1, x2, h0, gain, w_bytes, w_scale, u_wo
         w_weave(0, 0, "scalar")
         h0_turns(0, 6, 7)
         h0_turns(1, 4, 5)
-        warm_up(2)
+        warm_up(1)
+        h0_turns(2, 2, 3)
+        warm_up(1)
         h0_ready(0)
         h0_ready(1)
-        u_group(0, 0, 0)
-        w_quant(0, 0)
-        h0_turns(2, 6, 7)
         h0_ready(2)
-        u_group(1, 0, 1)
-        w_widen(0, 1, range(4), "scalar")
+        for b in range(3):
+            u_group(b, 0, b)
+        w_widen(0, 1, (0, 1, 2), "scalar")
+        w_widen(0, 1, (3,), "vector")
+        w_quant(0, 0)
+        w_weave(0, 1)
+        for b in range(3):
+            x_sort(1, b, "scalar")
         h0_turns(3, 4, 5)
-        x_sort(1, 0, "scalar")
         h0_empty(first[3])
-        x_sort(1, 1, "vector")
-        x_sort(1, 2, "scalar")
         h0_empty([(3, 2)])
         h0_quant(first[3])
         h0_quant([(3, 2)])
-        x_sort(1, 3, "vector")
-        u_group(2, 0, 2)
-        for b, i in enumerate((6, 7, 4, 5)):
+        for b, i in enumerate((6, 7, 3, 4)):
             x_turn(1, b, i)
             x_empty(1, b, "scalar")
-        w_weave(0, 1)
-        x_quant(1, 0)
         w_quant(0, 1)
-        for b in (1, 2, 3):
+        for b in range(NB):
             x_quant(1, b)
-        u_group(3, 0, 3)
         u_group(0, 1, 6)
+        u_group(3, 0, 5)
         u_group(1, 1, 7)
         w_widen(1, 0, (0, 1), "scalar")
         w_widen(1, 0, (2, 3), "vector")
@@ -365,8 +363,8 @@ def tile_two_step_rnn_fp4_s3_kernel(tc, x1, x2, h0, gain, w_bytes, w_scale, u_wo
         w_weave(1, 1)
         for b in range(NB):
             w_close(b, 0)
-        u_group(2, 1, 4)
-        u_group(3, 1, 5)
+        u_group(2, 1, 3)
+        u_group(3, 1, 4)
         finish(1, 0, 0)
         finish(1, 1, 0)
         w_widen(2, 0, (0, 1), "scalar")
@@ -374,11 +372,12 @@ def tile_two_step_rnn_fp4_s3_kernel(tc, x1, x2, h0, gain, w_bytes, w_scale, u_wo
         w_quant(1, 1)
         u_group(0, 2, 0)
         u_group(1, 2, 1)
-        w_widen(2, 1, (0, 1), "scalar")
         finish(1, 2, 0)
         finish(1, 3, 0)
-        w_widen(2, 1, (2, 3), "scalar")
+        w_widen(2, 1, range(4), "scalar")
         w_weave(2, 0)
+        u_group(2, 2, 2)
+        u_group(3, 2, 5)
         for b in range(NB):
             w_close(b, 1)
         x_sort(2, 0, "vector")
@@ -389,8 +388,6 @@ def tile_two_step_rnn_fp4_s3_kernel(tc, x1, x2, h0, gain, w_bytes, w_scale, u_wo
         finish(1, 1, 1)
         h1_scale(0, 0)
         w_quant(2, 1)
-        u_group(2, 2, 2)
-        u_group(3, 2, 3)
         x_turn(2, 0, 6)
         x_turn(2, 1, 7)
         finish(1, 2, 1)
@@ -424,7 +421,7 @@ def tile_two_step_rnn_fp4_s3_kernel(tc, x1, x2, h0, gain, w_bytes, w_scale, u_wo
             w_pass(2, b, j, 0, start=True)
             w_pass(2, b, j, 1)
 
-        for j, i in enumerate((4, 5, 0)):
+        for j, i in enumerate((3, 4, 0)):
             head(0, j, i)
         h1_turn(last[0], 6)
         h1_turn(first[2], 7)
@@ -455,7 +452,7 @@ def tile_two_step_rnn_fp4_s3_kernel(tc, x1, x2, h0, gain, w_bytes, w_scale, u_wo
 
         group2(1, 0, 1)
         h1_turn(last[1], 2)
-        x_turn(2, 2, 3)
+        x_turn(2, 2, 5)
         h1_turn(first[3], 6)
         x_turn(2, 3, 7)
         h1_empty(last[1], "vector")
@@ -466,12 +463,12 @@ def tile_two_step_rnn_fp4_s3_kernel(tc, x1, x2, h0, gain, w_bytes, w_scale, u_wo
         x_empty(2, 3, "vector")
         h1_quant(first[3])
         x_quant(2, 3)
-        group2(1, 1, 4)
-        group2(1, 2, 5)
+        group2(1, 1, 3)
+        group2(1, 2, 4)
         for j, i in enumerate((0, 1, 2)):
             group2(2, j, i)
-        group2(3, 0, 3)
-        group2(3, 1, 4)
-        group2(3, 2, 5, 0, 256)
+        group2(3, 0, 5)
+        group2(3, 1, 3)
+        group2(3, 2, 4, 0, 256)
         group2(3, 2, 0, 256, 384)
         group2(3, 2, 1, 384, 512)

@@ -341,18 +341,18 @@ def tile_two_step_rnn_fp4_s3_kernel(tc, x1, x2, h0, gain, w_bytes, w_scale, u_wo
         for b in range(3):
             x_sort(1, b, "scalar")
         h0_turns(3, 4, 5)
-        h0_empty(first[3])
         h0_empty([(3, 2)])
-        h0_quant(first[3])
+        h0_empty(first[3])
         h0_quant([(3, 2)])
-        for b, i in enumerate((6, 7, 3, 4)):
+        h0_quant(first[3])
+        for b, i in enumerate((6, 7, 3, 5)):
             x_turn(1, b, i)
             x_empty(1, b, "scalar")
         w_quant(0, 1)
         for b in range(NB):
             x_quant(1, b)
         u_group(0, 1, 6)
-        u_group(3, 0, 5)
+        u_group(3, 0, 4)
         u_group(1, 1, 7)
         w_widen(1, 0, (0, 1), "scalar")
         w_widen(1, 0, (2, 3), "vector")
@@ -364,7 +364,7 @@ def tile_two_step_rnn_fp4_s3_kernel(tc, x1, x2, h0, gain, w_bytes, w_scale, u_wo
         for b in range(NB):
             w_close(b, 0)
         u_group(2, 1, 3)
-        u_group(3, 1, 4)
+        u_group(3, 1, 5)
         finish(1, 0, 0)
         finish(1, 1, 0)
         w_widen(2, 0, (0, 1), "scalar")
@@ -374,20 +374,23 @@ def tile_two_step_rnn_fp4_s3_kernel(tc, x1, x2, h0, gain, w_bytes, w_scale, u_wo
         u_group(1, 2, 1)
         finish(1, 2, 0)
         finish(1, 3, 0)
-        w_widen(2, 1, range(4), "scalar")
+        w_widen(2, 1, (0, 1, 2), "scalar")
+        x_sort(2, 0, "scalar")
+        x_sort(2, 1, "scalar")
         w_weave(2, 0)
         u_group(2, 2, 2)
-        u_group(3, 2, 5)
+        u_group(3, 2, 4)
         for b in range(NB):
             w_close(b, 1)
-        x_sort(2, 0, "vector")
+        w_widen(2, 1, (3,), "vector")
         w_quant(2, 0)
-        x_sort(2, 1, "vector")
         w_weave(2, 1)
         finish(1, 0, 1)
         finish(1, 1, 1)
         h1_scale(0, 0)
         w_quant(2, 1)
+        for b in range(NB):
+            w_pass(1, b, 2, 0)
         x_turn(2, 0, 6)
         x_turn(2, 1, 7)
         finish(1, 2, 1)
@@ -399,8 +402,9 @@ def tile_two_step_rnn_fp4_s3_kernel(tc, x1, x2, h0, gain, w_bytes, w_scale, u_wo
         h1_scale(1, 1)
         x_quant(2, 0)
         x_quant(2, 1)
+        x_sort(2, 2, "vector")
         for b in range(NB):
-            w_close(b, 2)
+            w_pass(1, b, 2, 1, stop=True)
         h1_turn(first[0], 6)
         h1_turn(first[1], 7)
         finish(1, 0, 2)
@@ -411,9 +415,8 @@ def tile_two_step_rnn_fp4_s3_kernel(tc, x1, x2, h0, gain, w_bytes, w_scale, u_wo
         finish(1, 3, 2)
         h1_scale(0, 2)
         h1_scale(1, 2)
-        h1_scale(2, 0)
         h1_quant(first[0])
-        h1_scale(2, 1)
+        h1_scale(2, 0)
         h1_quant(first[1])
 
         def head(b, j, i):
@@ -421,26 +424,28 @@ def tile_two_step_rnn_fp4_s3_kernel(tc, x1, x2, h0, gain, w_bytes, w_scale, u_wo
             w_pass(2, b, j, 0, start=True)
             w_pass(2, b, j, 1)
 
-        for j, i in enumerate((3, 4, 0)):
+        for j, i in enumerate((3, 5, 0)):
             head(0, j, i)
         h1_turn(last[0], 6)
-        h1_turn(first[2], 7)
+        x_turn(2, 2, 7)
         h1_empty(last[0], "scalar")
-        h1_empty(first[2], "scalar")
+        x_empty(2, 2, "scalar")
+        h1_scale(2, 1)
         h1_scale(2, 2)
         h1_quant(last[0])
         h1_scale(3, 2)
         h1_scale(3, 0)
         h1_scale(3, 1)
-        x_sort(2, 2, "vector")
         x_sort(2, 3, "vector")
-        h1_quant(first[2])
-        for j in range(NJ):
-            u_pass(2, 0, j, 0)
-            u_pass(2, 0, j, 1)
-        for j in range(NJ):
-            u_pass(2, 0, j, 2, stop=True)
-            finish(2, 0, j)
+        x_quant(2, 2)
+        head(1, 0, 1)
+        early = [(0, 0), (0, 1), (0, 2), (1, 0)]
+        for b, j in early:
+            u_pass(2, b, j, 0)
+            u_pass(2, b, j, 1)
+        for b, j in early:
+            u_pass(2, b, j, 2, stop=True)
+            finish(2, b, j)
 
         def group2(b, j, i, c0=0, c1=N):
             open_group(2, b, j, i)
@@ -450,25 +455,31 @@ def tile_two_step_rnn_fp4_s3_kernel(tc, x1, x2, h0, gain, w_bytes, w_scale, u_wo
                 u_pass(2, b, j, g, stop=g == NJ - 1, c0=c0, c1=c1)
             finish(2, b, j, c0, c1)
 
-        group2(1, 0, 1)
-        h1_turn(last[1], 2)
-        x_turn(2, 2, 5)
+        h1_turn(first[2], 2)
+        h1_turn(last[1], 4)
         h1_turn(first[3], 6)
         x_turn(2, 3, 7)
+        h1_empty(first[2], "vector")
         h1_empty(last[1], "vector")
-        x_empty(2, 2, "vector")
+        h1_quant(first[2])
         h1_quant(last[1])
-        x_quant(2, 2)
         h1_empty(first[3], "vector")
         x_empty(2, 3, "vector")
         h1_quant(first[3])
         x_quant(2, 3)
-        group2(1, 1, 3)
-        group2(1, 2, 4)
-        for j, i in enumerate((0, 1, 2)):
-            group2(2, j, i)
-        group2(3, 0, 5)
-        group2(3, 1, 3)
-        group2(3, 2, 4, 0, 256)
-        group2(3, 2, 0, 256, 384)
-        group2(3, 2, 1, 384, 512)
+
+        def groups2(b, js, banks):
+            for j, i in zip(js, banks):
+                head(b, j, i)
+            for j in js:
+                for g in range(NJ):
+                    u_pass(2, b, j, g, stop=g == NJ - 1)
+                finish(2, b, j)
+
+        groups2(1, (1, 2), (3, 5))
+        groups2(2, (0, 1, 2), (0, 1, 2))
+        group2(3, 0, 4)
+        group2(3, 1, 6)
+        group2(3, 2, 7, 0, 256)
+        group2(3, 2, 3, 256, 384)
+        group2(3, 2, 5, 384, 512)

@@ -59,10 +59,10 @@ def tile_two_step_rnn_fp4_s3_kernel(tc, x1, x2, h0, gain, w_bytes, w_scale, u_wo
             for j in range(j0, j1):
                 u_planes[j] = (t, N * (j - j0))
 
-        def load_u_scales(j0, j1):
+        def load_u_scales(j0, j1, queue=nc.sync):
             t = u_planes[j0][0]
             for r in range(4):
-                nc.sync.dma_start(
+                queue.dma_start(
                     out=t[r:P:32, :, :].bitcast(I32),
                     in_=u_scales[:, r:16:4, N * j0 : N * j1].rearrange("g q n -> q g n").bitcast(I32),
                 )
@@ -76,9 +76,14 @@ def tile_two_step_rnn_fp4_s3_kernel(tc, x1, x2, h0, gain, w_bytes, w_scale, u_wo
             for j in range(j0, j1):
                 w_raw[j, g] = (t, N * (j - j0))
 
-        def load_x(s, b):
-            x_raw[s, b] = keep_tile([P, D], BF16, "x%d_%d" % (s, b))
-            nc.sync.dma_start(out=x_raw[s, b][:], in_=(x1 if s == 1 else x2)[P * b : P * b + P, :])
+        def load_x(s, b0, b1):
+            t = keep_tile([P, (b1 - b0) * D], BF16, "x%d_%d" % (s, b0))
+            nc.sync.dma_start(
+                out=t[:].rearrange("p (b k) -> p b k", k=D),
+                in_=(x1 if s == 1 else x2)[P * b0 : P * b1, :].rearrange("(b p) k -> p b k", p=P),
+            )
+            for b in range(b0, b1):
+                x_raw[s, b] = t[:, D * (b - b0) : D * (b - b0) + D]
 
         r_op, x_op, w_op = {}, {}, {}
         turned, grouped = {}, {}
@@ -98,14 +103,14 @@ def tile_two_step_rnn_fp4_s3_kernel(tc, x1, x2, h0, gain, w_bytes, w_scale, u_wo
             turned[key] = (bank, n)
 
         def every_second(raw, g):
-            words = raw[:].bitcast(F32)
+            words = raw.bitcast(F32)
             return [words[:, 256 * g + u : 256 * g + 256 : 2] for u in range(2)]
 
         def h0_key(parts):
             return "h0_%d_%d" % parts[0]
 
         def h0_turn(parts, i):
-            turn(h0_key(parts), i, [every_second(h0_raw[b], g) for b, g in parts])
+            turn(h0_key(parts), i, [every_second(h0_raw[b][:], g) for b, g in parts])
 
         def h0_empty(parts):
             key = h0_key(parts)
@@ -139,7 +144,7 @@ def tile_two_step_rnn_fp4_s3_kernel(tc, x1, x2, h0, gain, w_bytes, w_scale, u_wo
         def x_sort(s, b, engine):
             x_sorted[s, b] = work.tile([P, D], BF16, tag="sorted", name="sorted", align_bytes=ALIGN, bufs=4)
             dst = x_sorted[s, b][:].bitcast(F32).rearrange("p (u w) -> p u w", u=2)
-            frm = x_raw[s, b][:].bitcast(F32).rearrange("p (w u) -> p u w", u=2)
+            frm = x_raw[s, b].bitcast(F32).rearrange("p (w u) -> p u w", u=2)
             if engine == "scalar":
                 nc.scalar.copy(out=dst, in_=frm)
             else:
@@ -278,7 +283,6 @@ def tile_two_step_rnn_fp4_s3_kernel(tc, x1, x2, h0, gain, w_bytes, w_scale, u_wo
         zero_u_scales(0, 1)
         zero_u_scales(1, 2)
         zero_u_scales(2, 3)
-
         load_w(0, 0, 1)
         load_h0(0)
         load_h0(1)
@@ -287,8 +291,10 @@ def tile_two_step_rnn_fp4_s3_kernel(tc, x1, x2, h0, gain, w_bytes, w_scale, u_wo
         load_u_scales(0, 1)
         load_w(1, 0, 1)
         load_h0(3)
-        for b in range(NB):
-            load_x(1, b)
+        load_x(1, 0, 1)
+        load_x(1, 1, 2)
+        load_x(1, 2, 3)
+        load_x(1, 3, 4)
         load_u(1)
         load_u_scales(1, 2)
         load_w(0, 1, 2)
@@ -297,8 +303,10 @@ def tile_two_step_rnn_fp4_s3_kernel(tc, x1, x2, h0, gain, w_bytes, w_scale, u_wo
         load_w(1, 2, 3)
         load_u(2)
         load_u_scales(2, 3)
-        for b in range(NB):
-            load_x(2, b)
+        load_x(2, 0, 1)
+        load_x(2, 1, 2)
+        load_x(2, 2, 3)
+        load_x(2, 3, 4)
         gain_row = keep_tile([P, H], BF16, "gain_row")
         nc.sync.dma_start(out=gain_row[:], in_=gain.partition_broadcast(P))
 
@@ -332,27 +340,35 @@ def tile_two_step_rnn_fp4_s3_kernel(tc, x1, x2, h0, gain, w_bytes, w_scale, u_wo
         h0_ready(0)
         h0_ready(1)
         h0_ready(2)
-        for b in range(3):
-            u_group(b, 0, b)
+        u_group(0, 0, 0)
+        u_group(1, 0, 1)
+        h0_turns(3, 4, 5)
+        u_group(2, 0, 2)
         w_widen(0, 1, (0, 1, 2), "scalar")
         w_widen(0, 1, (3,), "vector")
-        w_quant(0, 0)
-        w_weave(0, 1)
-        for b in range(3):
-            x_sort(1, b, "scalar")
-        h0_turns(3, 4, 5)
+        x_sort(1, 0, "scalar")
+        x_sort(1, 1, "scalar")
         h0_empty([(3, 2)])
         h0_empty(first[3])
         h0_quant([(3, 2)])
         h0_quant(first[3])
-        for b, i in enumerate((6, 7, 3, 5)):
-            x_turn(1, b, i)
-            x_empty(1, b, "scalar")
+        w_quant(0, 0)
+        w_weave(0, 1)
+        x_turn(1, 0, 6)
+        x_turn(1, 1, 7)
+        x_turn(1, 2, 3)
+        x_turn(1, 3, 5)
+        x_empty(1, 0, "scalar")
+        x_empty(1, 1, "scalar")
+        x_empty(1, 2, "scalar")
+        x_empty(1, 3, "scalar")
+        x_quant(1, 0)
         w_quant(0, 1)
-        for b in range(NB):
-            x_quant(1, b)
-        u_group(0, 1, 6)
+        x_quant(1, 1)
+        x_quant(1, 2)
+        x_quant(1, 3)
         u_group(3, 0, 4)
+        u_group(0, 1, 6)
         u_group(1, 1, 7)
         w_widen(1, 0, (0, 1), "scalar")
         w_widen(1, 0, (2, 3), "vector")
@@ -389,10 +405,10 @@ def tile_two_step_rnn_fp4_s3_kernel(tc, x1, x2, h0, gain, w_bytes, w_scale, u_wo
         finish(1, 1, 1)
         h1_scale(0, 0)
         w_quant(2, 1)
-        for b in range(NB):
-            w_pass(1, b, 2, 0)
         x_turn(2, 0, 6)
         x_turn(2, 1, 7)
+        for b in range(NB):
+            w_pass(1, b, 2, 0)
         finish(1, 2, 1)
         finish(1, 3, 1)
         x_empty(2, 0, "scalar")
@@ -402,7 +418,6 @@ def tile_two_step_rnn_fp4_s3_kernel(tc, x1, x2, h0, gain, w_bytes, w_scale, u_wo
         h1_scale(1, 1)
         x_quant(2, 0)
         x_quant(2, 1)
-        x_sort(2, 2, "vector")
         for b in range(NB):
             w_pass(1, b, 2, 1, stop=True)
         h1_turn(first[0], 6)
@@ -436,7 +451,7 @@ def tile_two_step_rnn_fp4_s3_kernel(tc, x1, x2, h0, gain, w_bytes, w_scale, u_wo
         h1_scale(3, 2)
         h1_scale(3, 0)
         h1_scale(3, 1)
-        x_sort(2, 3, "vector")
+        x_sort(2, 3, "scalar")
         x_quant(2, 2)
         head(1, 0, 1)
         early = [(0, 0), (0, 1), (0, 2), (1, 0)]

@@ -124,6 +124,23 @@ def tile_two_step_rnn_fp4_s3_kernel(tc, x1, x2, h0, gain, w_bytes, w_scale, u_wo
                 op=MULT,
             )
 
+        def spread_gain(g, i, engine):
+            rows = bank_tile(i)
+            for t in range(4):
+                nc.tensor.matmul(
+                    rows[:, P * t : P * t + P],
+                    lhsT=gain_col[:, g, t : t + 1].to_broadcast([P, P]),
+                    rhs=ident_bf[:],
+                    start=True,
+                    stop=True,
+                )
+            dst = gain_row[:, g, :].rearrange("p (u w e) -> p u w e", u=2, e=2)
+            frm = rows[:].rearrange("p (u e w) -> p u w e", u=2, e=2)
+            if engine == "scalar":
+                nc.scalar.copy(out=dst, in_=frm)
+            else:
+                nc.vector.tensor_copy(out=dst, in_=frm)
+
         def h0_quant(parts):
             codes, scales = quantise(h0_key(parts), N * len(parts))
             for c, (b, g) in enumerate(parts):
@@ -238,7 +255,7 @@ def tile_two_step_rnn_fp4_s3_kernel(tc, x1, x2, h0, gain, w_bytes, w_scale, u_wo
             nc.vector.tensor_tensor(
                 out=scaled[b, j][:].rearrange("p (u w e) -> p u w e", u=2, e=2),
                 in0=h_sb[1, b, j][:].rearrange("p (w u e) -> p u w e", u=2, e=2),
-                in1=gain_row[:, N * j : N * j + N].rearrange("p (w u e) -> p u w e", u=2, e=2),
+                in1=gain_row[:, j, :].rearrange("p (u w e) -> p u w e", u=2, e=2),
                 op=MULT,
             )
 
@@ -274,7 +291,7 @@ def tile_two_step_rnn_fp4_s3_kernel(tc, x1, x2, h0, gain, w_bytes, w_scale, u_wo
         w_sc = keep_tile([P, NX, 4], F32, "w_sc")
         nc.scalar.dma_start(out=w_sc[:], in_=w_scale.rearrange("(g p t) o -> p g (t o)", p=P, t=4))
         zeros = keep_tile([P, N], BF16, "zeros")
-        nc.gpsimd.memset(zeros[:].bitcast(I32), 0)
+        nc.vector.memset(zeros[:].bitcast(I32), 0)
         table = keep_tile([P, 16], F32, "table")
         nc.vector.memset(table[:], 0.0)
         nc.scalar.activation(out=table[:, 0:1], in_=table[:, 8:9], func=TANH)
@@ -283,6 +300,8 @@ def tile_two_step_rnn_fp4_s3_kernel(tc, x1, x2, h0, gain, w_bytes, w_scale, u_wo
         zero_u_scales(0, 1)
         zero_u_scales(1, 2)
         zero_u_scales(2, 3)
+        ident_bf = keep_tile([P, P], BF16, "ident_bf")
+        nc.vector.tensor_copy(out=ident_bf[:], in_=ident[:])
         load_w(0, 0, 1)
         load_h0(0)
         load_h0(1)
@@ -307,8 +326,7 @@ def tile_two_step_rnn_fp4_s3_kernel(tc, x1, x2, h0, gain, w_bytes, w_scale, u_wo
         load_x(2, 1, 2)
         load_x(2, 2, 3)
         load_x(2, 3, 4)
-        gain_row = keep_tile([P, H], BF16, "gain_row")
-        nc.sync.dma_start(out=gain_row[:], in_=gain.partition_broadcast(P))
+        gain_row = keep_tile([P, NJ, N], BF16, "gain_row")
 
         first = [[(b, 0), (b, 1)] for b in range(NB)]
         last = [[(0, 2), (1, 2)], [(2, 2), (3, 2)]]
@@ -329,7 +347,10 @@ def tile_two_step_rnn_fp4_s3_kernel(tc, x1, x2, h0, gain, w_bytes, w_scale, u_wo
             for c in range(count):
                 nc.tensor.matmul(bank[:], lhsT=zeros[:, 0:P], rhs=zeros[:], start=True, stop=True)
 
-        warm_up(6)
+        warm_up(2)
+        spread_gain(0, 0, "scalar")
+        spread_gain(1, 2, "scalar")
+        spread_gain(2, 3, "scalar")
         w_widen(0, 0, range(4), "vector")
         w_weave(0, 0, "scalar")
         h0_turns(0, 6, 7)

@@ -40,6 +40,12 @@ def tile_two_step_rnn_fp4_s3_kernel(tc, x1, x2, h0, gain, w_bytes, w_scale, u_wo
         def bank_tile(i):
             return psum.tile([P, N], F32, tag="bank%d" % i, name="bank%d" % i)
 
+        def copy(engine, dst, frm):
+            if engine == "scalar":
+                nc.scalar.copy(out=dst, in_=frm)
+            else:
+                nc.vector.tensor_copy(out=dst, in_=frm)
+
         h0_raw, u_sb, u_planes, w_raw, x_raw = {}, {}, {}, {}, {}
 
         def load_h0(b):
@@ -183,6 +189,34 @@ def tile_two_step_rnn_fp4_s3_kernel(tc, x1, x2, h0, gain, w_bytes, w_scale, u_wo
             for g in range(NX):
                 x_op[s, b, g] = (codes, scales, P * g)
 
+        x2_quads = [keep_tile([P, NX, 8, P], BF16, "x2_quads_%d" % half) for half in range(2)]
+        x2_blocks = {}
+
+        def load_x2_half(half):
+            rows = x2[256 * half : 256 * half + 256, :].rearrange("(r i) k -> i r k", i=32)
+            for g in range(NX):
+                for a in (0, 2, 1, 3):
+                    nc.sync.dma_start(
+                        out=x2_quads[half][32 * a : 32 * a + 32, g, :, :],
+                        in_=rows[:, :, N * g + P * a : N * g + P * a + P],
+                    )
+
+        def x2_sort(b, engine):
+            x_sorted[2, b] = work.tile([P, D], BF16, tag="sorted", name="sorted", align_bytes=ALIGN, bufs=4)
+            dst = x_sorted[2, b][:].bitcast(F32).rearrange("p (g u w) -> p g u w", g=NX, u=2)
+            frm = x2_quads[b // 2][:, :, 4 * (b % 2) : 4 * (b % 2) + 4, :].rearrange("p g r k -> p g (r k)").bitcast(F32)
+            copy(engine, dst, frm.rearrange("p g (w u) -> p g u w", u=2))
+
+        def x2_turn(b):
+            x2_blocks[b] = work.tile([P, D // 2], F32, tag="blocks", name="blocks", align_bytes=ALIGN, bufs=2)
+            nc.vector.transpose(x2_blocks[b][:], x_sorted[2, b][:].bitcast(F32))
+
+        def x2_pair(b, engine):
+            key = "x2_%d" % b
+            grouped[key] = keep_tile([P, D], BF16, "g_" + key)
+            dst = grouped[key][:].bitcast(F32).rearrange("p (g r u) -> p g r u", g=NX, u=2)
+            copy(engine, dst, x2_blocks[b][:].rearrange("p (g u r) -> p g r u", g=NX, u=2))
+
         wide = {}
 
         def w_widen(j, g, ts, engine):
@@ -322,10 +356,8 @@ def tile_two_step_rnn_fp4_s3_kernel(tc, x1, x2, h0, gain, w_bytes, w_scale, u_wo
         load_w(1, 2, 3)
         load_u(2)
         load_u_scales(2, 3)
-        load_x(2, 0, 1)
-        load_x(2, 1, 2)
-        load_x(2, 2, 3)
-        load_x(2, 3, 4)
+        load_x2_half(0)
+        load_x2_half(1)
         gain_row = keep_tile([P, NJ, N], BF16, "gain_row")
 
         first = [[(b, 0), (b, 1)] for b in range(NB)]
@@ -412,8 +444,8 @@ def tile_two_step_rnn_fp4_s3_kernel(tc, x1, x2, h0, gain, w_bytes, w_scale, u_wo
         finish(1, 2, 0)
         finish(1, 3, 0)
         w_widen(2, 1, (0, 1, 2), "scalar")
-        x_sort(2, 0, "scalar")
-        x_sort(2, 1, "scalar")
+        x2_sort(0, "scalar")
+        x2_sort(1, "scalar")
         w_weave(2, 0)
         u_group(2, 2, 2)
         u_group(3, 2, 4)
@@ -422,64 +454,36 @@ def tile_two_step_rnn_fp4_s3_kernel(tc, x1, x2, h0, gain, w_bytes, w_scale, u_wo
         w_widen(2, 1, (3,), "vector")
         w_quant(2, 0)
         w_weave(2, 1)
+        x2_turn(0)
+        w_quant(2, 1)
+        x2_turn(1)
         finish(1, 0, 1)
         finish(1, 1, 1)
-        h1_scale(0, 0)
-        w_quant(2, 1)
-        x_turn(2, 0, 6)
-        x_turn(2, 1, 7)
+        x2_pair(0, "scalar")
         for b in range(NB):
             w_pass(1, b, 2, 0)
         finish(1, 2, 1)
         finish(1, 3, 1)
-        x_empty(2, 0, "scalar")
-        x_empty(2, 1, "scalar")
+        x2_pair(1, "scalar")
+        h1_scale(0, 0)
+        x_quant(2, 0)
         h1_scale(0, 1)
+        x_quant(2, 1)
         h1_scale(1, 0)
         h1_scale(1, 1)
-        x_quant(2, 0)
-        x_quant(2, 1)
         for b in range(NB):
             w_pass(1, b, 2, 1, stop=True)
-        h1_turn(first[0], 6)
-        h1_turn(first[1], 7)
-        finish(1, 0, 2)
-        finish(1, 1, 2)
-        h1_empty(first[0], "scalar")
-        h1_empty(first[1], "scalar")
-        finish(1, 2, 2)
-        finish(1, 3, 2)
+        for b in range(NB):
+            finish(1, b, 2)
         h1_scale(0, 2)
         h1_scale(1, 2)
-        h1_quant(first[0])
-        h1_scale(2, 0)
-        h1_quant(first[1])
 
         def head(b, j, i):
             open_group(2, b, j, i)
             w_pass(2, b, j, 0, start=True)
             w_pass(2, b, j, 1)
 
-        for j, i in enumerate((3, 5, 0)):
-            head(0, j, i)
-        h1_turn(last[0], 6)
-        x_turn(2, 2, 7)
-        h1_empty(last[0], "scalar")
-        x_empty(2, 2, "scalar")
-        h1_scale(2, 1)
-        h1_scale(2, 2)
-        h1_quant(last[0])
-        h1_scale(3, 2)
-        h1_scale(3, 0)
-        h1_scale(3, 1)
-        x_sort(2, 3, "scalar")
-        x_quant(2, 2)
-        head(1, 0, 1)
-        early = [(0, 0), (0, 1), (0, 2), (1, 0)]
-        for b, j in early:
-            u_pass(2, b, j, 0)
-            u_pass(2, b, j, 1)
-        for b, j in early:
+        def close(b, j):
             u_pass(2, b, j, 2, stop=True)
             finish(2, b, j)
 
@@ -491,31 +495,58 @@ def tile_two_step_rnn_fp4_s3_kernel(tc, x1, x2, h0, gain, w_bytes, w_scale, u_wo
                 u_pass(2, b, j, g, stop=g == NJ - 1, c0=c0, c1=c1)
             finish(2, b, j, c0, c1)
 
-        h1_turn(first[2], 2)
-        h1_turn(last[1], 4)
-        h1_turn(first[3], 6)
-        x_turn(2, 3, 7)
+        early = [(0, 0), (0, 1), (0, 2), (1, 0), (1, 1)]
+        for (b, j), i in zip(early[:4], (3, 5, 6, 7)):
+            head(b, j, i)
+        h1_turn(first[0], 0)
+        h1_turn(first[1], 1)
+        h1_turn(last[0], 2)
+        head(1, 1, 4)
+        h1_empty(first[0], "scalar")
+        h1_empty(first[1], "scalar")
+        h1_empty(last[0], "scalar")
+        x2_sort(2, "scalar")
+        x2_sort(3, "scalar")
+        h1_scale(2, 0)
+        h1_quant(first[0])
+        h1_scale(2, 1)
+        h1_quant(first[1])
+        h1_quant(last[0])
+        h1_scale(2, 2)
+        h1_scale(3, 2)
+        h1_scale(3, 0)
+        h1_scale(3, 1)
+        x2_turn(2)
+        x2_turn(3)
+        for b, j in early:
+            u_pass(2, b, j, 0)
+            u_pass(2, b, j, 1)
+        for b, j in early[:3]:
+            close(b, j)
+        x2_pair(2, "scalar")
+        h1_turn(first[2], 0)
+        h1_turn(last[1], 1)
+        h1_turn(first[3], 2)
+        x_quant(2, 2)
         h1_empty(first[2], "vector")
         h1_empty(last[1], "vector")
         h1_quant(first[2])
         h1_quant(last[1])
         h1_empty(first[3], "vector")
-        x_empty(2, 3, "vector")
+        x2_pair(3, "vector")
         h1_quant(first[3])
         x_quant(2, 3)
-
-        def groups2(b, js, banks):
-            for j, i in zip(js, banks):
-                head(b, j, i)
-            for j in js:
-                for g in range(NJ):
-                    u_pass(2, b, j, g, stop=g == NJ - 1)
-                finish(2, b, j)
-
-        groups2(1, (1, 2), (3, 5))
-        groups2(2, (0, 1, 2), (0, 1, 2))
+        for b, j in early[3:]:
+            close(b, j)
+        group2(1, 2, 3)
+        for j, i in enumerate((5, 6, 7)):
+            head(2, j, i)
+        for j in range(NJ):
+            u_pass(2, 2, j, 0)
+            u_pass(2, 2, j, 1)
+            close(2, j)
         group2(3, 0, 4)
-        group2(3, 1, 6)
-        group2(3, 2, 7, 0, 256)
-        group2(3, 2, 3, 256, 384)
-        group2(3, 2, 5, 384, 512)
+        group2(3, 1, 0)
+        group2(3, 2, 1, 0, 256)
+        group2(3, 2, 2, 256, 384)
+        group2(3, 2, 3, 384, 512)

@@ -189,7 +189,7 @@ def tile_two_step_rnn_fp4_s3_kernel(tc, x1, x2, h0, gain, w_bytes, w_scale, u_wo
             for g in range(NX):
                 x_op[s, b, g] = (codes, scales, P * g)
 
-        x2_quads = [keep_tile([P, NX, 8, P], BF16, "x2_quads_%d" % half) for half in range(2)]
+        x2_quads = {1: keep_tile([P, NX, 8, P], BF16, "x2_quads")}
         x2_blocks = {}
 
         def load_x2_half(half):
@@ -278,7 +278,7 @@ def tile_two_step_rnn_fp4_s3_kernel(tc, x1, x2, h0, gain, w_bytes, w_scale, u_wo
         h_sb, scaled = {}, {}
 
         def finish(s, b, j, c0=0, c1=N):
-            h = work.tile([P, N], F32, tag="h", name="h", align_bytes=ALIGN, bufs=10)
+            h = work.tile([P, N], F32, tag="h", name="h", align_bytes=ALIGN, bufs=12)
             h_sb[s, b, j] = h
             nc.scalar.activation(out=h[:, 0 : c1 - c0], in_=acc[s, b, j][:, 0 : c1 - c0], func=TANH)
             out = out_0 if s == 1 else out_1
@@ -356,7 +356,8 @@ def tile_two_step_rnn_fp4_s3_kernel(tc, x1, x2, h0, gain, w_bytes, w_scale, u_wo
         load_w(1, 2, 3)
         load_u(2)
         load_u_scales(2, 3)
-        load_x2_half(0)
+        load_x(2, 0, 1)
+        load_x(2, 1, 2)
         load_x2_half(1)
         gain_row = keep_tile([P, NJ, N], BF16, "gain_row")
 
@@ -444,8 +445,8 @@ def tile_two_step_rnn_fp4_s3_kernel(tc, x1, x2, h0, gain, w_bytes, w_scale, u_wo
         finish(1, 2, 0)
         finish(1, 3, 0)
         w_widen(2, 1, (0, 1, 2), "scalar")
-        x2_sort(0, "scalar")
-        x2_sort(1, "scalar")
+        x_sort(2, 0, "scalar")
+        x_sort(2, 1, "scalar")
         w_weave(2, 0)
         u_group(2, 2, 2)
         u_group(3, 2, 4)
@@ -454,23 +455,23 @@ def tile_two_step_rnn_fp4_s3_kernel(tc, x1, x2, h0, gain, w_bytes, w_scale, u_wo
         w_widen(2, 1, (3,), "vector")
         w_quant(2, 0)
         w_weave(2, 1)
-        x2_turn(0)
-        w_quant(2, 1)
-        x2_turn(1)
         finish(1, 0, 1)
         finish(1, 1, 1)
-        x2_pair(0, "scalar")
+        h1_scale(0, 0)
+        w_quant(2, 1)
+        x_turn(2, 0, 6)
+        x_turn(2, 1, 7)
         for b in range(NB):
             w_pass(1, b, 2, 0)
         finish(1, 2, 1)
         finish(1, 3, 1)
-        x2_pair(1, "scalar")
-        h1_scale(0, 0)
-        x_quant(2, 0)
+        x_empty(2, 0, "scalar")
+        x_empty(2, 1, "scalar")
         h1_scale(0, 1)
-        x_quant(2, 1)
         h1_scale(1, 0)
+        x_quant(2, 0)
         h1_scale(1, 1)
+        x_quant(2, 1)
         for b in range(NB):
             w_pass(1, b, 2, 1, stop=True)
         for b in range(NB):
@@ -496,11 +497,12 @@ def tile_two_step_rnn_fp4_s3_kernel(tc, x1, x2, h0, gain, w_bytes, w_scale, u_wo
             finish(2, b, j, c0, c1)
 
         early = [(0, 0), (0, 1), (0, 2), (1, 0), (1, 1)]
-        for (b, j), i in zip(early[:4], (3, 5, 6, 7)):
-            head(b, j, i)
+        for j, i in enumerate((3, 5, 6)):
+            head(0, j, i)
         h1_turn(first[0], 0)
         h1_turn(first[1], 1)
         h1_turn(last[0], 2)
+        head(1, 0, 7)
         head(1, 1, 4)
         h1_empty(first[0], "scalar")
         h1_empty(first[1], "scalar")
@@ -511,8 +513,8 @@ def tile_two_step_rnn_fp4_s3_kernel(tc, x1, x2, h0, gain, w_bytes, w_scale, u_wo
         h1_quant(first[0])
         h1_scale(2, 1)
         h1_quant(first[1])
-        h1_quant(last[0])
         h1_scale(2, 2)
+        h1_quant(last[0])
         h1_scale(3, 2)
         h1_scale(3, 0)
         h1_scale(3, 1)
@@ -523,21 +525,21 @@ def tile_two_step_rnn_fp4_s3_kernel(tc, x1, x2, h0, gain, w_bytes, w_scale, u_wo
             u_pass(2, b, j, 1)
         for b, j in early[:3]:
             close(b, j)
-        x2_pair(2, "scalar")
         h1_turn(first[2], 0)
         h1_turn(last[1], 1)
         h1_turn(first[3], 2)
-        x_quant(2, 2)
+        x2_pair(2, "vector")
         h1_empty(first[2], "vector")
+        x_quant(2, 2)
         h1_empty(last[1], "vector")
         h1_quant(first[2])
         h1_quant(last[1])
-        h1_empty(first[3], "vector")
-        x2_pair(3, "vector")
-        h1_quant(first[3])
-        x_quant(2, 3)
         for b, j in early[3:]:
             close(b, j)
+        x2_pair(3, "scalar")
+        h1_empty(first[3], "vector")
+        x_quant(2, 3)
+        h1_quant(first[3])
         group2(1, 2, 3)
         for j, i in enumerate((5, 6, 7)):
             head(2, j, i)
@@ -546,7 +548,8 @@ def tile_two_step_rnn_fp4_s3_kernel(tc, x1, x2, h0, gain, w_bytes, w_scale, u_wo
             u_pass(2, 2, j, 1)
             close(2, j)
         group2(3, 0, 4)
-        group2(3, 1, 0)
-        group2(3, 2, 1, 0, 256)
-        group2(3, 2, 2, 256, 384)
-        group2(3, 2, 3, 384, 512)
+        group2(3, 1, 0, 0, 256)
+        group2(3, 1, 1, 256, 512)
+        group2(3, 2, 2, 0, 256)
+        group2(3, 2, 3, 256, 384)
+        group2(3, 2, 5, 384, 512)

@@ -53,11 +53,19 @@ def tile_two_step_rnn_fp4_s3_kernel(tc, x1, x2, h0, gain, w_bytes, w_scale, u_wo
             nc.sync.dma_start(out=h0_raw[b][:], in_=h0[P * b : P * b + P, :])
 
         def load_u(j):
-            u_sb[j] = keep_tile([P, NJ, 2 * N], U8, "u_%d" % j)
+            t = keep_tile([P, NJ, 2 * N], U8, "u_%d" % j)
+            u_sb[j] = [t[:, g, :] for g in range(NJ)]
             nc.sync.dma_start(
-                out=u_sb[j][:].bitcast(I32),
+                out=t[:].bitcast(I32),
                 in_=u_words[:, :, 2 * N * j : 2 * N * j + 2 * N].rearrange("g p n -> p g n").bitcast(I32),
             )
+
+        def load_u_by_pass(j):
+            u_sb[j] = [keep_tile([P, 2 * N], U8, "u_%d_%d" % (j, g)) for g in range(NJ)]
+            for g in range(NJ):
+                nc.sync.dma_start(
+                    out=u_sb[j][g][:].bitcast(I32), in_=u_words[g, :, 2 * N * j : 2 * N * j + 2 * N].bitcast(I32)
+                )
 
         def zero_u_scales(j0, j1):
             t = keep_tile([P, NJ, N * (j1 - j0)], U8, "us_%d" % j0)
@@ -232,11 +240,12 @@ def tile_two_step_rnn_fp4_s3_kernel(tc, x1, x2, h0, gain, w_bytes, w_scale, u_wo
                         out=wide[j, g][:, t, :], in0=src, scalar1=w_sc[:, g, t : t + 1], scalar2=None, op0=MULT
                     )
 
-        def w_weave(j, g, engine="vector"):
+        def w_weave(j, g, engine="vector", c0=0, c1=N):
             key = "w_%d_%d" % (j, g)
-            grouped[key] = work.tile([P, 4 * N], BF16, tag="w_grp", name="w_grp", align_bytes=ALIGN)
-            dst = grouped[key][:].rearrange("p (c i t) -> p c t i", i=4, t=4)
-            frm = wide[j, g][:].rearrange("p t (c i) -> p c t i", i=4)
+            if key not in grouped:
+                grouped[key] = work.tile([P, 4 * N], BF16, tag="w_grp", name="w_grp", align_bytes=ALIGN)
+            dst = grouped[key][:, 4 * c0 : 4 * c1].rearrange("p (c i t) -> p c t i", i=4, t=4)
+            frm = wide[j, g][:, :, c0:c1].rearrange("p t (c i) -> p c t i", i=4)
             if engine == "scalar":
                 nc.scalar.copy(out=dst, in_=frm)
             else:
@@ -257,7 +266,7 @@ def tile_two_step_rnn_fp4_s3_kernel(tc, x1, x2, h0, gain, w_bytes, w_scale, u_wo
                 out=acc[s, b, j][:, 0 : c1 - c0],
                 lhsT=codes[:, c : c + P].bitcast(E4M3X4),
                 lhsT_scale=scales[:, c : c + P],
-                rhs=u_sb[j][:, g, 2 * c0 : 2 * c1].bitcast(E2M1X4),
+                rhs=u_sb[j][g][:, 2 * c0 : 2 * c1].bitcast(E2M1X4),
                 rhs_scale=plane[:, g, p0 + c0 : p0 + c1],
                 start=start,
                 stop=stop,
@@ -320,6 +329,11 @@ def tile_two_step_rnn_fp4_s3_kernel(tc, x1, x2, h0, gain, w_bytes, w_scale, u_wo
             w_pass(1, b, j, 0)
             w_pass(1, b, j, 1, stop=True)
 
+        gain_row = keep_tile([P, NJ, N], BF16, "gain_row")
+
+        def load_gain_row():
+            nc.sync.dma_start(out=gain_row[:].rearrange("p j n -> p (j n)"), in_=gain.partition_broadcast(P))
+
         gain_col = keep_tile([P, NJ, 4], BF16, "gain_col")
         nc.scalar.dma_start(out=gain_col[:], in_=gain.rearrange("(g p t) -> p g t", p=P, t=4))
         w_sc = keep_tile([P, NX, 4], F32, "w_sc")
@@ -359,7 +373,6 @@ def tile_two_step_rnn_fp4_s3_kernel(tc, x1, x2, h0, gain, w_bytes, w_scale, u_wo
         load_x(2, 0, 1)
         load_x(2, 1, 2)
         load_x2_half(1)
-        gain_row = keep_tile([P, NJ, N], BF16, "gain_row")
 
         first = [[(b, 0), (b, 1)] for b in range(NB)]
         last = [[(0, 2), (1, 2)], [(2, 2), (3, 2)]]
@@ -400,59 +413,57 @@ def tile_two_step_rnn_fp4_s3_kernel(tc, x1, x2, h0, gain, w_bytes, w_scale, u_wo
         u_group(2, 0, 2)
         w_widen(0, 1, (0, 1, 2), "scalar")
         w_widen(0, 1, (3,), "vector")
+        w_quant(0, 0)
         x_sort(1, 0, "scalar")
         x_sort(1, 1, "scalar")
         h0_empty([(3, 2)])
         h0_empty(first[3])
         h0_quant([(3, 2)])
         h0_quant(first[3])
-        w_quant(0, 0)
         w_weave(0, 1)
         x_turn(1, 0, 6)
         x_turn(1, 1, 7)
         x_turn(1, 2, 3)
         x_turn(1, 3, 5)
-        x_empty(1, 0, "scalar")
-        x_empty(1, 1, "scalar")
-        x_empty(1, 2, "scalar")
-        x_empty(1, 3, "scalar")
+        for b in range(NB):
+            x_empty(1, b, "scalar")
         x_quant(1, 0)
         w_quant(0, 1)
         x_quant(1, 1)
+        w_widen(1, 0, (0, 1), "vector")
         x_quant(1, 2)
+        w_widen(1, 0, (2, 3), "vector")
         x_quant(1, 3)
+        w_weave(1, 0)
         u_group(3, 0, 4)
         u_group(0, 1, 6)
         u_group(1, 1, 7)
-        w_widen(1, 0, (0, 1), "scalar")
-        w_widen(1, 0, (2, 3), "vector")
         w_widen(1, 1, (0, 1, 2), "scalar")
-        w_weave(1, 0)
         w_widen(1, 1, (3,), "vector")
         w_quant(1, 0)
         w_weave(1, 1)
+        w_widen(2, 0, (0, 1), "scalar")
+        w_widen(2, 0, (2, 3), "vector")
+        w_quant(1, 1)
+        w_weave(2, 0)
         for b in range(NB):
             w_close(b, 0)
         u_group(2, 1, 3)
         u_group(3, 1, 5)
         finish(1, 0, 0)
         finish(1, 1, 0)
-        w_widen(2, 0, (0, 1), "scalar")
-        w_widen(2, 0, (2, 3), "vector")
-        w_quant(1, 1)
         u_group(0, 2, 0)
         u_group(1, 2, 1)
         finish(1, 2, 0)
         finish(1, 3, 0)
-        w_widen(2, 1, (0, 1, 2), "scalar")
+        w_widen(2, 1, (0, 1), "scalar")
+        w_widen(2, 1, (2, 3), "vector")
         x_sort(2, 0, "scalar")
         x_sort(2, 1, "scalar")
-        w_weave(2, 0)
         u_group(2, 2, 2)
         u_group(3, 2, 4)
         for b in range(NB):
             w_close(b, 1)
-        w_widen(2, 1, (3,), "vector")
         w_quant(2, 0)
         w_weave(2, 1)
         finish(1, 0, 1)
@@ -510,16 +521,15 @@ def tile_two_step_rnn_fp4_s3_kernel(tc, x1, x2, h0, gain, w_bytes, w_scale, u_wo
         x2_sort(2, "scalar")
         x2_sort(3, "scalar")
         h1_scale(2, 0)
-        h1_quant(first[0])
         h1_scale(2, 1)
-        h1_quant(first[1])
+        h1_quant(first[0])
         h1_scale(2, 2)
-        h1_quant(last[0])
+        h1_quant(first[1])
         h1_scale(3, 2)
+        h1_quant(last[0])
         h1_scale(3, 0)
         h1_scale(3, 1)
         x2_turn(2)
-        x2_turn(3)
         for b, j in early:
             u_pass(2, b, j, 0)
             u_pass(2, b, j, 1)
@@ -533,10 +543,11 @@ def tile_two_step_rnn_fp4_s3_kernel(tc, x1, x2, h0, gain, w_bytes, w_scale, u_wo
         x_quant(2, 2)
         h1_empty(last[1], "vector")
         h1_quant(first[2])
+        x2_turn(3)
         h1_quant(last[1])
         for b, j in early[3:]:
             close(b, j)
-        x2_pair(3, "scalar")
+        x2_pair(3, "vector")
         h1_empty(first[3], "vector")
         x_quant(2, 3)
         h1_quant(first[3])

@@ -138,8 +138,11 @@ def tile_two_step_rnn_fp4_s3_kernel(tc, x1, x2, h0, gain, w_bytes, w_scale, u_wo
                 op=MULT,
             )
 
-        def spread_gain(g, i, engine):
+        gain_banks = {}
+
+        def spread_gain(g, i, engine=None):
             rows = bank_tile(i)
+            gain_banks[g] = rows
             for t in range(4):
                 nc.tensor.matmul(
                     rows[:, P * t : P * t + P],
@@ -148,6 +151,11 @@ def tile_two_step_rnn_fp4_s3_kernel(tc, x1, x2, h0, gain, w_bytes, w_scale, u_wo
                     start=True,
                     stop=True,
                 )
+            if engine:
+                gain_empty(g, engine)
+
+        def gain_empty(g, engine):
+            rows = gain_banks[g]
             dst = gain_row[:, g, :].rearrange("p (u w e) -> p u w e", u=2, e=2)
             frm = rows[:].rearrange("p (u e w) -> p u w e", u=2, e=2)
             if engine == "scalar":
@@ -388,8 +396,8 @@ def tile_two_step_rnn_fp4_s3_kernel(tc, x1, x2, h0, gain, w_bytes, w_scale, u_wo
             h0_quant([(b, 2)])
 
 
-        def warm_up(count):
-            bank = bank_tile(1)
+        def warm_up(count, i=1):
+            bank = bank_tile(i)
             for c in range(count):
                 nc.tensor.matmul(bank[:], lhsT=zeros[:, 0:P], rhs=zeros[:], start=True, stop=True)
 
@@ -416,11 +424,12 @@ def tile_two_step_rnn_fp4_s3_kernel(tc, x1, x2, h0, gain, w_bytes, w_scale, u_wo
         w_quant(0, 0)
         x_sort(1, 0, "scalar")
         x_sort(1, 1, "scalar")
+        w_weave(0, 1, "scalar", 0, N // 2)
         h0_empty([(3, 2)])
         h0_empty(first[3])
         h0_quant([(3, 2)])
         h0_quant(first[3])
-        w_weave(0, 1)
+        w_weave(0, 1, "vector", N // 2, N)
         x_turn(1, 0, 6)
         x_turn(1, 1, 7)
         x_turn(1, 2, 3)
@@ -456,8 +465,8 @@ def tile_two_step_rnn_fp4_s3_kernel(tc, x1, x2, h0, gain, w_bytes, w_scale, u_wo
         u_group(1, 2, 1)
         finish(1, 2, 0)
         finish(1, 3, 0)
-        w_widen(2, 1, (0, 1), "scalar")
-        w_widen(2, 1, (2, 3), "vector")
+        w_widen(2, 1, (0, 1, 2), "scalar")
+        w_widen(2, 1, (3,), "vector")
         x_sort(2, 0, "scalar")
         x_sort(2, 1, "scalar")
         u_group(2, 2, 2)

@@ -302,7 +302,7 @@ def tile_two_step_rnn_fp4_s3_kernel(tc, x1, x2, h0, gain, w_bytes, w_scale, u_wo
             nc.sync.dma_start(out=out[P * b : P * b + P, N * j + c0 : N * j + c1], in_=h[:, 0 : c1 - c0])
 
         def h1_scale(b, j):
-            scaled[b, j] = work.tile([P, N], BF16, tag="scaled", name="scaled", align_bytes=ALIGN, bufs=8)
+            scaled[b, j] = work.tile([P, N], BF16, tag="scaled", name="scaled", align_bytes=ALIGN, bufs=6)
             nc.vector.tensor_tensor(
                 out=scaled[b, j][:].rearrange("p (u w e) -> p u w e", u=2, e=2),
                 in0=h_sb[1, b, j][:].rearrange("p (w u e) -> p u w e", u=2, e=2),
@@ -327,6 +327,44 @@ def tile_two_step_rnn_fp4_s3_kernel(tc, x1, x2, h0, gain, w_bytes, w_scale, u_wo
             codes, scales = quantise(h1_key(parts), N * len(parts))
             for c, (b, j) in enumerate(parts):
                 r_op[2, b, j] = (codes, scales, P * c)
+
+        park = out_1[3 * P : 4 * P, :].bitcast(BF16).rearrange("r n -> (r n)").rearrange("(s a m w) -> s a m w", a=4, m=P, w=P)
+        back, h1_blocks = {}, {}
+
+        def late_scale(parts):
+            key = h1_key(parts)
+            scaled[key] = work.tile([P, N * len(parts)], BF16, tag="late", name="late", align_bytes=ALIGN, bufs=1)
+            for c, (b, j) in enumerate(parts):
+                dst = scaled[key][:, N * c : N * c + N].rearrange("p (a u w e) -> p u a w e", a=4, u=2, e=2)
+                frm = h_sb[1, b, j][:].rearrange("p (a w u e) -> p u a w e", a=4, u=2, e=2)
+                by = gain_row[:, j, :].rearrange("p (u a w e) -> p u a w e", a=4, u=2, e=2)
+                for u in range(2):
+                    nc.vector.tensor_tensor(out=dst[:, u], in0=frm[:, u], in1=by[:, u], op=MULT)
+
+        def late_park(parts, s0):
+            words = scaled[h1_key(parts)][:].rearrange("p (x w) -> p x w", w=P)
+            nc.sync.dma_start(out=park[s0 : s0 + len(parts)].rearrange("s a m w -> m (s a) w"), in_=words)
+
+        def late_fetch(parts, s0):
+            key = h1_key(parts)
+            n = len(parts)
+            back[key] = work.tile([P, N * n], BF16, tag="back", name="back", align_bytes=ALIGN, bufs=1)
+            nc.sync.dma_start(
+                out=back[key][:].rearrange("p (s x) -> p s x", s=n),
+                in_=park[s0 : s0 + n].rearrange("s a (i r) w -> (a i) s (r w)", r=4),
+            )
+
+        def late_turn(parts):
+            key = h1_key(parts)
+            h1_blocks[key] = work.tile([P, 2 * P * len(parts)], F32, tag="blocks", name="blocks", align_bytes=ALIGN, bufs=2)
+            nc.vector.transpose(h1_blocks[key][:], back[key][:].bitcast(F32))
+
+        def late_pair(parts, engine):
+            key = h1_key(parts)
+            n = len(parts)
+            grouped[key] = keep_tile([P, N * n], BF16, "g_" + key)
+            dst = grouped[key][:].bitcast(F32).rearrange("p (s c i t) -> p s c t i", s=n, i=2, t=8)
+            copy(engine, dst, h1_blocks[key][:].rearrange("p (s t c i) -> p s c t i", s=n, t=8, i=2))
 
         def u_group(b, j, i):
             open_group(1, b, j, i)
@@ -529,15 +567,16 @@ def tile_two_step_rnn_fp4_s3_kernel(tc, x1, x2, h0, gain, w_bytes, w_scale, u_wo
         h1_empty(last[0], "scalar")
         x2_sort(2, "scalar")
         x2_sort(3, "scalar")
-        h1_scale(2, 0)
-        h1_scale(2, 1)
+        late_scale(first[3])
+        late_park(first[3], 0)
         h1_quant(first[0])
-        h1_scale(2, 2)
+        h1_scale(2, 0)
         h1_quant(first[1])
-        h1_scale(3, 2)
+        h1_scale(2, 1)
         h1_quant(last[0])
-        h1_scale(3, 0)
-        h1_scale(3, 1)
+        h1_scale(2, 2)
+        h1_scale(3, 2)
+        late_fetch(first[3], 0)
         x2_turn(2)
         for b, j in early:
             u_pass(2, b, j, 0)
@@ -546,21 +585,21 @@ def tile_two_step_rnn_fp4_s3_kernel(tc, x1, x2, h0, gain, w_bytes, w_scale, u_wo
             close(b, j)
         h1_turn(first[2], 0)
         h1_turn(last[1], 1)
-        h1_turn(first[3], 2)
         x2_pair(2, "vector")
         h1_empty(first[2], "vector")
         x_quant(2, 2)
-        h1_empty(last[1], "vector")
+        h1_empty(last[1], "scalar")
         h1_quant(first[2])
         x2_turn(3)
         h1_quant(last[1])
         for b, j in early[3:]:
             close(b, j)
-        x2_pair(3, "vector")
-        h1_empty(first[3], "vector")
+        late_turn(first[3])
+        group2(1, 2, 3)
+        x2_pair(3, "scalar")
+        late_pair(first[3], "vector")
         x_quant(2, 3)
         h1_quant(first[3])
-        group2(1, 2, 3)
         for j, i in enumerate((5, 6, 7)):
             head(2, j, i)
         for j in range(NJ):

@@ -130,7 +130,7 @@ def tile_two_step_rnn_fp4_s3_kernel(tc, x1, x2, h0, gain, w_bytes, w_scale, u_wo
             key = h0_key(parts)
             bank, n = turned[key]
             g0, g1 = parts[0][1], parts[-1][1] + 1
-            grouped[key] = keep_tile([P, N * n], BF16, "g_" + key)
+            grouped[key] = work.tile([P, N * n], BF16, tag="grouped", name="grouped", align_bytes=ALIGN, bufs=10)
             nc.vector.tensor_tensor(
                 out=grouped[key][:].rearrange("p (c r u e) -> p c r u e", c=n, u=2, e=2),
                 in0=bank[:, 0 : 2 * P * n].bitcast(BF16).rearrange("p (u c r e) -> p c r u e", u=2, c=n, e=2),
@@ -170,7 +170,7 @@ def tile_two_step_rnn_fp4_s3_kernel(tc, x1, x2, h0, gain, w_bytes, w_scale, u_wo
 
         def empty(key, engine):
             bank, n = turned[key]
-            grouped[key] = keep_tile([P, N * n], BF16, "g_" + key)
+            grouped[key] = work.tile([P, N * n], BF16, tag="grouped", name="grouped", align_bytes=ALIGN, bufs=10)
             dst = grouped[key][:].bitcast(F32).rearrange("p (r u) -> p r u", u=2)
             frm = bank[:, 0 : 2 * P * n].rearrange("p (u r) -> p r u", u=2)
             if engine == "scalar":
@@ -224,12 +224,12 @@ def tile_two_step_rnn_fp4_s3_kernel(tc, x1, x2, h0, gain, w_bytes, w_scale, u_wo
             copy(engine, dst, frm.rearrange("p g (w u) -> p g u w", u=2))
 
         def x2_turn(b):
-            x2_blocks[b] = work.tile([P, D // 2], F32, tag="blocks", name="blocks", align_bytes=ALIGN, bufs=2)
+            x2_blocks[b] = work.tile([P, D // 2], F32, tag="blocks", name="blocks", align_bytes=ALIGN, bufs=3)
             nc.vector.transpose(x2_blocks[b][:], x_sorted[2, b][:].bitcast(F32))
 
         def x2_pair(b, engine):
             key = "x2_%d" % b
-            grouped[key] = keep_tile([P, D], BF16, "g_" + key)
+            grouped[key] = work.tile([P, D], BF16, tag="grouped", name="grouped", align_bytes=ALIGN, bufs=10)
             dst = grouped[key][:].bitcast(F32).rearrange("p (g r u) -> p g r u", g=NX, u=2)
             copy(engine, dst, x2_blocks[b][:].rearrange("p (g u r) -> p g r u", g=NX, u=2))
 
@@ -333,7 +333,7 @@ def tile_two_step_rnn_fp4_s3_kernel(tc, x1, x2, h0, gain, w_bytes, w_scale, u_wo
 
         def late_scale(parts):
             key = h1_key(parts)
-            scaled[key] = work.tile([P, N * len(parts)], BF16, tag="late", name="late", align_bytes=ALIGN, bufs=1)
+            scaled[key] = work.tile([P, N * len(parts)], BF16, tag="late", name="late", align_bytes=ALIGN, bufs=3)
             for c, (b, j) in enumerate(parts):
                 dst = scaled[key][:, N * c : N * c + N].rearrange("p (a u w e) -> p u a w e", a=4, u=2, e=2)
                 frm = h_sb[1, b, j][:].rearrange("p (a w u e) -> p u a w e", a=4, u=2, e=2)
@@ -348,7 +348,7 @@ def tile_two_step_rnn_fp4_s3_kernel(tc, x1, x2, h0, gain, w_bytes, w_scale, u_wo
         def late_fetch(parts, s0):
             key = h1_key(parts)
             n = len(parts)
-            back[key] = work.tile([P, N * n], BF16, tag="back", name="back", align_bytes=ALIGN, bufs=1)
+            back[key] = work.tile([P, N * n], BF16, tag="back", name="back", align_bytes=ALIGN, bufs=3)
             nc.sync.dma_start(
                 out=back[key][:].rearrange("p (s x) -> p s x", s=n),
                 in_=park[s0 : s0 + n].rearrange("s a (i r) w -> (a i) s (r w)", r=4),
@@ -356,13 +356,13 @@ def tile_two_step_rnn_fp4_s3_kernel(tc, x1, x2, h0, gain, w_bytes, w_scale, u_wo
 
         def late_turn(parts):
             key = h1_key(parts)
-            h1_blocks[key] = work.tile([P, 2 * P * len(parts)], F32, tag="blocks", name="blocks", align_bytes=ALIGN, bufs=2)
+            h1_blocks[key] = work.tile([P, 2 * P * len(parts)], F32, tag="blocks", name="blocks", align_bytes=ALIGN, bufs=3)
             nc.vector.transpose(h1_blocks[key][:], back[key][:].bitcast(F32))
 
         def late_pair(parts, engine):
             key = h1_key(parts)
             n = len(parts)
-            grouped[key] = keep_tile([P, N * n], BF16, "g_" + key)
+            grouped[key] = work.tile([P, N * n], BF16, tag="grouped", name="grouped", align_bytes=ALIGN, bufs=10)
             dst = grouped[key][:].bitcast(F32).rearrange("p (s c i t) -> p s c t i", s=n, i=2, t=8)
             copy(engine, dst, h1_blocks[key][:].rearrange("p (s t c i) -> p s c t i", s=n, t=8, i=2))
 
@@ -562,53 +562,58 @@ def tile_two_step_rnn_fp4_s3_kernel(tc, x1, x2, h0, gain, w_bytes, w_scale, u_wo
         h1_turn(last[0], 2)
         head(1, 0, 7)
         head(1, 1, 4)
+        x2_sort(2, "scalar")
         h1_empty(first[0], "scalar")
         h1_empty(first[1], "scalar")
         h1_empty(last[0], "scalar")
-        x2_sort(2, "scalar")
         x2_sort(3, "scalar")
-        late_scale(first[3])
-        late_park(first[3], 0)
+        late_scale(first[2])
+        late_park(first[2], 0)
         h1_quant(first[0])
-        h1_scale(2, 0)
+        late_scale(first[3])
+        late_park(first[3], 2)
+        late_fetch(first[2], 0)
+        late_fetch(first[3], 2)
         h1_quant(first[1])
-        h1_scale(2, 1)
         h1_quant(last[0])
+        x2_turn(2)
+        x2_pair(2, "scalar")
         h1_scale(2, 2)
         h1_scale(3, 2)
-        late_fetch(first[3], 0)
-        x2_turn(2)
+        x_quant(2, 2)
         for b, j in early:
             u_pass(2, b, j, 0)
             u_pass(2, b, j, 1)
         for b, j in early[:3]:
             close(b, j)
-        h1_turn(first[2], 0)
+        for b, j in early[3:]:
+            u_pass(2, b, j, 2, stop=True)
         h1_turn(last[1], 1)
-        x2_pair(2, "vector")
-        h1_empty(first[2], "vector")
-        x_quant(2, 2)
+        late_turn(first[2])
         h1_empty(last[1], "scalar")
-        h1_quant(first[2])
+        late_pair(first[2], "scalar")
         x2_turn(3)
         h1_quant(last[1])
-        for b, j in early[3:]:
-            close(b, j)
-        late_turn(first[3])
-        group2(1, 2, 3)
+        h1_quant(first[2])
+        finish(2, 1, 0)
         x2_pair(3, "scalar")
-        late_pair(first[3], "vector")
+        finish(2, 1, 1)
+        late_turn(first[3])
+        group2(1, 2, 0)
         x_quant(2, 3)
+        late_pair(first[3], "vector")
         h1_quant(first[3])
-        for j, i in enumerate((5, 6, 7)):
+        for j, i in enumerate((2, 3, 5)):
             head(2, j, i)
         for j in range(NJ):
+            u_pass(2, 2, j, 2)
+        for j in range(NJ):
             u_pass(2, 2, j, 0)
-            u_pass(2, 2, j, 1)
-            close(2, j)
-        group2(3, 0, 4)
-        group2(3, 1, 0, 0, 256)
-        group2(3, 1, 1, 256, 512)
-        group2(3, 2, 2, 0, 256)
-        group2(3, 2, 3, 256, 384)
-        group2(3, 2, 5, 384, 512)
+            u_pass(2, 2, j, 1, stop=True)
+            finish(2, 2, j)
+        group2(3, 0, 6)
+        group2(3, 1, 7, 0, 256)
+        group2(3, 1, 4, 256, 512)
+        group2(3, 2, 1, 0, 256)
+        group2(3, 2, 0, 256, 384)
+        group2(3, 2, 2, 384, 512)

@@ -294,12 +294,16 @@ def tile_two_step_rnn_fp4_s3_kernel(tc, x1, x2, h0, gain, w_bytes, w_scale, u_wo
 
         h_sb, scaled = {}, {}
 
-        def finish(s, b, j, c0=0, c1=N):
+        def store(s, b, j, c0=0, c1=N):
+            out = out_0 if s == 1 else out_1
+            nc.sync.dma_start(out=out[P * b : P * b + P, N * j + c0 : N * j + c1], in_=h_sb[s, b, j][:, 0 : c1 - c0])
+
+        def finish(s, b, j, c0=0, c1=N, later=False):
             h = work.tile([P, N], F32, tag="h", name="h", align_bytes=ALIGN, bufs=12)
             h_sb[s, b, j] = h
             nc.scalar.activation(out=h[:, 0 : c1 - c0], in_=acc[s, b, j][:, 0 : c1 - c0], func=TANH)
-            out = out_0 if s == 1 else out_1
-            nc.sync.dma_start(out=out[P * b : P * b + P, N * j + c0 : N * j + c1], in_=h[:, 0 : c1 - c0])
+            if not later:
+                store(s, b, j, c0, c1)
 
         def h1_scale(b, j):
             scaled[b, j] = work.tile([P, N], BF16, tag="scaled", name="scaled", align_bytes=ALIGN, bufs=6)
@@ -331,14 +335,16 @@ def tile_two_step_rnn_fp4_s3_kernel(tc, x1, x2, h0, gain, w_bytes, w_scale, u_wo
         park = out_1[3 * P : 4 * P, :].bitcast(BF16).rearrange("r n -> (r n)").rearrange("(s a m w) -> s a m w", a=4, m=P, w=P)
         back, h1_blocks = {}, {}
 
-        def late_scale(parts):
+        def late_scale(parts, c0=0, c1=2, us=(0, 1)):
             key = h1_key(parts)
-            scaled[key] = work.tile([P, N * len(parts)], BF16, tag="late", name="late", align_bytes=ALIGN, bufs=3)
-            for c, (b, j) in enumerate(parts):
+            if key not in scaled:
+                scaled[key] = work.tile([P, N * len(parts)], BF16, tag="late", name="late", align_bytes=ALIGN, bufs=3)
+            for c in range(c0, c1):
+                b, j = parts[c]
                 dst = scaled[key][:, N * c : N * c + N].rearrange("p (a u w e) -> p u a w e", a=4, u=2, e=2)
                 frm = h_sb[1, b, j][:].rearrange("p (a w u e) -> p u a w e", a=4, u=2, e=2)
                 by = gain_row[:, j, :].rearrange("p (u a w e) -> p u a w e", a=4, u=2, e=2)
-                for u in range(2):
+                for u in us:
                     nc.vector.tensor_tensor(out=dst[:, u], in0=frm[:, u], in1=by[:, u], op=MULT)
 
         def late_park(parts, s0):
@@ -365,6 +371,17 @@ def tile_two_step_rnn_fp4_s3_kernel(tc, x1, x2, h0, gain, w_bytes, w_scale, u_wo
             grouped[key] = work.tile([P, N * n], BF16, tag="grouped", name="grouped", align_bytes=ALIGN, bufs=10)
             dst = grouped[key][:].bitcast(F32).rearrange("p (s c i t) -> p s c t i", s=n, i=2, t=8)
             copy(engine, dst, h1_blocks[key][:].rearrange("p (s t c i) -> p s c t i", s=n, t=8, i=2))
+
+        def h1_empty_pass(parts, c, engine):
+            bank, n = turned[h1_key(parts)]
+            key = "pass_%d_%d" % parts[c]
+            grouped[key] = work.tile([P, N], BF16, tag="grouped", name="grouped", align_bytes=ALIGN, bufs=10)
+            frm = bank[:, 0 : 2 * P * n].rearrange("p (u c r) -> p c r u", u=2, c=n)
+            copy(engine, grouped[key][:].bitcast(F32).rearrange("p (r u) -> p r u", u=2), frm[:, c])
+
+        def h1_quant_pass(parts, c):
+            codes, scales = quantise("pass_%d_%d" % parts[c], N)
+            r_op[(2,) + parts[c]] = (codes, scales, 0)
 
         def u_group(b, j, i):
             open_group(1, b, j, i)
@@ -533,7 +550,7 @@ def tile_two_step_rnn_fp4_s3_kernel(tc, x1, x2, h0, gain, w_bytes, w_scale, u_wo
         for b in range(NB):
             w_pass(1, b, 2, 1, stop=True)
         for b in range(NB):
-            finish(1, b, 2)
+            finish(1, b, 2, later=b >= 2)
         h1_scale(0, 2)
         h1_scale(1, 2)
 
@@ -562,32 +579,42 @@ def tile_two_step_rnn_fp4_s3_kernel(tc, x1, x2, h0, gain, w_bytes, w_scale, u_wo
         h1_turn(last[0], 2)
         head(1, 0, 7)
         head(1, 1, 4)
-        x2_sort(2, "scalar")
-        h1_empty(first[0], "scalar")
+        h1_empty_pass(first[0], 0, "scalar")
+        h1_empty_pass(first[0], 1, "scalar")
         h1_empty(first[1], "scalar")
         h1_empty(last[0], "scalar")
+        x2_sort(2, "scalar")
         x2_sort(3, "scalar")
         late_scale(first[2])
         late_park(first[2], 0)
-        h1_quant(first[0])
-        late_scale(first[3])
+        h1_quant_pass(first[0], 0)
+        late_scale(first[3], 0, 1, (0,))
+        h1_quant_pass(first[0], 1)
+        late_scale(first[3], 0, 1, (1,))
+        h1_quant(first[1])
+        late_scale(first[3], 1, 2)
         late_park(first[3], 2)
         late_fetch(first[2], 0)
+        store(1, 2, 2)
+        store(1, 3, 2)
         late_fetch(first[3], 2)
-        h1_quant(first[1])
         h1_quant(last[0])
         x2_turn(2)
         x2_pair(2, "scalar")
         h1_scale(2, 2)
         h1_scale(3, 2)
         x_quant(2, 2)
-        for b, j in early:
+        for g in range(2):
+            for j in range(NJ):
+                u_pass(2, 0, j, g)
+        for b, j in early[3:]:
             u_pass(2, b, j, 0)
             u_pass(2, b, j, 1)
         for b, j in early[:3]:
             close(b, j)
         for b, j in early[3:]:
             u_pass(2, b, j, 2, stop=True)
+        head(1, 2, 0)
         h1_turn(last[1], 1)
         late_turn(first[2])
         h1_empty(last[1], "scalar")
@@ -599,7 +626,9 @@ def tile_two_step_rnn_fp4_s3_kernel(tc, x1, x2, h0, gain, w_bytes, w_scale, u_wo
         x2_pair(3, "scalar")
         finish(2, 1, 1)
         late_turn(first[3])
-        group2(1, 2, 0)
+        u_pass(2, 1, 2, 0)
+        u_pass(2, 1, 2, 1)
+        close(1, 2)
         x_quant(2, 3)
         late_pair(first[3], "vector")
         h1_quant(first[3])

@@ -81,14 +81,15 @@ def tile_two_step_rnn_fp4_s3_kernel(tc, x1, x2, h0, gain, w_bytes, w_scale, u_wo
                     in_=u_scales[:, r:16:4, N * j0 : N * j1].rearrange("g q n -> q g n").bitcast(I32),
                 )
 
-        def load_w(g, j0, j1):
-            t = keep_tile([P, 4, N * (j1 - j0)], U8, "w_bytes_%d_%d" % (g, j0))
+        def load_w(g, j0, j1, t0=0, t1=4):
+            t = keep_tile([P, t1 - t0, N * (j1 - j0)], U8, "w_bytes_%d_%d_%d" % (g, j0, t0))
             nc.sync.dma_start(
                 out=t[:],
-                in_=w_bytes[N * g : N * g + N, N * j0 : N * j1].rearrange("(p t) n -> p t n", t=4),
+                in_=w_bytes[N * g : N * g + N, N * j0 : N * j1].rearrange("(p t) n -> p t n", t=4)[:, t0:t1, :],
             )
             for j in range(j0, j1):
-                w_raw[j, g] = (t, N * (j - j0))
+                for r in range(t0, t1):
+                    w_raw[j, g, r] = t[:, r - t0, N * (j - j0) : N * (j - j0) + N]
 
         def load_x(s, b0, b1):
             t = keep_tile([P, (b1 - b0) * D], BF16, "x%d_%d" % (s, b0))
@@ -238,9 +239,8 @@ def tile_two_step_rnn_fp4_s3_kernel(tc, x1, x2, h0, gain, w_bytes, w_scale, u_wo
         def w_widen(j, g, ts, engine):
             if (j, g) not in wide:
                 wide[j, g] = work.tile([P, 4, N], BF16, tag="wide", name="wide", align_bytes=ALIGN, bufs=4)
-            raw, c0 = w_raw[j, g]
             for t in ts:
-                src = raw[:, t, c0 : c0 + N].bitcast(E4M3)
+                src = w_raw[j, g, t].bitcast(E4M3)
                 if engine == "scalar":
                     nc.scalar.activation(out=wide[j, g][:, t, :], in_=src, func=COPY, scale=w_sc[:, g, t : t + 1])
                 else:
@@ -332,45 +332,46 @@ def tile_two_step_rnn_fp4_s3_kernel(tc, x1, x2, h0, gain, w_bytes, w_scale, u_wo
             for c, (b, j) in enumerate(parts):
                 r_op[2, b, j] = (codes, scales, P * c)
 
-        park = out_1[3 * P : 4 * P, :].bitcast(BF16).rearrange("r n -> (r n)").rearrange("(s a m w) -> s a m w", a=4, m=P, w=P)
+        parked = out_1[2 * P : 4 * P, :].bitcast(BF16).rearrange("r n -> (r n)")
         back, h1_blocks = {}, {}
 
-        def late_scale(parts, c0=0, c1=2, us=(0, 1)):
+        def park_area(parts, slot):
+            n = len(parts)
+            return parked[slot * N * P : (slot + n) * N * P].rearrange("(a m x) -> a m x", a=4, m=P)
+
+        def late_scale(parts, c0=0, c1=None, us=(0, 1)):
             key = h1_key(parts)
+            n = len(parts)
             if key not in scaled:
-                scaled[key] = work.tile([P, N * len(parts)], BF16, tag="late", name="late", align_bytes=ALIGN, bufs=3)
-            for c in range(c0, c1):
+                scaled[key] = work.tile([P, N * n], BF16, tag="late", name="late", align_bytes=ALIGN, bufs=3)
+            for c in range(c0, n if c1 is None else c1):
                 b, j = parts[c]
-                dst = scaled[key][:, N * c : N * c + N].rearrange("p (a u w e) -> p u a w e", a=4, u=2, e=2)
+                dst = scaled[key][:].rearrange("p (a s u w e) -> p s u a w e", a=4, s=n, u=2, e=2)[:, c]
                 frm = h_sb[1, b, j][:].rearrange("p (a w u e) -> p u a w e", a=4, u=2, e=2)
                 by = gain_row[:, j, :].rearrange("p (u a w e) -> p u a w e", a=4, u=2, e=2)
                 for u in us:
                     nc.vector.tensor_tensor(out=dst[:, u], in0=frm[:, u], in1=by[:, u], op=MULT)
 
-        def late_park(parts, s0):
-            words = scaled[h1_key(parts)][:].rearrange("p (x w) -> p x w", w=P)
-            nc.sync.dma_start(out=park[s0 : s0 + len(parts)].rearrange("s a m w -> m (s a) w"), in_=words)
+        def late_park(parts, slot):
+            words = scaled[h1_key(parts)][:].rearrange("p (a x) -> p a x", a=4)
+            nc.sync.dma_start(out=park_area(parts, slot).rearrange("a m x -> m a x"), in_=words)
 
-        def late_fetch(parts, s0):
+        def late_fetch(parts, slot):
             key = h1_key(parts)
-            n = len(parts)
-            back[key] = work.tile([P, N * n], BF16, tag="back", name="back", align_bytes=ALIGN, bufs=3)
-            nc.sync.dma_start(
-                out=back[key][:].rearrange("p (s x) -> p s x", s=n),
-                in_=park[s0 : s0 + n].rearrange("s a (i r) w -> (a i) s (r w)", r=4),
-            )
+            back[key] = work.tile([P, N * len(parts)], BF16, tag="back", name="back", align_bytes=ALIGN, bufs=2)
+            nc.sync.dma_start(out=back[key][:], in_=park_area(parts, slot).rearrange("a (i r) x -> (a i) (r x)", r=4))
 
         def late_turn(parts):
             key = h1_key(parts)
             h1_blocks[key] = work.tile([P, 2 * P * len(parts)], F32, tag="blocks", name="blocks", align_bytes=ALIGN, bufs=3)
             nc.vector.transpose(h1_blocks[key][:], back[key][:].bitcast(F32))
 
-        def late_pair(parts, engine):
-            key = h1_key(parts)
-            n = len(parts)
-            grouped[key] = work.tile([P, N * n], BF16, tag="grouped", name="grouped", align_bytes=ALIGN, bufs=10)
-            dst = grouped[key][:].bitcast(F32).rearrange("p (s c i t) -> p s c t i", s=n, i=2, t=8)
-            copy(engine, dst, h1_blocks[key][:].rearrange("p (s t c i) -> p s c t i", s=n, t=8, i=2))
+        def late_pair(parts, c, engine):
+            key = "pass_%d_%d" % parts[c]
+            grouped[key] = work.tile([P, N], BF16, tag="grouped", name="grouped", align_bytes=ALIGN, bufs=10)
+            dst = grouped[key][:].bitcast(F32).rearrange("p (c i r u) -> p c r u i", i=2, r=4, u=2)
+            frm = h1_blocks[h1_key(parts)][:].rearrange("p (r s u c i) -> p s c r u i", r=4, s=len(parts), u=2, i=2)
+            copy(engine, dst, frm[:, c])
 
         def h1_empty_pass(parts, c, engine):
             bank, n = turned[h1_key(parts)]
@@ -398,44 +399,17 @@ def tile_two_step_rnn_fp4_s3_kernel(tc, x1, x2, h0, gain, w_bytes, w_scale, u_wo
             nc.sync.dma_start(out=gain_row[:].rearrange("p j n -> p (j n)"), in_=gain.partition_broadcast(P))
 
         gain_col = keep_tile([P, NJ, 4], BF16, "gain_col")
-        nc.scalar.dma_start(out=gain_col[:], in_=gain.rearrange("(g p t) -> p g t", p=P, t=4))
         w_sc = keep_tile([P, NX, 4], F32, "w_sc")
-        nc.scalar.dma_start(out=w_sc[:], in_=w_scale.rearrange("(g p t) o -> p g (t o)", p=P, t=4))
         zeros = keep_tile([P, N], BF16, "zeros")
-        nc.vector.memset(zeros[:].bitcast(I32), 0)
         table = keep_tile([P, 16], F32, "table")
-        nc.vector.memset(table[:], 0.0)
-        nc.scalar.activation(out=table[:, 0:1], in_=table[:, 8:9], func=TANH)
         ident = keep_tile([P, P], F32, "ident")
-        make_identity(nc, ident[:])
-        zero_u_scales(0, 1)
-        zero_u_scales(1, 2)
-        zero_u_scales(2, 3)
         ident_bf = keep_tile([P, P], BF16, "ident_bf")
-        nc.vector.tensor_copy(out=ident_bf[:], in_=ident[:])
-        load_w(0, 0, 1)
-        load_h0(0)
-        load_h0(1)
-        load_h0(2)
-        load_u(0)
-        load_u_scales(0, 1)
-        load_w(1, 0, 1)
-        load_h0(3)
-        load_x(1, 0, 1)
-        load_x(1, 1, 2)
-        load_x(1, 2, 3)
-        load_x(1, 3, 4)
-        load_u(1)
-        load_u_scales(1, 2)
-        load_w(0, 1, 2)
-        load_w(1, 1, 2)
-        load_w(0, 2, 3)
-        load_w(1, 2, 3)
-        load_u(2)
-        load_u_scales(2, 3)
-        load_x(2, 0, 1)
-        load_x(2, 1, 2)
-        load_x2_half(1)
+
+        def load_gain(queue=nc.sync):
+            queue.dma_start(out=gain_col[:], in_=gain.rearrange("(g p t) -> p g t", p=P, t=4))
+
+        def load_w_scale(queue=nc.sync):
+            queue.dma_start(out=w_sc[:], in_=w_scale.rearrange("(g p t) o -> p g (t o)", p=P, t=4))
 
         first = [[(b, 0), (b, 1)] for b in range(NB)]
         last = [[(0, 2), (1, 2)], [(2, 2), (3, 2)]]
@@ -450,11 +424,74 @@ def tile_two_step_rnn_fp4_s3_kernel(tc, x1, x2, h0, gain, w_bytes, w_scale, u_wo
             h0_quant(first[b])
             h0_quant([(b, 2)])
 
-
         def warm_up(count, i=1):
             bank = bank_tile(i)
             for c in range(count):
                 nc.tensor.matmul(bank[:], lhsT=zeros[:, 0:P], rhs=zeros[:], start=True, stop=True)
+
+        def head(b, j, i):
+            open_group(2, b, j, i)
+            w_pass(2, b, j, 0, start=True)
+            w_pass(2, b, j, 1)
+
+        def piece_head(key, i, c0, c1):
+            open_group(2, *key, i)
+            w_pass(2, *key, 0, start=True, c0=c0, c1=c1)
+            w_pass(2, *key, 1, c0=c0, c1=c1)
+            return acc[(2,) + key]
+
+        def piece_close(key, bank, c0, c1):
+            acc[(2,) + key] = bank
+            for g in range(NJ):
+                u_pass(2, *key, g, stop=g == NJ - 1, c0=c0, c1=c1)
+            finish(2, *key, c0, c1)
+
+        def close(b, j):
+            u_pass(2, b, j, 2, stop=True)
+            finish(2, b, j)
+
+        def group2(b, j, i, c0=0, c1=N):
+            open_group(2, b, j, i)
+            w_pass(2, b, j, 0, start=True, c0=c0, c1=c1)
+            w_pass(2, b, j, 1, c0=c0, c1=c1)
+            for g in range(NJ):
+                u_pass(2, b, j, g, stop=g == NJ - 1, c0=c0, c1=c1)
+            finish(2, b, j, c0, c1)
+
+        load_gain(nc.scalar)
+        load_w_scale(nc.scalar)
+        nc.vector.memset(zeros[:].bitcast(I32), 0)
+        zero_u_scales(0, 1)
+        nc.vector.memset(table[:], 0.0)
+        nc.scalar.activation(out=table[:, 0:1], in_=table[:, 8:9], func=TANH)
+        make_identity(nc, ident[:])
+        zero_u_scales(1, 2)
+        zero_u_scales(2, 3)
+        nc.vector.tensor_copy(out=ident_bf[:], in_=ident[:])
+        load_w(0, 0, 1)
+        load_h0(0)
+        load_h0(1)
+        load_h0(2)
+        load_u_scales(0, 1)
+        load_u_by_pass(0)
+        load_w(1, 0, 1, 0, 2)
+        load_h0(3)
+        load_x(1, 0, 1)
+        load_x(1, 1, 2)
+        load_w(1, 0, 1, 2, 4)
+        load_x(1, 2, 3)
+        load_x(1, 3, 4)
+        load_u(1)
+        load_u_scales(1, 2)
+        load_w(0, 1, 2)
+        load_w(1, 1, 2)
+        load_w(0, 2, 3)
+        load_w(1, 2, 3)
+        load_u(2)
+        load_u_scales(2, 3)
+        load_x(2, 0, 1)
+        load_x(2, 1, 2)
+        load_x2_half(1)
 
         warm_up(2)
         spread_gain(0, 0, "scalar")
@@ -466,7 +503,6 @@ def tile_two_step_rnn_fp4_s3_kernel(tc, x1, x2, h0, gain, w_bytes, w_scale, u_wo
         h0_turns(1, 4, 5)
         warm_up(1)
         h0_turns(2, 2, 3)
-        warm_up(1)
         h0_ready(0)
         h0_ready(1)
         h0_ready(2)
@@ -474,28 +510,28 @@ def tile_two_step_rnn_fp4_s3_kernel(tc, x1, x2, h0, gain, w_bytes, w_scale, u_wo
         u_group(1, 0, 1)
         h0_turns(3, 4, 5)
         u_group(2, 0, 2)
-        w_widen(0, 1, (0, 1, 2), "scalar")
-        w_widen(0, 1, (3,), "vector")
         w_quant(0, 0)
+        w_widen(0, 1, (0, 1), "scalar")
         x_sort(1, 0, "scalar")
         x_sort(1, 1, "scalar")
-        w_weave(0, 1, "scalar", 0, N // 2)
+        w_widen(0, 1, (2,), "scalar")
         h0_empty([(3, 2)])
         h0_empty(first[3])
         h0_quant([(3, 2)])
+        w_widen(0, 1, (3,), "vector")
         h0_quant(first[3])
-        w_weave(0, 1, "vector", N // 2, N)
         x_turn(1, 0, 6)
         x_turn(1, 1, 7)
         x_turn(1, 2, 3)
         x_turn(1, 3, 5)
         for b in range(NB):
             x_empty(1, b, "scalar")
+        w_weave(0, 1)
         x_quant(1, 0)
         w_quant(0, 1)
         x_quant(1, 1)
-        w_widen(1, 0, (0, 1), "vector")
         x_quant(1, 2)
+        w_widen(1, 0, (0, 1), "scalar")
         w_widen(1, 0, (2, 3), "vector")
         x_quant(1, 3)
         w_weave(1, 0)
@@ -506,8 +542,8 @@ def tile_two_step_rnn_fp4_s3_kernel(tc, x1, x2, h0, gain, w_bytes, w_scale, u_wo
         w_widen(1, 1, (3,), "vector")
         w_quant(1, 0)
         w_weave(1, 1)
-        w_widen(2, 0, (0, 1), "scalar")
-        w_widen(2, 0, (2, 3), "vector")
+        w_widen(2, 0, (0,), "scalar")
+        w_widen(2, 0, (1, 2, 3), "vector")
         w_quant(1, 1)
         w_weave(2, 0)
         for b in range(NB):
@@ -520,8 +556,7 @@ def tile_two_step_rnn_fp4_s3_kernel(tc, x1, x2, h0, gain, w_bytes, w_scale, u_wo
         u_group(1, 2, 1)
         finish(1, 2, 0)
         finish(1, 3, 0)
-        w_widen(2, 1, (0, 1, 2), "scalar")
-        w_widen(2, 1, (3,), "vector")
+        w_widen(2, 1, range(4), "scalar")
         x_sort(2, 0, "scalar")
         x_sort(2, 1, "scalar")
         u_group(2, 2, 2)
@@ -542,107 +577,95 @@ def tile_two_step_rnn_fp4_s3_kernel(tc, x1, x2, h0, gain, w_bytes, w_scale, u_wo
         finish(1, 3, 1)
         x_empty(2, 0, "scalar")
         x_empty(2, 1, "scalar")
+        x2_sort(2, "scalar")
         h1_scale(0, 1)
-        h1_scale(1, 0)
+        rows = [[(b, j) for j in range(NJ)] for b in range(NB)]
+        late_scale(first[1], 0, 1)
         x_quant(2, 0)
-        h1_scale(1, 1)
+        late_scale(first[1], 1, 2)
+        late_park(first[1], 0)
+        late_scale(rows[2], 0, 1)
         x_quant(2, 1)
         for b in range(NB):
             w_pass(1, b, 2, 1, stop=True)
         for b in range(NB):
-            finish(1, b, 2, later=b >= 2)
+            finish(1, b, 2, later=True)
+        late_fetch(first[1], 0)
+        store(1, 0, 2)
         h1_scale(0, 2)
         h1_scale(1, 2)
-
-        def head(b, j, i):
-            open_group(2, b, j, i)
-            w_pass(2, b, j, 0, start=True)
-            w_pass(2, b, j, 1)
-
-        def close(b, j):
-            u_pass(2, b, j, 2, stop=True)
-            finish(2, b, j)
-
-        def group2(b, j, i, c0=0, c1=N):
-            open_group(2, b, j, i)
-            w_pass(2, b, j, 0, start=True, c0=c0, c1=c1)
-            w_pass(2, b, j, 1, c0=c0, c1=c1)
-            for g in range(NJ):
-                u_pass(2, b, j, g, stop=g == NJ - 1, c0=c0, c1=c1)
-            finish(2, b, j, c0, c1)
-
-        early = [(0, 0), (0, 1), (0, 2), (1, 0), (1, 1)]
+        late_scale(rows[2], 1, 3)
+        late_park(rows[2], 2)
+        store(1, 1, 2)
         for j, i in enumerate((3, 5, 6)):
             head(0, j, i)
-        h1_turn(first[0], 0)
-        h1_turn(first[1], 1)
-        h1_turn(last[0], 2)
-        head(1, 0, 7)
-        head(1, 1, 4)
+        h1_turn(first[0], 7)
+        h1_turn(last[0], 0)
+        for j, i in enumerate((1, 2, 4)):
+            head(1, j, i)
         h1_empty_pass(first[0], 0, "scalar")
         h1_empty_pass(first[0], 1, "scalar")
-        h1_empty(first[1], "scalar")
         h1_empty(last[0], "scalar")
-        x2_sort(2, "scalar")
         x2_sort(3, "scalar")
-        late_scale(first[2])
-        late_park(first[2], 0)
+        late_scale(rows[3], 0, 1)
         h1_quant_pass(first[0], 0)
-        late_scale(first[3], 0, 1, (0,))
         h1_quant_pass(first[0], 1)
-        late_scale(first[3], 0, 1, (1,))
-        h1_quant(first[1])
-        late_scale(first[3], 1, 2)
-        late_park(first[3], 2)
-        late_fetch(first[2], 0)
-        store(1, 2, 2)
-        store(1, 3, 2)
-        late_fetch(first[3], 2)
-        h1_quant(last[0])
         x2_turn(2)
         x2_pair(2, "scalar")
-        h1_scale(2, 2)
-        h1_scale(3, 2)
+        h1_quant(last[0])
+        late_scale(rows[3], 1, 2)
+        late_scale(rows[3], 2, 3)
         x_quant(2, 2)
-        for g in range(2):
+        late_fetch(rows[2], 2)
+        late_park(rows[3], 6)
+        store(1, 2, 2)
+        late_turn(first[1])
+        for g in range(NJ):
             for j in range(NJ):
-                u_pass(2, 0, j, g)
-        for b, j in early[3:]:
-            u_pass(2, b, j, 0)
-            u_pass(2, b, j, 1)
-        for b, j in early[:3]:
-            close(b, j)
-        for b, j in early[3:]:
-            u_pass(2, b, j, 2, stop=True)
-        head(1, 2, 0)
-        h1_turn(last[1], 1)
-        late_turn(first[2])
-        h1_empty(last[1], "scalar")
-        late_pair(first[2], "scalar")
+                u_pass(2, 0, j, g, stop=g == NJ - 1)
+        finish(2, 0, 0, later=True)
+        for c in range(2):
+            late_pair(first[1], c, "scalar")
         x2_turn(3)
-        h1_quant(last[1])
-        h1_quant(first[2])
-        finish(2, 1, 0)
+        for c in range(2):
+            h1_quant_pass(first[1], c)
+        late_fetch(rows[3], 6)
+        store(1, 3, 2)
+        store(2, 0, 0)
+        finish(2, 0, 1)
         x2_pair(3, "scalar")
-        finish(2, 1, 1)
-        late_turn(first[3])
-        u_pass(2, 1, 2, 0)
-        u_pass(2, 1, 2, 1)
-        close(1, 2)
-        x_quant(2, 3)
-        late_pair(first[3], "vector")
-        h1_quant(first[3])
-        for j, i in enumerate((2, 3, 5)):
+        finish(2, 0, 2)
+        for j, i in enumerate((7, 0, 3)):
             head(2, j, i)
+        late_turn(rows[2])
+        x_quant(2, 3)
+        for g in (2, 0, 1):
+            for j in range(NJ):
+                u_pass(2, 1, j, g, stop=g == 1)
+        late_pair(rows[2], 0, "vector")
+        late_pair(rows[2], 1, "vector")
+        late_pair(rows[2], 2, "scalar")
+        for c in range(NJ):
+            h1_quant_pass(rows[2], c)
+        late_turn(rows[3])
+        finish(2, 1, 0)
+        finish(2, 1, 1)
+        finish(2, 1, 2)
+        pieces = [((3, 0), 5, 0, 512), ((3, 1), 6, 0, 256), ((3, 1), 1, 256, 512)]
+        banks = [piece_head(*pieces[0])]
         for j in range(NJ):
-            u_pass(2, 2, j, 2)
-        for j in range(NJ):
-            u_pass(2, 2, j, 0)
-            u_pass(2, 2, j, 1, stop=True)
-            finish(2, 2, j)
-        group2(3, 0, 6)
-        group2(3, 1, 7, 0, 256)
-        group2(3, 1, 4, 256, 512)
-        group2(3, 2, 1, 0, 256)
-        group2(3, 2, 0, 256, 384)
-        group2(3, 2, 2, 384, 512)
+            for g in range(NJ):
+                u_pass(2, 2, j, g, stop=g == NJ - 1)
+        finish(2, 2, 0)
+        for c in range(NJ):
+            late_pair(rows[3], c, "vector")
+        for c in range(NJ):
+            h1_quant_pass(rows[3], c)
+        finish(2, 2, 1)
+        finish(2, 2, 2)
+        banks.extend([piece_head(*piece) for piece in pieces[1:]])
+        for (key, i, c0, c1), bank in zip(pieces, banks):
+            piece_close(key, bank, c0, c1)
+        group2(3, 2, 2, 0, 256)
+        group2(3, 2, 4, 256, 384)
+        group2(3, 2, 7, 384, 512)

@@ -343,7 +343,7 @@ def tile_two_step_rnn_fp4_s3_kernel(tc, x1, x2, h0, gain, w_bytes, w_scale, u_wo
             key = h1_key(parts)
             n = len(parts)
             if key not in scaled:
-                scaled[key] = work.tile([P, N * n], BF16, tag="late", name="late", align_bytes=ALIGN, bufs=3)
+                scaled[key] = work.tile([P, N * n], BF16, tag="late", name="late", align_bytes=ALIGN, bufs=4)
             for c in range(c0, n if c1 is None else c1):
                 b, j = parts[c]
                 dst = scaled[key][:].rearrange("p (a s u w e) -> p s u a w e", a=4, s=n, u=2, e=2)[:, c]
@@ -358,7 +358,7 @@ def tile_two_step_rnn_fp4_s3_kernel(tc, x1, x2, h0, gain, w_bytes, w_scale, u_wo
 
         def late_fetch(parts, slot):
             key = h1_key(parts)
-            back[key] = work.tile([P, N * len(parts)], BF16, tag="back", name="back", align_bytes=ALIGN, bufs=2)
+            back[key] = work.tile([P, N * len(parts)], BF16, tag="back", name="back", align_bytes=ALIGN, bufs=3)
             nc.sync.dma_start(out=back[key][:], in_=park_area(parts, slot).rearrange("a (i r) x -> (a i) (r x)", r=4))
 
         def late_turn(parts):
@@ -472,13 +472,12 @@ def tile_two_step_rnn_fp4_s3_kernel(tc, x1, x2, h0, gain, w_bytes, w_scale, u_wo
         load_h0(0)
         load_h0(1)
         load_h0(2)
+        load_u(0)
         load_u_scales(0, 1)
-        load_u_by_pass(0)
-        load_w(1, 0, 1, 0, 2)
+        load_w(1, 0, 1)
         load_h0(3)
         load_x(1, 0, 1)
         load_x(1, 1, 2)
-        load_w(1, 0, 1, 2, 4)
         load_x(1, 2, 3)
         load_x(1, 3, 4)
         load_u(1)
@@ -503,6 +502,7 @@ def tile_two_step_rnn_fp4_s3_kernel(tc, x1, x2, h0, gain, w_bytes, w_scale, u_wo
         h0_turns(1, 4, 5)
         warm_up(1)
         h0_turns(2, 2, 3)
+        warm_up(1)
         h0_ready(0)
         h0_ready(1)
         h0_ready(2)
@@ -510,28 +510,28 @@ def tile_two_step_rnn_fp4_s3_kernel(tc, x1, x2, h0, gain, w_bytes, w_scale, u_wo
         u_group(1, 0, 1)
         h0_turns(3, 4, 5)
         u_group(2, 0, 2)
+        w_widen(0, 1, (0, 1, 2), "scalar")
+        w_widen(0, 1, (3,), "vector")
         w_quant(0, 0)
-        w_widen(0, 1, (0, 1), "scalar")
         x_sort(1, 0, "scalar")
         x_sort(1, 1, "scalar")
-        w_widen(0, 1, (2,), "scalar")
+        w_weave(0, 1, "scalar", 0, N // 2)
         h0_empty([(3, 2)])
         h0_empty(first[3])
         h0_quant([(3, 2)])
-        w_widen(0, 1, (3,), "vector")
         h0_quant(first[3])
+        w_weave(0, 1, "vector", N // 2, N)
         x_turn(1, 0, 6)
         x_turn(1, 1, 7)
         x_turn(1, 2, 3)
         x_turn(1, 3, 5)
         for b in range(NB):
             x_empty(1, b, "scalar")
-        w_weave(0, 1)
         x_quant(1, 0)
         w_quant(0, 1)
         x_quant(1, 1)
+        w_widen(1, 0, (0, 1), "vector")
         x_quant(1, 2)
-        w_widen(1, 0, (0, 1), "scalar")
         w_widen(1, 0, (2, 3), "vector")
         x_quant(1, 3)
         w_weave(1, 0)
@@ -542,8 +542,8 @@ def tile_two_step_rnn_fp4_s3_kernel(tc, x1, x2, h0, gain, w_bytes, w_scale, u_wo
         w_widen(1, 1, (3,), "vector")
         w_quant(1, 0)
         w_weave(1, 1)
-        w_widen(2, 0, (0,), "scalar")
-        w_widen(2, 0, (1, 2, 3), "vector")
+        w_widen(2, 0, (0, 1), "scalar")
+        w_widen(2, 0, (2, 3), "vector")
         w_quant(1, 1)
         w_weave(2, 0)
         for b in range(NB):
@@ -556,7 +556,8 @@ def tile_two_step_rnn_fp4_s3_kernel(tc, x1, x2, h0, gain, w_bytes, w_scale, u_wo
         u_group(1, 2, 1)
         finish(1, 2, 0)
         finish(1, 3, 0)
-        w_widen(2, 1, range(4), "scalar")
+        w_widen(2, 1, (0, 1, 2), "scalar")
+        w_widen(2, 1, (3,), "vector")
         x_sort(2, 0, "scalar")
         x_sort(2, 1, "scalar")
         u_group(2, 2, 2)
@@ -579,23 +580,24 @@ def tile_two_step_rnn_fp4_s3_kernel(tc, x1, x2, h0, gain, w_bytes, w_scale, u_wo
         x_empty(2, 1, "scalar")
         x2_sort(2, "scalar")
         h1_scale(0, 1)
-        rows = [[(b, j) for j in range(NJ)] for b in range(NB)]
-        late_scale(first[1], 0, 1)
+        pair_a, pair_b, pair_c, pair_d = first[1], first[2], last[1], first[3]
+        late_scale(pair_a, 0, 1)
         x_quant(2, 0)
-        late_scale(first[1], 1, 2)
-        late_park(first[1], 0)
-        late_scale(rows[2], 0, 1)
+        late_scale(pair_a, 1, 2)
+        late_park(pair_a, 4)
+        late_scale(pair_b, 0, 1)
         x_quant(2, 1)
         for b in range(NB):
             w_pass(1, b, 2, 1, stop=True)
         for b in range(NB):
-            finish(1, b, 2, later=True)
-        late_fetch(first[1], 0)
-        store(1, 0, 2)
+            finish(1, b, 2, later=b >= 1)
         h1_scale(0, 2)
         h1_scale(1, 2)
-        late_scale(rows[2], 1, 3)
-        late_park(rows[2], 2)
+        late_scale(pair_b, 1, 2)
+        late_park(pair_b, 6)
+        late_fetch(pair_a, 4)
+        late_scale(pair_c)
+        late_park(pair_c, 8)
         store(1, 1, 2)
         for j, i in enumerate((3, 5, 6)):
             head(0, j, i)
@@ -607,60 +609,62 @@ def tile_two_step_rnn_fp4_s3_kernel(tc, x1, x2, h0, gain, w_bytes, w_scale, u_wo
         h1_empty_pass(first[0], 1, "scalar")
         h1_empty(last[0], "scalar")
         x2_sort(3, "scalar")
-        late_scale(rows[3], 0, 1)
         h1_quant_pass(first[0], 0)
         h1_quant_pass(first[0], 1)
         x2_turn(2)
         x2_pair(2, "scalar")
         h1_quant(last[0])
-        late_scale(rows[3], 1, 2)
-        late_scale(rows[3], 2, 3)
+        late_scale(pair_d)
         x_quant(2, 2)
-        late_fetch(rows[2], 2)
-        late_park(rows[3], 6)
+        late_fetch(pair_b, 6)
+        late_park(pair_d, 10)
+        late_fetch(pair_c, 8)
         store(1, 2, 2)
-        late_turn(first[1])
+        store(1, 3, 2)
+        late_turn(pair_a)
         for g in range(NJ):
             for j in range(NJ):
                 u_pass(2, 0, j, g, stop=g == NJ - 1)
-        finish(2, 0, 0, later=True)
+        finish(2, 0, 0)
         for c in range(2):
-            late_pair(first[1], c, "scalar")
+            late_pair(pair_a, c, "scalar")
         x2_turn(3)
         for c in range(2):
-            h1_quant_pass(first[1], c)
-        late_fetch(rows[3], 6)
-        store(1, 3, 2)
-        store(2, 0, 0)
+            h1_quant_pass(pair_a, c)
+        late_fetch(pair_d, 10)
         finish(2, 0, 1)
         x2_pair(3, "scalar")
         finish(2, 0, 2)
         for j, i in enumerate((7, 0, 3)):
             head(2, j, i)
-        late_turn(rows[2])
+        late_turn(pair_b)
         x_quant(2, 3)
         for g in (2, 0, 1):
             for j in range(NJ):
                 u_pass(2, 1, j, g, stop=g == 1)
-        late_pair(rows[2], 0, "vector")
-        late_pair(rows[2], 1, "vector")
-        late_pair(rows[2], 2, "scalar")
-        for c in range(NJ):
-            h1_quant_pass(rows[2], c)
-        late_turn(rows[3])
+        for c in range(2):
+            late_pair(pair_b, c, "scalar")
+        late_turn(pair_c)
+        for c in range(2):
+            h1_quant_pass(pair_b, c)
+        for c in range(2):
+            late_pair(pair_c, c, "scalar")
+        for c in range(2):
+            h1_quant_pass(pair_c, c)
+        late_turn(pair_d)
         finish(2, 1, 0)
         finish(2, 1, 1)
         finish(2, 1, 2)
         pieces = [((3, 0), 5, 0, 512), ((3, 1), 6, 0, 256), ((3, 1), 1, 256, 512)]
         banks = [piece_head(*pieces[0])]
-        for j in range(NJ):
-            for g in range(NJ):
+        for g in range(NJ):
+            for j in range(NJ):
                 u_pass(2, 2, j, g, stop=g == NJ - 1)
         finish(2, 2, 0)
-        for c in range(NJ):
-            late_pair(rows[3], c, "vector")
-        for c in range(NJ):
-            h1_quant_pass(rows[3], c)
+        for c in range(2):
+            late_pair(pair_d, c, "vector")
+        for c in range(2):
+            h1_quant_pass(pair_d, c)
         finish(2, 2, 1)
         finish(2, 2, 2)
         banks.extend([piece_head(*piece) for piece in pieces[1:]])

@@ -339,7 +339,7 @@ def tile_two_step_rnn_fp4_s3_kernel(tc, x1, x2, h0, gain, w_bytes, w_scale, u_wo
             n = len(parts)
             return parked[slot * N * P : (slot + n) * N * P].rearrange("(a m x) -> a m x", a=4, m=P)
 
-        def late_scale(parts, c0=0, c1=None, us=(0, 1)):
+        def late_scale(parts, c0=0, c1=None):
             key = h1_key(parts)
             n = len(parts)
             if key not in scaled:
@@ -349,8 +349,7 @@ def tile_two_step_rnn_fp4_s3_kernel(tc, x1, x2, h0, gain, w_bytes, w_scale, u_wo
                 dst = scaled[key][:].rearrange("p (a s u w e) -> p s u a w e", a=4, s=n, u=2, e=2)[:, c]
                 frm = h_sb[1, b, j][:].rearrange("p (a w u e) -> p u a w e", a=4, u=2, e=2)
                 by = gain_row[:, j, :].rearrange("p (u a w e) -> p u a w e", a=4, u=2, e=2)
-                for u in us:
-                    nc.vector.tensor_tensor(out=dst[:, u], in0=frm[:, u], in1=by[:, u], op=MULT)
+                nc.vector.tensor_tensor(out=dst, in0=frm, in1=by, op=MULT)
 
         def late_park(parts, slot):
             words = scaled[h1_key(parts)][:].rearrange("p (a x) -> p a x", a=4)
@@ -372,6 +371,14 @@ def tile_two_step_rnn_fp4_s3_kernel(tc, x1, x2, h0, gain, w_bytes, w_scale, u_wo
             dst = grouped[key][:].bitcast(F32).rearrange("p (c i r u) -> p c r u i", i=2, r=4, u=2)
             frm = h1_blocks[h1_key(parts)][:].rearrange("p (r s u c i) -> p s c r u i", r=4, s=len(parts), u=2, i=2)
             copy(engine, dst, frm[:, c])
+
+        def late_pair_both(parts, engine):
+            key = h1_key(parts)
+            grouped[key] = work.tile([P, 2 * N], BF16, tag="grouped", name="grouped", align_bytes=ALIGN, bufs=10)
+            frm = h1_blocks[key][:].rearrange("p (r s u c i) -> p s c r u i", r=4, s=2, u=2, i=2)
+            for c in range(2):
+                dst = grouped[key][:, N * c : N * c + N].bitcast(F32).rearrange("p (c i r u) -> p c r u i", i=2, r=4, u=2)
+                copy(engine, dst, frm[:, c])
 
         def h1_empty_pass(parts, c, engine):
             bank, n = turned[h1_key(parts)]
@@ -442,8 +449,8 @@ def tile_two_step_rnn_fp4_s3_kernel(tc, x1, x2, h0, gain, w_bytes, w_scale, u_wo
 
         def piece_close(key, bank, c0, c1):
             acc[(2,) + key] = bank
-            for g in range(NJ):
-                u_pass(2, *key, g, stop=g == NJ - 1, c0=c0, c1=c1)
+            for g in (2, 0, 1):
+                u_pass(2, *key, g, stop=g == 1, c0=c0, c1=c1)
             finish(2, *key, c0, c1)
 
         def close(b, j):
@@ -472,12 +479,13 @@ def tile_two_step_rnn_fp4_s3_kernel(tc, x1, x2, h0, gain, w_bytes, w_scale, u_wo
         load_h0(0)
         load_h0(1)
         load_h0(2)
-        load_u(0)
         load_u_scales(0, 1)
-        load_w(1, 0, 1)
+        load_u_by_pass(0)
+        load_w(1, 0, 1, 0, 2)
         load_h0(3)
         load_x(1, 0, 1)
         load_x(1, 1, 2)
+        load_w(1, 0, 1, 2, 4)
         load_x(1, 2, 3)
         load_x(1, 3, 4)
         load_u(1)
@@ -502,7 +510,6 @@ def tile_two_step_rnn_fp4_s3_kernel(tc, x1, x2, h0, gain, w_bytes, w_scale, u_wo
         h0_turns(1, 4, 5)
         warm_up(1)
         h0_turns(2, 2, 3)
-        warm_up(1)
         h0_ready(0)
         h0_ready(1)
         h0_ready(2)
@@ -510,28 +517,28 @@ def tile_two_step_rnn_fp4_s3_kernel(tc, x1, x2, h0, gain, w_bytes, w_scale, u_wo
         u_group(1, 0, 1)
         h0_turns(3, 4, 5)
         u_group(2, 0, 2)
-        w_widen(0, 1, (0, 1, 2), "scalar")
-        w_widen(0, 1, (3,), "vector")
         w_quant(0, 0)
+        w_widen(0, 1, (0, 1), "scalar")
         x_sort(1, 0, "scalar")
         x_sort(1, 1, "scalar")
-        w_weave(0, 1, "scalar", 0, N // 2)
+        w_widen(0, 1, (2,), "scalar")
         h0_empty([(3, 2)])
         h0_empty(first[3])
         h0_quant([(3, 2)])
+        w_widen(0, 1, (3,), "vector")
         h0_quant(first[3])
-        w_weave(0, 1, "vector", N // 2, N)
         x_turn(1, 0, 6)
         x_turn(1, 1, 7)
         x_turn(1, 2, 3)
         x_turn(1, 3, 5)
         for b in range(NB):
             x_empty(1, b, "scalar")
+        w_weave(0, 1)
         x_quant(1, 0)
         w_quant(0, 1)
         x_quant(1, 1)
-        w_widen(1, 0, (0, 1), "vector")
         x_quant(1, 2)
+        w_widen(1, 0, (0, 1), "scalar")
         w_widen(1, 0, (2, 3), "vector")
         x_quant(1, 3)
         w_weave(1, 0)
@@ -542,8 +549,8 @@ def tile_two_step_rnn_fp4_s3_kernel(tc, x1, x2, h0, gain, w_bytes, w_scale, u_wo
         w_widen(1, 1, (3,), "vector")
         w_quant(1, 0)
         w_weave(1, 1)
-        w_widen(2, 0, (0, 1), "scalar")
-        w_widen(2, 0, (2, 3), "vector")
+        w_widen(2, 0, (0,), "scalar")
+        w_widen(2, 0, (1, 2, 3), "vector")
         w_quant(1, 1)
         w_weave(2, 0)
         for b in range(NB):
@@ -556,19 +563,19 @@ def tile_two_step_rnn_fp4_s3_kernel(tc, x1, x2, h0, gain, w_bytes, w_scale, u_wo
         u_group(1, 2, 1)
         finish(1, 2, 0)
         finish(1, 3, 0)
-        w_widen(2, 1, (0, 1, 2), "scalar")
-        w_widen(2, 1, (3,), "vector")
+        w_widen(2, 1, range(4), "scalar")
         x_sort(2, 0, "scalar")
         x_sort(2, 1, "scalar")
         u_group(2, 2, 2)
         u_group(3, 2, 4)
         for b in range(NB):
             w_close(b, 1)
+        h1_scale(0, 0)
         w_quant(2, 0)
         w_weave(2, 1)
         finish(1, 0, 1)
         finish(1, 1, 1)
-        h1_scale(0, 0)
+        h1_scale(1, 0)
         w_quant(2, 1)
         x_turn(2, 0, 6)
         x_turn(2, 1, 7)
@@ -580,82 +587,79 @@ def tile_two_step_rnn_fp4_s3_kernel(tc, x1, x2, h0, gain, w_bytes, w_scale, u_wo
         x_empty(2, 1, "scalar")
         x2_sort(2, "scalar")
         h1_scale(0, 1)
-        pair_a, pair_b, pair_c, pair_d = first[1], first[2], last[1], first[3]
-        late_scale(pair_a, 0, 1)
+        pair_b, pair_c, pair_d = first[2], last[1], first[3]
+        h1_scale(1, 1)
         x_quant(2, 0)
-        late_scale(pair_a, 1, 2)
-        late_park(pair_a, 4)
         late_scale(pair_b, 0, 1)
         x_quant(2, 1)
         for b in range(NB):
             w_pass(1, b, 2, 1, stop=True)
         for b in range(NB):
-            finish(1, b, 2, later=b >= 1)
+            finish(1, b, 2, later=b >= 2)
         h1_scale(0, 2)
         h1_scale(1, 2)
         late_scale(pair_b, 1, 2)
         late_park(pair_b, 6)
-        late_fetch(pair_a, 4)
-        late_scale(pair_c)
-        late_park(pair_c, 8)
-        store(1, 1, 2)
+        late_scale(pair_c, 0, 1)
         for j, i in enumerate((3, 5, 6)):
             head(0, j, i)
         h1_turn(first[0], 7)
-        h1_turn(last[0], 0)
-        for j, i in enumerate((1, 2, 4)):
-            head(1, j, i)
+        h1_turn(first[1], 0)
+        h1_turn(last[0], 1)
+        head(1, 0, 2)
+        head(1, 1, 4)
         h1_empty_pass(first[0], 0, "scalar")
         h1_empty_pass(first[0], 1, "scalar")
         h1_empty(last[0], "scalar")
+        h1_empty(first[1], "scalar")
         x2_sort(3, "scalar")
         h1_quant_pass(first[0], 0)
+        late_scale(pair_c, 1, 2)
+        late_park(pair_c, 8)
         h1_quant_pass(first[0], 1)
+        late_scale(pair_d, 0, 1)
+        h1_quant(last[0])
+        late_scale(pair_d, 1, 2)
+        h1_quant(first[1])
         x2_turn(2)
         x2_pair(2, "scalar")
-        h1_quant(last[0])
-        late_scale(pair_d)
-        x_quant(2, 2)
         late_fetch(pair_b, 6)
         late_park(pair_d, 10)
         late_fetch(pair_c, 8)
         store(1, 2, 2)
         store(1, 3, 2)
-        late_turn(pair_a)
         for g in range(NJ):
             for j in range(NJ):
                 u_pass(2, 0, j, g, stop=g == NJ - 1)
         finish(2, 0, 0)
-        for c in range(2):
-            late_pair(pair_a, c, "scalar")
         x2_turn(3)
-        for c in range(2):
-            h1_quant_pass(pair_a, c)
-        late_fetch(pair_d, 10)
         finish(2, 0, 1)
+        late_fetch(pair_d, 10)
         x2_pair(3, "scalar")
         finish(2, 0, 2)
-        for j, i in enumerate((7, 0, 3)):
-            head(2, j, i)
+        head(1, 2, 7)
+        x_quant(2, 2)
         late_turn(pair_b)
         x_quant(2, 3)
-        for g in (2, 0, 1):
-            for j in range(NJ):
-                u_pass(2, 1, j, g, stop=g == 1)
+        for j in range(NJ):
+            for g in range(NJ):
+                u_pass(2, 1, j, g, stop=g == NJ - 1)
         for c in range(2):
             late_pair(pair_b, c, "scalar")
         late_turn(pair_c)
         for c in range(2):
             h1_quant_pass(pair_b, c)
+        finish(2, 1, 0)
         for c in range(2):
             late_pair(pair_c, c, "scalar")
         for c in range(2):
             h1_quant_pass(pair_c, c)
         late_turn(pair_d)
-        finish(2, 1, 0)
         finish(2, 1, 1)
         finish(2, 1, 2)
-        pieces = [((3, 0), 5, 0, 512), ((3, 1), 6, 0, 256), ((3, 1), 1, 256, 512)]
+        for j, i in enumerate((0, 1, 3)):
+            head(2, j, i)
+        pieces = [((3, 0), 5, 0, 512), ((3, 1), 6, 0, 256), ((3, 1), 2, 256, 512)]
         banks = [piece_head(*pieces[0])]
         for g in range(NJ):
             for j in range(NJ):
@@ -670,6 +674,6 @@ def tile_two_step_rnn_fp4_s3_kernel(tc, x1, x2, h0, gain, w_bytes, w_scale, u_wo
         banks.extend([piece_head(*piece) for piece in pieces[1:]])
         for (key, i, c0, c1), bank in zip(pieces, banks):
             piece_close(key, bank, c0, c1)
-        group2(3, 2, 2, 0, 256)
-        group2(3, 2, 4, 256, 384)
-        group2(3, 2, 7, 384, 512)
+        group2(3, 2, 4, 0, 256)
+        group2(3, 2, 7, 256, 384)
+        group2(3, 2, 0, 384, 512)

@@ -479,13 +479,12 @@ def tile_two_step_rnn_fp4_s3_kernel(tc, x1, x2, h0, gain, w_bytes, w_scale, u_wo
         load_h0(0)
         load_h0(1)
         load_h0(2)
+        load_u(0)
         load_u_scales(0, 1)
-        load_u_by_pass(0)
-        load_w(1, 0, 1, 0, 2)
+        load_w(1, 0, 1)
         load_h0(3)
         load_x(1, 0, 1)
         load_x(1, 1, 2)
-        load_w(1, 0, 1, 2, 4)
         load_x(1, 2, 3)
         load_x(1, 3, 4)
         load_u(1)
@@ -510,6 +509,7 @@ def tile_two_step_rnn_fp4_s3_kernel(tc, x1, x2, h0, gain, w_bytes, w_scale, u_wo
         h0_turns(1, 4, 5)
         warm_up(1)
         h0_turns(2, 2, 3)
+        warm_up(1)
         h0_ready(0)
         h0_ready(1)
         h0_ready(2)
@@ -517,28 +517,28 @@ def tile_two_step_rnn_fp4_s3_kernel(tc, x1, x2, h0, gain, w_bytes, w_scale, u_wo
         u_group(1, 0, 1)
         h0_turns(3, 4, 5)
         u_group(2, 0, 2)
+        w_widen(0, 1, (0, 1, 2), "scalar")
+        w_widen(0, 1, (3,), "vector")
         w_quant(0, 0)
-        w_widen(0, 1, (0, 1), "scalar")
         x_sort(1, 0, "scalar")
         x_sort(1, 1, "scalar")
-        w_widen(0, 1, (2,), "scalar")
+        w_weave(0, 1, "scalar", 0, N // 2)
         h0_empty([(3, 2)])
         h0_empty(first[3])
         h0_quant([(3, 2)])
-        w_widen(0, 1, (3,), "vector")
         h0_quant(first[3])
+        w_weave(0, 1, "vector", N // 2, N)
         x_turn(1, 0, 6)
         x_turn(1, 1, 7)
         x_turn(1, 2, 3)
         x_turn(1, 3, 5)
         for b in range(NB):
             x_empty(1, b, "scalar")
-        w_weave(0, 1)
         x_quant(1, 0)
         w_quant(0, 1)
         x_quant(1, 1)
+        w_widen(1, 0, (0, 1), "vector")
         x_quant(1, 2)
-        w_widen(1, 0, (0, 1), "scalar")
         w_widen(1, 0, (2, 3), "vector")
         x_quant(1, 3)
         w_weave(1, 0)
@@ -549,8 +549,8 @@ def tile_two_step_rnn_fp4_s3_kernel(tc, x1, x2, h0, gain, w_bytes, w_scale, u_wo
         w_widen(1, 1, (3,), "vector")
         w_quant(1, 0)
         w_weave(1, 1)
-        w_widen(2, 0, (0,), "scalar")
-        w_widen(2, 0, (1, 2, 3), "vector")
+        w_widen(2, 0, (0, 1), "scalar")
+        w_widen(2, 0, (2, 3), "vector")
         w_quant(1, 1)
         w_weave(2, 0)
         for b in range(NB):
@@ -563,19 +563,19 @@ def tile_two_step_rnn_fp4_s3_kernel(tc, x1, x2, h0, gain, w_bytes, w_scale, u_wo
         u_group(1, 2, 1)
         finish(1, 2, 0)
         finish(1, 3, 0)
-        w_widen(2, 1, range(4), "scalar")
+        w_widen(2, 1, (0, 1, 2), "scalar")
+        w_widen(2, 1, (3,), "vector")
         x_sort(2, 0, "scalar")
         x_sort(2, 1, "scalar")
         u_group(2, 2, 2)
         u_group(3, 2, 4)
         for b in range(NB):
             w_close(b, 1)
-        h1_scale(0, 0)
         w_quant(2, 0)
         w_weave(2, 1)
         finish(1, 0, 1)
         finish(1, 1, 1)
-        h1_scale(1, 0)
+        h1_scale(0, 0)
         w_quant(2, 1)
         x_turn(2, 0, 6)
         x_turn(2, 1, 7)
@@ -585,17 +585,17 @@ def tile_two_step_rnn_fp4_s3_kernel(tc, x1, x2, h0, gain, w_bytes, w_scale, u_wo
         finish(1, 3, 1)
         x_empty(2, 0, "scalar")
         x_empty(2, 1, "scalar")
-        x2_sort(2, "scalar")
         h1_scale(0, 1)
         pair_b, pair_c, pair_d = first[2], last[1], first[3]
-        h1_scale(1, 1)
+        h1_scale(1, 0)
         x_quant(2, 0)
-        late_scale(pair_b, 0, 1)
+        h1_scale(1, 1)
         x_quant(2, 1)
+        late_scale(pair_b, 0, 1)
         for b in range(NB):
             w_pass(1, b, 2, 1, stop=True)
         for b in range(NB):
-            finish(1, b, 2, later=b >= 2)
+            finish(1, b, 2, later=b >= 3)
         h1_scale(0, 2)
         h1_scale(1, 2)
         late_scale(pair_b, 1, 2)
@@ -612,6 +612,7 @@ def tile_two_step_rnn_fp4_s3_kernel(tc, x1, x2, h0, gain, w_bytes, w_scale, u_wo
         h1_empty_pass(first[0], 1, "scalar")
         h1_empty(last[0], "scalar")
         h1_empty(first[1], "scalar")
+        x2_sort(2, "scalar")
         x2_sort(3, "scalar")
         h1_quant_pass(first[0], 0)
         late_scale(pair_c, 1, 2)
@@ -621,59 +622,63 @@ def tile_two_step_rnn_fp4_s3_kernel(tc, x1, x2, h0, gain, w_bytes, w_scale, u_wo
         h1_quant(last[0])
         late_scale(pair_d, 1, 2)
         h1_quant(first[1])
-        x2_turn(2)
-        x2_pair(2, "scalar")
         late_fetch(pair_b, 6)
         late_park(pair_d, 10)
         late_fetch(pair_c, 8)
-        store(1, 2, 2)
         store(1, 3, 2)
+        late_fetch(pair_d, 10)
+        x2_turn(2)
+        x2_pair(2, "scalar")
+        x2_turn(3)
+        x_quant(2, 2)
+        late_turn(pair_b)
         for g in range(NJ):
             for j in range(NJ):
                 u_pass(2, 0, j, g, stop=g == NJ - 1)
         finish(2, 0, 0)
-        x2_turn(3)
-        finish(2, 0, 1)
-        late_fetch(pair_d, 10)
         x2_pair(3, "scalar")
+        finish(2, 0, 1)
+        x_quant(2, 3)
+        for c in range(2):
+            late_pair(pair_b, c, "vector")
+        late_turn(pair_c)
+        for c in range(2):
+            h1_quant_pass(pair_b, c)
         finish(2, 0, 2)
         head(1, 2, 7)
-        x_quant(2, 2)
-        late_turn(pair_b)
-        x_quant(2, 3)
         for j in range(NJ):
             for g in range(NJ):
                 u_pass(2, 1, j, g, stop=g == NJ - 1)
         for c in range(2):
-            late_pair(pair_b, c, "scalar")
-        late_turn(pair_c)
-        for c in range(2):
-            h1_quant_pass(pair_b, c)
-        finish(2, 1, 0)
-        for c in range(2):
-            late_pair(pair_c, c, "scalar")
+            late_pair(pair_c, c, "vector")
         for c in range(2):
             h1_quant_pass(pair_c, c)
         late_turn(pair_d)
+        finish(2, 1, 0)
         finish(2, 1, 1)
         finish(2, 1, 2)
         for j, i in enumerate((0, 1, 3)):
             head(2, j, i)
         pieces = [((3, 0), 5, 0, 512), ((3, 1), 6, 0, 256), ((3, 1), 2, 256, 512)]
         banks = [piece_head(*pieces[0])]
+        u_pass(2, 2, 0, 0)
+        u_pass(2, 2, 0, 1)
+        u_pass(2, 2, 1, 0)
+        close(2, 0)
+        u_pass(2, 2, 1, 1)
+        close(2, 1)
         for g in range(NJ):
-            for j in range(NJ):
-                u_pass(2, 2, j, g, stop=g == NJ - 1)
-        finish(2, 2, 0)
+            u_pass(2, 2, 2, g, stop=g == NJ - 1)
+        finish(2, 2, 2)
         for c in range(2):
             late_pair(pair_d, c, "vector")
         for c in range(2):
             h1_quant_pass(pair_d, c)
-        finish(2, 2, 1)
-        finish(2, 2, 2)
-        banks.extend([piece_head(*piece) for piece in pieces[1:]])
+        banks.extend([piece_head(*piece) for piece in pieces[len(banks):2]])
         for (key, i, c0, c1), bank in zip(pieces, banks):
             piece_close(key, bank, c0, c1)
+        for key, i, c0, c1 in pieces[2:]:
+            group2(*key, i, c0, c1)
         group2(3, 2, 4, 0, 256)
         group2(3, 2, 7, 256, 384)
         group2(3, 2, 0, 384, 512)

@@ -600,6 +600,7 @@ def tile_two_step_rnn_fp4_s3_kernel(tc, x1, x2, h0, gain, w_bytes, w_scale, u_wo
         h1_scale(1, 2)
         late_scale(pair_b, 1, 2)
         late_park(pair_b, 6)
+        store(1, 3, 2)
         late_scale(pair_c, 0, 1)
         for j, i in enumerate((3, 5, 6)):
             head(0, j, i)
@@ -625,22 +626,21 @@ def tile_two_step_rnn_fp4_s3_kernel(tc, x1, x2, h0, gain, w_bytes, w_scale, u_wo
         late_fetch(pair_b, 6)
         late_park(pair_d, 10)
         late_fetch(pair_c, 8)
-        store(1, 3, 2)
-        late_fetch(pair_d, 10)
+        for g in range(NJ):
+            for j in range(NJ):
+                u_pass(2, 0, j, g, stop=g == NJ - 1)
+        finish(2, 0, 0)
         x2_turn(2)
         x2_pair(2, "scalar")
         x2_turn(3)
         x_quant(2, 2)
         late_turn(pair_b)
-        for g in range(NJ):
-            for j in range(NJ):
-                u_pass(2, 0, j, g, stop=g == NJ - 1)
-        finish(2, 0, 0)
-        x2_pair(3, "scalar")
         finish(2, 0, 1)
+        late_fetch(pair_d, 10)
+        x2_pair(3, "scalar")
         x_quant(2, 3)
         for c in range(2):
-            late_pair(pair_b, c, "vector")
+            late_pair(pair_b, c, "scalar")
         late_turn(pair_c)
         for c in range(2):
             h1_quant_pass(pair_b, c)
@@ -649,12 +649,12 @@ def tile_two_step_rnn_fp4_s3_kernel(tc, x1, x2, h0, gain, w_bytes, w_scale, u_wo
         for j in range(NJ):
             for g in range(NJ):
                 u_pass(2, 1, j, g, stop=g == NJ - 1)
+        finish(2, 1, 0)
         for c in range(2):
             late_pair(pair_c, c, "vector")
         for c in range(2):
             h1_quant_pass(pair_c, c)
         late_turn(pair_d)
-        finish(2, 1, 0)
         finish(2, 1, 1)
         finish(2, 1, 2)
         for j, i in enumerate((0, 1, 3)):

@@ -563,19 +563,19 @@ def tile_two_step_rnn_fp4_s3_kernel(tc, x1, x2, h0, gain, w_bytes, w_scale, u_wo
         u_group(1, 2, 1)
         finish(1, 2, 0)
         finish(1, 3, 0)
-        w_widen(2, 1, (0, 1, 2), "scalar")
-        w_widen(2, 1, (3,), "vector")
+        w_widen(2, 1, range(4), "scalar")
         x_sort(2, 0, "scalar")
         x_sort(2, 1, "scalar")
         u_group(2, 2, 2)
         u_group(3, 2, 4)
         for b in range(NB):
             w_close(b, 1)
+        h1_scale(0, 0)
         w_quant(2, 0)
         w_weave(2, 1)
         finish(1, 0, 1)
         finish(1, 1, 1)
-        h1_scale(0, 0)
+        h1_scale(1, 0)
         w_quant(2, 1)
         x_turn(2, 0, 6)
         x_turn(2, 1, 7)
@@ -587,7 +587,6 @@ def tile_two_step_rnn_fp4_s3_kernel(tc, x1, x2, h0, gain, w_bytes, w_scale, u_wo
         x_empty(2, 1, "scalar")
         h1_scale(0, 1)
         pair_b, pair_c, pair_d = first[2], last[1], first[3]
-        h1_scale(1, 0)
         x_quant(2, 0)
         h1_scale(1, 1)
         x_quant(2, 1)
@@ -674,10 +673,10 @@ def tile_two_step_rnn_fp4_s3_kernel(tc, x1, x2, h0, gain, w_bytes, w_scale, u_wo
             late_pair(pair_d, c, "vector")
         for c in range(2):
             h1_quant_pass(pair_d, c)
-        banks.extend([piece_head(*piece) for piece in pieces[len(banks):2]])
+        banks.extend([piece_head(*piece) for piece in pieces[len(banks):3]])
         for (key, i, c0, c1), bank in zip(pieces, banks):
             piece_close(key, bank, c0, c1)
-        for key, i, c0, c1 in pieces[2:]:
+        for key, i, c0, c1 in pieces[3:]:
             group2(*key, i, c0, c1)
         group2(3, 2, 4, 0, 256)
         group2(3, 2, 7, 256, 384)

@@ -308,9 +308,9 @@ def tile_two_step_rnn_fp4_s3_kernel(tc, x1, x2, h0, gain, w_bytes, w_scale, u_wo
         def h1_scale(b, j):
             scaled[b, j] = work.tile([P, N], BF16, tag="scaled", name="scaled", align_bytes=ALIGN, bufs=6)
             nc.vector.tensor_tensor(
-                out=scaled[b, j][:].rearrange("p (u w e) -> p u w e", u=2, e=2),
-                in0=h_sb[1, b, j][:].rearrange("p (w u e) -> p u w e", u=2, e=2),
-                in1=gain_row[:, j, :].rearrange("p (u w e) -> p u w e", u=2, e=2),
+                out=scaled[b, j][:].rearrange("p (u w e) -> p w u e", u=2, e=2),
+                in0=h_sb[1, b, j][:].rearrange("p (w u e) -> p w u e", u=2, e=2),
+                in1=gain_row[:, j, :].rearrange("p (u w e) -> p w u e", u=2, e=2),
                 op=MULT,
             )
 

from contextlib import ExitStack

import concourse.mybir as mybir
from concourse.masks import make_identity

B, D, H = 512, 1024, 1536
FLOPS = 2 * 2 * B * H * (D + H)

F32 = mybir.dt.float32
BF16 = mybir.dt.bfloat16
I32 = mybir.dt.int32
U32 = mybir.dt.uint32
U8 = mybir.dt.uint8
E4M3 = mybir.dt.float8_e4m3fn
E4M3X4 = mybir.dt.float8_e4m3fn_x4
E2M1X4 = mybir.dt.float4_e2m1fn_x4
MULT = mybir.AluOpType.mult
COPY = mybir.ActivationFunctionType.Copy
TANH = mybir.ActivationFunctionType.Tanh

P = 128
N = 512
NB = B // P
NJ = H // N
NX = D // N
ALIGN = 256


def tile_two_step_rnn_fp4_s3_kernel(tc, x1, x2, h0, gain, w_bytes, w_scale, u_words, u_scales, out_0, out_1):
    nc = tc.nc
    with ExitStack() as ctx:
        keep = ctx.enter_context(tc.tile_pool(name="keep", bufs=1))
        work = ctx.enter_context(tc.tile_pool(name="work", bufs=3))
        psum = ctx.enter_context(tc.psum_pool(name="psum", bufs=1))
        ctx.enter_context(tc.manual_schedule())

        def keep_tile(shape, dtype, name):
            return keep.tile(shape, dtype, name=name, align_bytes=ALIGN)

        def bank_tile(i):
            return psum.tile([P, N], F32, tag="bank%d" % i, name="bank%d" % i)

        def copy(engine, dst, frm):
            if engine == "scalar":
                nc.scalar.copy(out=dst, in_=frm)
            else:
                nc.vector.tensor_copy(out=dst, in_=frm)

        h0_raw, u_sb, u_planes, w_raw, x_raw = {}, {}, {}, {}, {}

        def load_h0(b):
            h0_raw[b] = keep_tile([P, H], BF16, "h0_%d" % b)
            nc.sync.dma_start(out=h0_raw[b][:], in_=h0[P * b : P * b + P, :])

        def load_u(j):
            t = keep_tile([P, NJ, 2 * N], U8, "u_%d" % j)
            u_sb[j] = [t[:, g, :] for g in range(NJ)]
            nc.sync.dma_start(
                out=t[:].bitcast(I32),
                in_=u_words[:, :, 2 * N * j : 2 * N * j + 2 * N].rearrange("g p n -> p g n").bitcast(I32),
            )

        def load_u_by_pass(j):
            u_sb[j] = [keep_tile([P, 2 * N], U8, "u_%d_%d" % (j, g)) for g in range(NJ)]
            for g in range(NJ):
                nc.sync.dma_start(
                    out=u_sb[j][g][:].bitcast(I32), in_=u_words[g, :, 2 * N * j : 2 * N * j + 2 * N].bitcast(I32)
                )

        def zero_u_scales(j0, j1):
            t = keep_tile([P, NJ, N * (j1 - j0)], U8, "us_%d" % j0)
            nc.vector.memset(t[:].rearrange("p g n -> p (g n)").bitcast(I32), 0)
            for j in range(j0, j1):
                u_planes[j] = (t, N * (j - j0))

        def load_u_scales(j0, j1, queue=nc.sync):
            t = u_planes[j0][0]
            for r in range(4):
                queue.dma_start(
                    out=t[r:P:32, :, :].bitcast(I32),
                    in_=u_scales[:, r:16:4, N * j0 : N * j1].rearrange("g q n -> q g n").bitcast(I32),
                )

        def load_w(g, j0, j1, t0=0, t1=4):
            t = keep_tile([P, t1 - t0, N * (j1 - j0)], U8, "w_bytes_%d_%d_%d" % (g, j0, t0))
            nc.sync.dma_start(
                out=t[:],
                in_=w_bytes[N * g : N * g + N, N * j0 : N * j1].rearrange("(p t) n -> p t n", t=4)[:, t0:t1, :],
            )
            for j in range(j0, j1):
                for r in range(t0, t1):
                    w_raw[j, g, r] = t[:, r - t0, N * (j - j0) : N * (j - j0) + N]

        def load_x(s, b0, b1):
            t = keep_tile([P, (b1 - b0) * D], BF16, "x%d_%d" % (s, b0))
            nc.sync.dma_start(
                out=t[:].rearrange("p (b k) -> p b k", k=D),
                in_=(x1 if s == 1 else x2)[P * b0 : P * b1, :].rearrange("(b p) k -> p b k", p=P),
            )
            for b in range(b0, b1):
                x_raw[s, b] = t[:, D * (b - b0) : D * (b - b0) + D]

        r_op, x_op, w_op = {}, {}, {}
        turned, grouped = {}, {}

        def quantise(key, width):
            codes = keep_tile([P, width // 4], U32, "c_" + key)
            scales = keep_tile([P, width // 4], U8, "s_" + key)
            nc.vector.quantize_mx(out=codes[:].bitcast(E4M3X4), scales=scales[:], in_=grouped[key][:])
            return codes, scales

        def turn(key, i, sources):
            bank = bank_tile(i)
            n = len(sources)
            for u in range(2):
                for c in range(n):
                    nc.tensor.transpose(bank[:, P * (n * u + c) : P * (n * u + c) + P], sources[c][u], ident[:])
            turned[key] = (bank, n)

        def every_second(raw, g):
            words = raw.bitcast(F32)
            return [words[:, 256 * g + u : 256 * g + 256 : 2] for u in range(2)]

        def h0_key(parts):
            return "h0_%d_%d" % parts[0]

        def h0_turn(parts, i):
            turn(h0_key(parts), i, [every_second(h0_raw[b][:], g) for b, g in parts])

        def h0_empty(parts):
            key = h0_key(parts)
            bank, n = turned[key]
            g0, g1 = parts[0][1], parts[-1][1] + 1
            grouped[key] = work.tile([P, N * n], BF16, tag="grouped", name="grouped", align_bytes=ALIGN, bufs=10)
            nc.vector.tensor_tensor(
                out=grouped[key][:].rearrange("p (c r u e) -> p c r u e", c=n, u=2, e=2),
                in0=bank[:, 0 : 2 * P * n].bitcast(BF16).rearrange("p (u c r e) -> p c r u e", u=2, c=n, e=2),
                in1=gain_col[:, g0:g1, :].rearrange("p g (u e) -> p g u e", e=2).unsqueeze(2).to_broadcast([P, n, P, 2, 2]),
                op=MULT,
            )

        gain_banks = {}

        def spread_gain(g, i, engine=None):
            rows = bank_tile(i)
            gain_banks[g] = rows
            for t in range(4):
                nc.tensor.matmul(
                    rows[:, P * t : P * t + P],
                    lhsT=gain_col[:, g, t : t + 1].to_broadcast([P, P]),
                    rhs=ident_bf[:],
                    start=True,
                    stop=True,
                )
            if engine:
                gain_empty(g, engine)

        def gain_empty(g, engine):
            rows = gain_banks[g]
            dst = gain_row[:, g, :].rearrange("p (u w e) -> p u w e", u=2, e=2)
            frm = rows[:].rearrange("p (u e w) -> p u w e", u=2, e=2)
            if engine == "scalar":
                nc.scalar.copy(out=dst, in_=frm)
            else:
                nc.vector.tensor_copy(out=dst, in_=frm)

        def h0_quant(parts):
            codes, scales = quantise(h0_key(parts), N * len(parts))
            for c, (b, g) in enumerate(parts):
                r_op[1, b, g] = (codes, scales, P * c)

        def empty(key, engine):
            bank, n = turned[key]
            grouped[key] = work.tile([P, N * n], BF16, tag="grouped", name="grouped", align_bytes=ALIGN, bufs=10)
            dst = grouped[key][:].bitcast(F32).rearrange("p (r u) -> p r u", u=2)
            frm = bank[:, 0 : 2 * P * n].rearrange("p (u r) -> p r u", u=2)
            if engine == "scalar":
                nc.scalar.copy(out=dst, in_=frm)
            else:
                nc.vector.tensor_copy(out=dst, in_=frm)

        x_sorted = {}

        def x_sort(s, b, engine):
            x_sorted[s, b] = work.tile([P, D], BF16, tag="sorted", name="sorted", align_bytes=ALIGN, bufs=4)
            dst = x_sorted[s, b][:].bitcast(F32).rearrange("p (u w) -> p u w", u=2)
            frm = x_raw[s, b].bitcast(F32).rearrange("p (w u) -> p u w", u=2)
            if engine == "scalar":
                nc.scalar.copy(out=dst, in_=frm)
            else:
                nc.vector.tensor_copy(out=dst, in_=frm)

        def x_turn(s, b, i):
            if (s, b) in x_sorted:
                words = x_sorted[s, b][:].bitcast(F32)
                sources = [[words[:, 256 * u + P * g : 256 * u + P * g + P] for u in range(2)] for g in range(NX)]
            else:
                sources = [every_second(x_raw[s, b], g) for g in range(NX)]
            turn("x%d_%d" % (s, b), i, sources)

        def x_empty(s, b, engine):
            empty("x%d_%d" % (s, b), engine)

        def x_quant(s, b):
            codes, scales = quantise("x%d_%d" % (s, b), D)
            for g in range(NX):
                x_op[s, b, g] = (codes, scales, P * g)

        x2_quads = {1: keep_tile([P, NX, 8, P], BF16, "x2_quads")}
        x2_blocks = {}

        def load_x2_half(half):
            rows = x2[256 * half : 256 * half + 256, :].rearrange("(r i) k -> i r k", i=32)
            for g in range(NX):
                for a in (0, 2, 1, 3):
                    nc.sync.dma_start(
                        out=x2_quads[half][32 * a : 32 * a + 32, g, :, :],
                        in_=rows[:, :, N * g + P * a : N * g + P * a + P],
                    )

        def x2_sort(b, engine):
            x_sorted[2, b] = work.tile([P, D], BF16, tag="sorted", name="sorted", align_bytes=ALIGN, bufs=4)
            dst = x_sorted[2, b][:].bitcast(F32).rearrange("p (g u w) -> p g u w", g=NX, u=2)
            frm = x2_quads[b // 2][:, :, 4 * (b % 2) : 4 * (b % 2) + 4, :].rearrange("p g r k -> p g (r k)").bitcast(F32)
            copy(engine, dst, frm.rearrange("p g (w u) -> p g u w", u=2))

        def x2_turn(b):
            x2_blocks[b] = work.tile([P, D // 2], F32, tag="blocks", name="blocks", align_bytes=ALIGN, bufs=3)
            nc.vector.transpose(x2_blocks[b][:], x_sorted[2, b][:].bitcast(F32))

        def x2_pair(b, engine):
            key = "x2_%d" % b
            grouped[key] = work.tile([P, D], BF16, tag="grouped", name="grouped", align_bytes=ALIGN, bufs=10)
            dst = grouped[key][:].bitcast(F32).rearrange("p (g r u) -> p g r u", g=NX, u=2)
            copy(engine, dst, x2_blocks[b][:].rearrange("p (g u r) -> p g r u", g=NX, u=2))

        wide = {}

        def w_widen(j, g, ts, engine):
            if (j, g) not in wide:
                wide[j, g] = work.tile([P, 4, N], BF16, tag="wide", name="wide", align_bytes=ALIGN, bufs=4)
            for t in ts:
                src = w_raw[j, g, t].bitcast(E4M3)
                if engine == "scalar":
                    nc.scalar.activation(out=wide[j, g][:, t, :], in_=src, func=COPY, scale=w_sc[:, g, t : t + 1])
                else:
                    nc.vector.tensor_scalar(
                        out=wide[j, g][:, t, :], in0=src, scalar1=w_sc[:, g, t : t + 1], scalar2=None, op0=MULT
                    )

        def w_weave(j, g, engine="vector", c0=0, c1=N):
            key = "w_%d_%d" % (j, g)
            if key not in grouped:
                grouped[key] = work.tile([P, 4 * N], BF16, tag="w_grp", name="w_grp", align_bytes=ALIGN)
            dst = grouped[key][:, 4 * c0 : 4 * c1].rearrange("p (c i t) -> p c t i", i=4, t=4)
            frm = wide[j, g][:, :, c0:c1].rearrange("p t (c i) -> p c t i", i=4)
            if engine == "scalar":
                nc.scalar.copy(out=dst, in_=frm)
            else:
                nc.vector.tensor_copy(out=dst, in_=frm)

        def w_quant(j, g):
            w_op[j, g] = quantise("w_%d_%d" % (j, g), 4 * N)

        acc = {}

        def open_group(s, b, j, i):
            acc[s, b, j] = bank_tile(i)

        def u_pass(s, b, j, g, start=False, stop=False, c0=0, c1=N):
            codes, scales, c = r_op[s, b, g]
            plane, p0 = u_planes[j]
            nc.tensor.matmul_mx(
                out=acc[s, b, j][:, 0 : c1 - c0],
                lhsT=codes[:, c : c + P].bitcast(E4M3X4),
                lhsT_scale=scales[:, c : c + P],
                rhs=u_sb[j][g][:, 2 * c0 : 2 * c1].bitcast(E2M1X4),
                rhs_scale=plane[:, g, p0 + c0 : p0 + c1],
                start=start,
                stop=stop,
            )

        def w_pass(s, b, j, g, start=False, stop=False, c0=0, c1=N):
            codes, scales, c = x_op[s, b, g]
            nc.tensor.matmul_mx(
                out=acc[s, b, j][:, 0 : c1 - c0],
                lhsT=codes[:, c : c + P].bitcast(E4M3X4),
                lhsT_scale=scales[:, c : c + P],
                rhs=w_op[j, g][0][:, c0:c1].bitcast(E4M3X4),
                rhs_scale=w_op[j, g][1][:, c0:c1],
                start=start,
                stop=stop,
            )

        h_sb, scaled = {}, {}

        def store(s, b, j, c0=0, c1=N):
            out = out_0 if s == 1 else out_1
            nc.sync.dma_start(out=out[P * b : P * b + P, N * j + c0 : N * j + c1], in_=h_sb[s, b, j][:, 0 : c1 - c0])

        def finish(s, b, j, c0=0, c1=N, later=False):
            h = work.tile([P, N], F32, tag="h", name="h", align_bytes=ALIGN, bufs=12)
            h_sb[s, b, j] = h
            nc.scalar.activation(out=h[:, 0 : c1 - c0], in_=acc[s, b, j][:, 0 : c1 - c0], func=TANH)
            if not later:
                store(s, b, j, c0, c1)

        def h1_scale(b, j):
            scaled[b, j] = work.tile([P, N], BF16, tag="scaled", name="scaled", align_bytes=ALIGN, bufs=6)
            nc.vector.tensor_tensor(
                out=scaled[b, j][:].rearrange("p (u w e) -> p w u e", u=2, e=2),
                in0=h_sb[1, b, j][:].rearrange("p (w u e) -> p w u e", u=2, e=2),
                in1=gain_row[:, j, :].rearrange("p (u w e) -> p w u e", u=2, e=2),
                op=MULT,
            )

        def h1_key(parts):
            return "h1_%d_%d" % parts[0]

        def h1_turn(parts, i):
            sources = []
            for b, j in parts:
                words = scaled[b, j][:].bitcast(F32)
                sources.append([words[:, P * u : P * u + P] for u in range(2)])
            turn(h1_key(parts), i, sources)

        def h1_empty(parts, engine):
            empty(h1_key(parts), engine)

        def h1_quant(parts):
            codes, scales = quantise(h1_key(parts), N * len(parts))
            for c, (b, j) in enumerate(parts):
                r_op[2, b, j] = (codes, scales, P * c)

        parked = out_1[2 * P : 4 * P, :].bitcast(BF16).rearrange("r n -> (r n)")
        back, h1_blocks = {}, {}

        def park_area(parts, slot):
            n = len(parts)
            return parked[slot * N * P : (slot + n) * N * P].rearrange("(a m x) -> a m x", a=4, m=P)

        def late_scale(parts, c0=0, c1=None):
            key = h1_key(parts)
            n = len(parts)
            if key not in scaled:
                scaled[key] = work.tile([P, N * n], BF16, tag="late", name="late", align_bytes=ALIGN, bufs=4)
            for c in range(c0, n if c1 is None else c1):
                b, j = parts[c]
                dst = scaled[key][:].rearrange("p (a s u w e) -> p s u a w e", a=4, s=n, u=2, e=2)[:, c]
                frm = h_sb[1, b, j][:].rearrange("p (a w u e) -> p u a w e", a=4, u=2, e=2)
                by = gain_row[:, j, :].rearrange("p (u a w e) -> p u a w e", a=4, u=2, e=2)
                nc.vector.tensor_tensor(out=dst, in0=frm, in1=by, op=MULT)

        def late_park(parts, slot):
            words = scaled[h1_key(parts)][:].rearrange("p (a x) -> p a x", a=4)
            nc.sync.dma_start(out=park_area(parts, slot).rearrange("a m x -> m a x"), in_=words)

        def late_fetch(parts, slot):
            key = h1_key(parts)
            back[key] = work.tile([P, N * len(parts)], BF16, tag="back", name="back", align_bytes=ALIGN, bufs=3)
            nc.sync.dma_start(out=back[key][:], in_=park_area(parts, slot).rearrange("a (i r) x -> (a i) (r x)", r=4))

        def late_turn(parts):
            key = h1_key(parts)
            h1_blocks[key] = work.tile([P, 2 * P * len(parts)], F32, tag="blocks", name="blocks", align_bytes=ALIGN, bufs=3)
            nc.vector.transpose(h1_blocks[key][:], back[key][:].bitcast(F32))

        def late_pair(parts, c, engine):
            key = "pass_%d_%d" % parts[c]
            grouped[key] = work.tile([P, N], BF16, tag="grouped", name="grouped", align_bytes=ALIGN, bufs=10)
            dst = grouped[key][:].bitcast(F32).rearrange("p (c i r u) -> p c r u i", i=2, r=4, u=2)
            frm = h1_blocks[h1_key(parts)][:].rearrange("p (r s u c i) -> p s c r u i", r=4, s=len(parts), u=2, i=2)
            copy(engine, dst, frm[:, c])

        def late_pair_both(parts, engine):
            key = h1_key(parts)
            grouped[key] = work.tile([P, 2 * N], BF16, tag="grouped", name="grouped", align_bytes=ALIGN, bufs=10)
            frm = h1_blocks[key][:].rearrange("p (r s u c i) -> p s c r u i", r=4, s=2, u=2, i=2)
            for c in range(2):
                dst = grouped[key][:, N * c : N * c + N].bitcast(F32).rearrange("p (c i r u) -> p c r u i", i=2, r=4, u=2)
                copy(engine, dst, frm[:, c])

        def h1_empty_pass(parts, c, engine):
            bank, n = turned[h1_key(parts)]
            key = "pass_%d_%d" % parts[c]
            grouped[key] = work.tile([P, N], BF16, tag="grouped", name="grouped", align_bytes=ALIGN, bufs=10)
            frm = bank[:, 0 : 2 * P * n].rearrange("p (u c r) -> p c r u", u=2, c=n)
            copy(engine, grouped[key][:].bitcast(F32).rearrange("p (r u) -> p r u", u=2), frm[:, c])

        def h1_quant_pass(parts, c):
            codes, scales = quantise("pass_%d_%d" % parts[c], N)
            r_op[(2,) + parts[c]] = (codes, scales, 0)

        def u_group(b, j, i):
            open_group(1, b, j, i)
            for g in range(NJ):
                u_pass(1, b, j, g, start=g == 0)

        def w_close(b, j):
            w_pass(1, b, j, 0)
            w_pass(1, b, j, 1, stop=True)

        gain_row = keep_tile([P, NJ, N], BF16, "gain_row")

        def load_gain_row():
            nc.sync.dma_start(out=gain_row[:].rearrange("p j n -> p (j n)"), in_=gain.partition_broadcast(P))

        gain_col = keep_tile([P, NJ, 4], BF16, "gain_col")
        w_sc = keep_tile([P, NX, 4], F32, "w_sc")
        zeros = keep_tile([P, N], BF16, "zeros")
        table = keep_tile([P, 16], F32, "table")
        ident = keep_tile([P, P], F32, "ident")
        ident_bf = keep_tile([P, P], BF16, "ident_bf")

        def load_gain(queue=nc.sync):
            queue.dma_start(out=gain_col[:], in_=gain.rearrange("(g p t) -> p g t", p=P, t=4))

        def load_w_scale(queue=nc.sync):
            queue.dma_start(out=w_sc[:], in_=w_scale.rearrange("(g p t) o -> p g (t o)", p=P, t=4))

        first = [[(b, 0), (b, 1)] for b in range(NB)]
        last = [[(0, 2), (1, 2)], [(2, 2), (3, 2)]]

        def h0_turns(b, i0, i1):
            h0_turn(first[b], i0)
            h0_turn([(b, 2)], i1)

        def h0_ready(b):
            h0_empty(first[b])
            h0_empty([(b, 2)])
            h0_quant(first[b])
            h0_quant([(b, 2)])

        def warm_up(count, i=1):
            bank = bank_tile(i)
            for c in range(count):
                nc.tensor.matmul(bank[:], lhsT=zeros[:, 0:P], rhs=zeros[:], start=True, stop=True)

        def head(b, j, i):
            open_group(2, b, j, i)
            w_pass(2, b, j, 0, start=True)
            w_pass(2, b, j, 1)

        def piece_head(key, i, c0, c1):
            open_group(2, *key, i)
            w_pass(2, *key, 0, start=True, c0=c0, c1=c1)
            w_pass(2, *key, 1, c0=c0, c1=c1)
            return acc[(2,) + key]

        def piece_close(key, bank, c0, c1):
            acc[(2,) + key] = bank
            for g in (2, 0, 1):
                u_pass(2, *key, g, stop=g == 1, c0=c0, c1=c1)
            finish(2, *key, c0, c1)

        def close(b, j):
            u_pass(2, b, j, 2, stop=True)
            finish(2, b, j)

        def group2(b, j, i, c0=0, c1=N):
            open_group(2, b, j, i)
            w_pass(2, b, j, 0, start=True, c0=c0, c1=c1)
            w_pass(2, b, j, 1, c0=c0, c1=c1)
            for g in range(NJ):
                u_pass(2, b, j, g, stop=g == NJ - 1, c0=c0, c1=c1)
            finish(2, b, j, c0, c1)

        load_gain(nc.scalar)
        load_w_scale(nc.scalar)
        nc.vector.memset(zeros[:].bitcast(I32), 0)
        zero_u_scales(0, 1)
        nc.vector.memset(table[:], 0.0)
        nc.scalar.activation(out=table[:, 0:1], in_=table[:, 8:9], func=TANH)
        make_identity(nc, ident[:])
        zero_u_scales(1, 2)
        zero_u_scales(2, 3)
        nc.vector.tensor_copy(out=ident_bf[:], in_=ident[:])
        load_w(0, 0, 1)
        load_h0(0)
        load_h0(1)
        load_h0(2)
        load_u(0)
        load_u_scales(0, 1)
        load_w(1, 0, 1)
        load_h0(3)
        load_x(1, 0, 1)
        load_x(1, 1, 2)
        load_x(1, 2, 3)
        load_x(1, 3, 4)
        load_u(1)
        load_u_scales(1, 2)
        load_w(0, 1, 2)
        load_w(1, 1, 2)
        load_w(0, 2, 3)
        load_w(1, 2, 3)
        load_u(2)
        load_u_scales(2, 3)
        load_x(2, 0, 1)
        load_x(2, 1, 2)
        load_x2_half(1)

        warm_up(2)
        spread_gain(0, 0, "scalar")
        spread_gain(1, 2, "scalar")
        spread_gain(2, 3, "scalar")
        w_widen(0, 0, range(4), "vector")
        w_weave(0, 0, "scalar")
        h0_turns(0, 6, 7)
        h0_turns(1, 4, 5)
        warm_up(1)
        h0_turns(2, 2, 3)
        warm_up(1)
        h0_ready(0)
        h0_ready(1)
        h0_ready(2)
        u_group(0, 0, 0)
        u_group(1, 0, 1)
        h0_turns(3, 4, 5)
        u_group(2, 0, 2)
        w_widen(0, 1, (0, 1, 2), "scalar")
        w_widen(0, 1, (3,), "vector")
        w_quant(0, 0)
        x_sort(1, 0, "scalar")
        x_sort(1, 1, "scalar")
        w_weave(0, 1, "scalar", 0, N // 2)
        h0_empty([(3, 2)])
        h0_empty(first[3])
        h0_quant([(3, 2)])
        h0_quant(first[3])
        w_weave(0, 1, "vector", N // 2, N)
        x_turn(1, 0, 6)
        x_turn(1, 1, 7)
        x_turn(1, 2, 3)
        x_turn(1, 3, 5)
        for b in range(NB):
            x_empty(1, b, "scalar")
        x_quant(1, 0)
        w_quant(0, 1)
        x_quant(1, 1)
        w_widen(1, 0, (0, 1), "vector")
        x_quant(1, 2)
        w_widen(1, 0, (2, 3), "vector")
        x_quant(1, 3)
        w_weave(1, 0)
        u_group(3, 0, 4)
        u_group(0, 1, 6)
        u_group(1, 1, 7)
        w_widen(1, 1, (0, 1, 2), "scalar")
        w_widen(1, 1, (3,), "vector")
        w_quant(1, 0)
        w_weave(1, 1)
        w_widen(2, 0, (0, 1), "scalar")
        w_widen(2, 0, (2, 3), "vector")
        w_quant(1, 1)
        w_weave(2, 0)
        for b in range(NB):
            w_close(b, 0)
        u_group(2, 1, 3)
        u_group(3, 1, 5)
        finish(1, 0, 0)
        finish(1, 1, 0)
        u_group(0, 2, 0)
        u_group(1, 2, 1)
        finish(1, 2, 0)
        finish(1, 3, 0)
        w_widen(2, 1, range(4), "scalar")
        x_sort(2, 0, "scalar")
        x_sort(2, 1, "scalar")
        u_group(2, 2, 2)
        u_group(3, 2, 4)
        for b in range(NB):
            w_close(b, 1)
        h1_scale(0, 0)
        w_quant(2, 0)
        w_weave(2, 1)
        finish(1, 0, 1)
        finish(1, 1, 1)
        h1_scale(1, 0)
        w_quant(2, 1)
        x_turn(2, 0, 6)
        x_turn(2, 1, 7)
        for b in range(NB):
            w_pass(1, b, 2, 0)
        finish(1, 2, 1)
        finish(1, 3, 1)
        x_empty(2, 0, "scalar")
        x_empty(2, 1, "scalar")
        h1_scale(0, 1)
        pair_b, pair_c, pair_d = first[2], last[1], first[3]
        x_quant(2, 0)
        h1_scale(1, 1)
        x_quant(2, 1)
        late_scale(pair_b, 0, 1)
        for b in range(NB):
            w_pass(1, b, 2, 1, stop=True)
        for b in range(NB):
            finish(1, b, 2, later=b >= 3)
        h1_scale(0, 2)
        h1_scale(1, 2)
        late_scale(pair_b, 1, 2)
        late_park(pair_b, 6)
        store(1, 3, 2)
        late_scale(pair_c, 0, 1)
        for j, i in enumerate((3, 5, 6)):
            head(0, j, i)
        h1_turn(first[0], 7)
        h1_turn(first[1], 0)
        h1_turn(last[0], 1)
        head(1, 0, 2)
        head(1, 1, 4)
        h1_empty_pass(first[0], 0, "scalar")
        h1_empty_pass(first[0], 1, "scalar")
        h1_empty(last[0], "scalar")
        h1_empty(first[1], "scalar")
        x2_sort(2, "scalar")
        x2_sort(3, "scalar")
        h1_quant_pass(first[0], 0)
        late_scale(pair_c, 1, 2)
        late_park(pair_c, 8)
        h1_quant_pass(first[0], 1)
        late_scale(pair_d, 0, 1)
        h1_quant(last[0])
        late_scale(pair_d, 1, 2)
        h1_quant(first[1])
        late_fetch(pair_b, 6)
        late_park(pair_d, 10)
        late_fetch(pair_c, 8)
        for g in range(NJ):
            for j in range(NJ):
                u_pass(2, 0, j, g, stop=g == NJ - 1)
        finish(2, 0, 0)
        x2_turn(2)
        x2_pair(2, "scalar")
        x2_turn(3)
        x_quant(2, 2)
        late_turn(pair_b)
        finish(2, 0, 1)
        late_fetch(pair_d, 10)
        x2_pair(3, "scalar")
        x_quant(2, 3)
        for c in range(2):
            late_pair(pair_b, c, "scalar")
        late_turn(pair_c)
        for c in range(2):
            h1_quant_pass(pair_b, c)
        finish(2, 0, 2)
        head(1, 2, 7)
        for j in range(NJ):
            for g in range(NJ):
                u_pass(2, 1, j, g, stop=g == NJ - 1)
        finish(2, 1, 0)
        for c in range(2):
            late_pair(pair_c, c, "vector")
        for c in range(2):
            h1_quant_pass(pair_c, c)
        late_turn(pair_d)
        finish(2, 1, 1)
        finish(2, 1, 2)
        for j, i in enumerate((0, 1, 3)):
            head(2, j, i)
        pieces = [((3, 0), 5, 0, 512), ((3, 1), 6, 0, 256), ((3, 1), 2, 256, 512)]
        banks = [piece_head(*pieces[0])]
        u_pass(2, 2, 0, 0)
        u_pass(2, 2, 0, 1)
        u_pass(2, 2, 1, 0)
        close(2, 0)
        u_pass(2, 2, 1, 1)
        close(2, 1)
        for g in range(NJ):
            u_pass(2, 2, 2, g, stop=g == NJ - 1)
        finish(2, 2, 2)
        for c in range(2):
            late_pair(pair_d, c, "vector")
        for c in range(2):
            h1_quant_pass(pair_d, c)
        banks.extend([piece_head(*piece) for piece in pieces[len(banks):3]])
        for (key, i, c0, c1), bank in zip(pieces, banks):
            piece_close(key, bank, c0, c1)
        for key, i, c0, c1 in pieces[3:]:
            group2(*key, i, c0, c1)
        group2(3, 2, 4, 0, 256)
        group2(3, 2, 7, 256, 384)
        group2(3, 2, 0, 384, 512)
